import numpy as np
import ml_dtypes


def mxq(x, axis, fmt="e4m3"):
    dtype, down = {"e4m3": (ml_dtypes.float8_e4m3fn, 7), "e5m2": (ml_dtypes.float8_e5m2, 14)}[fmt]
    v = np.moveaxis(np.asarray(x, np.float32).astype(ml_dtypes.bfloat16).astype(np.float64), axis, -1)
    blocks = v.reshape(v.shape[:-1] + (-1, 32))
    amax = np.abs(blocks).max(-1, keepdims=True)
    byte = np.maximum(np.where(amax > 0, np.frexp(amax)[1] - 1 + 127, 0) - down, 1)
    scale = np.exp2(byte - 127.0)
    codes = (blocks / scale).astype(np.float32).astype(dtype).astype(np.float64)
    return np.moveaxis((codes * scale).reshape(v.shape), -1, axis)


WIDE = False


def mx_kscale(k):
    if not WIDE:
        return np.ones(k)
    levels = np.array([24, -24, 12, -12, 0])
    if k % 512:
        return np.exp2(np.random.permutation(np.resize(levels, k // 32))).repeat(32)
    a = np.empty((k // 512, 16))
    for p in range(k // 512):
        a[p, :8] = np.random.permutation(np.resize(levels, 8))
        for g in range(8):
            far = levels[np.abs(levels - a[p, g]) >= 10]
            a[p, g + 8] = far[np.random.randint(len(far))]
    return np.exp2(a.ravel()).repeat(32)


def f64(x):
    return np.asarray(x).astype(np.float64)


def striped8(idx):
    return np.concatenate([v.reshape(-1, 16).T for v in idx]).astype(np.uint16)


def unstriped8(offs):
    return np.stack([offs[16 * g:16 * g + 16].T.reshape(-1) for g in range(8)]).astype(np.int64)


E2M1 = np.array([0.0, 0.5, 1.0, 1.5, 2.0, 3.0, 4.0, 6.0, -0.0, -0.5, -1.0, -1.5, -2.0, -3.0, -4.0, -6.0])


def pack_weight(w, fmt):
    k, n = w.shape
    w = f64(np.asarray(w, np.float32).astype(ml_dtypes.bfloat16)).reshape(k // 32, 32, n)
    amax = np.abs(w).max(1)
    if fmt == "e4m3":
        byte = np.frexp(amax)[1] - 1 + 127 - 7
    else:
        mant, ex = np.frexp(amax / 6.0)
        byte = np.where(mant > 0.5, ex, ex - 1) + 127
    byte = np.clip(np.where(amax > 0, byte, 1), 1, 254)
    scaled = (w * np.exp2(127.0 - byte)[:, None, :]).reshape(k, n).astype(np.float32)
    by_word = np.ascontiguousarray(scaled.reshape(k // 512, 128, 4, n).transpose(0, 1, 3, 2))
    if fmt == "e4m3":
        words = by_word.astype(ml_dtypes.float8_e4m3fn).view(np.uint8)
    else:
        c = by_word.astype(ml_dtypes.float4_e2m1fn).view(np.uint8) & 0xF
        words = (c[..., 0::2] | (c[..., 1::2] << 4)).reshape(k // 512, 128, 2 * n)
    return np.ascontiguousarray(words), np.ascontiguousarray(byte.astype(np.uint8).reshape(k // 512, 16, n))


def unpack_weight(words, scales, fmt):
    g, _, n = scales.shape
    words = np.ascontiguousarray(words).reshape(g, 128, n, -1)
    if fmt == "e4m3":
        vals = words.view(ml_dtypes.float8_e4m3fn).astype(np.float64)
    else:
        nib = np.empty((g, 128, n, 4), np.uint8)
        nib[..., 0::2] = words & 0xF
        nib[..., 1::2] = words >> 4
        vals = E2M1[nib]
    vals = vals * np.repeat(np.exp2(scales.astype(np.float64) - 127.0), 8, axis=1)[..., None]
    return vals.transpose(0, 1, 3, 2).reshape(g * 512, n)


def planes(y):
    n, m = y.shape
    v = y.astype(np.float32).astype(ml_dtypes.bfloat16).astype(np.float64).reshape(n // 32, 32, m)
    top = np.abs(v).max(1)
    byte = np.clip(np.where(top > 0, np.frexp(top)[1] - 1 + 127 - 7, 1), 1, 254)
    codes = (v * np.exp2(127.0 - byte)[:, None, :]).reshape(n, m).astype(np.float32).astype(ml_dtypes.float8_e4m3fn).view(np.uint8)
    words = codes.reshape(n // 512, 128, 4, m).transpose(0, 1, 3, 2)
    return np.ascontiguousarray(words), np.ascontiguousarray(byte.astype(np.uint8).reshape(n // 512, 16, m))


def silu(f):
    return f / (1.0 + np.exp(-np.maximum(f, -700.0)))


K, R, N, T, J = 1024, 1024, 512, 2048, 1024


def setup_inputs():
    n = np.random.standard_normal
    s = mx_kscale(K)[:, None]
    u = mx_kscale(R)[:, None]
    p_wg = pack_weight(n((K, R)) / np.sqrt(K) / s, "e4m3")
    p_wu = pack_weight(n((K, R)) / np.sqrt(K) / s * u.T, "e4m3")
    p_wd = pack_weight(n((R, N)) / np.sqrt(R) / u, "e2m1")
    return {
        "xT": (n((K, T)) * s).astype(np.float32),
        "wgt": np.repeat(np.random.uniform(0.5, 2.0, (8, J)), 16, axis=0).astype(np.float32),
        "wg_words": p_wg[0],
        "wg_scales": p_wg[1],
        "wu_words": p_wu[0],
        "wu_scales": p_wu[1],
        "wd_words": p_wd[0],
        "wd_scales": p_wd[1],
        "offs": striped8(np.stack([np.random.permutation(T)[:J] for _ in range(8)])),
    }


def reference(xT, wgt, wg_words, wg_scales, wu_words, wu_scales, wd_words, wd_scales, offs):
    idx = unstriped8(offs)
    rows = np.arange(K)
    xg = f64(wgt)[rows // 4 % 128] * f64(xT)[rows[:, None], idx[rows % 512 // 64]]
    xT_ = mxq(xg, 0, "e4m3")
    wg_ = unpack_weight(wg_words, wg_scales, "e4m3")
    wu_ = unpack_weight(wu_words, wu_scales, "e4m3")
    ga = wg_.T @ xT_
    ub = wu_.T @ xT_
    h = silu(ga) * ub
    h_ = mxq(h, 0, "e4m3")
    wd_ = unpack_weight(wd_words, wd_scales, "e2m1")
    y = wd_.T @ h_
    return (y,) + planes(y)

@@ -1,0 +1,235 @@
+from contextlib import ExitStack
+
+import concourse.mybir as mybir
+
+K, R, N, T, J = 1024, 1024, 512, 2048, 1024
+FLOPS = 2 * J * (2 * K * R + R * N)
+
+F32 = mybir.dt.float32
+BF16 = mybir.dt.bfloat16
+I32 = mybir.dt.int32
+U32 = mybir.dt.uint32
+U16 = mybir.dt.uint16
+U8 = mybir.dt.uint8
+E4M3X4 = mybir.dt.float8_e4m3fn_x4
+E2M1X4 = mybir.dt.float4_e2m1fn_x4
+MULT = mybir.AluOpType.mult
+SILU = mybir.ActivationFunctionType.Silu
+
+P = 128
+PACK = 4
+SPAN = P * PACK
+PASSES = 2
+TILE = 128
+TILES = J // TILE
+CHUNKS = ((0, 128), (128, 256), (256, 512), (512, 1024))
+STORES = ((0, 256), (256, 512), (512, 768), (768, 896), (896, 1024))
+
+
+def tile_list_silu_noneP_kernel(
+    tc, xT, wgt, wg_words, wg_scales, wu_words, wu_scales, wd_words, wd_scales, offs, out_0, out_1, out_2
+):
+    nc = tc.nc
+    with ExitStack() as ctx:
+        keep = ctx.enter_context(tc.tile_pool(name="keep", bufs=1))
+        ring = ctx.enter_context(tc.tile_pool(name="ring", bufs=3))
+        psum = ctx.enter_context(tc.psum_pool(name="psum", bufs=1))
+
+        offsets = keep.tile([P, J // 16], U16, name="offsets")
+        nc.sync.dma_start(offsets[:], offs)
+
+        warm = keep.tile([P, 8], F32, name="warm")
+        warm2 = keep.tile([P, 8], F32, name="warm2")
+        nc.vector.memset(warm[:], 0.0)
+        nc.scalar.activation(warm2[:], warm[:], SILU)
+
+        up_raw = keep.tile([P, R], U8, name="up_raw", align_bytes=64)
+        down_raw = keep.tile([P, PASSES * N], U8, name="down_raw", align_bytes=64)
+        nc.gpsimd.memset(up_raw[:].bitcast(I32), 0)
+        nc.gpsimd.memset(down_raw[:].bitcast(I32), 0)
+        for w, scales in enumerate((wg_scales, wu_scales)):
+            for q in range(4):
+                nc.gpsimd.dma_start(
+                    up_raw[32 * q + 8 * w : 32 * q + 8 * w + 8, :].bitcast(I32),
+                    scales[:, 4 * q : 4 * q + 4, :].bitcast(I32),
+                )
+        for q in range(4):
+            nc.gpsimd.dma_start(
+                down_raw[32 * q : 32 * q + 4, :].bitcast(I32).rearrange("r (a n) -> r a n", a=PASSES),
+                wd_scales[:, 4 * q : 4 * q + 4, :].bitcast(I32).rearrange("a r n -> r a n"),
+            )
+
+        weight = keep.tile([P, J], F32, name="weight")
+        planes = {}
+        raw = {}
+
+        def load_plane(a, i):
+            planes[a, i] = keep.tile([P, T], F32, name="plane%d%d" % (a, i))
+            rows = xT[SPAN * a : SPAN * (a + 1), :].rearrange("(p i) t -> p i t", i=PACK)
+            nc.sync.dma_start(planes[a, i][:], rows[:, i, :])
+
+        def load_up(b):
+            for a in range(PASSES):
+                for w, words in enumerate((wg_words, wu_words)):
+                    raw[w, a, b] = keep.tile([P, SPAN], I32, name="raw%d%d%d" % (w, a, b))
+                    src = words[a].rearrange("p r i -> p (r i)").bitcast(I32)
+                    nc.sync.dma_start(raw[w, a, b][:], src[:, SPAN * b : SPAN * (b + 1)])
+
+        load_plane(0, 0)
+        nc.sync.dma_start(weight[:], wgt)
+        for i in range(1, PACK):
+            load_plane(0, i)
+        load_plane(1, 0)
+        load_plane(1, 1)
+        load_up(0)
+        load_plane(1, 2)
+        load_plane(1, 3)
+        load_up(1)
+        wd_raw = keep.tile([P, PASSES, 2 * N], U8, name="wd_raw")
+        nc.sync.dma_start(wd_raw[:].bitcast(I32), wd_words.bitcast(I32).rearrange("a p n -> p a n"))
+
+        up_scale = keep.tile([P, R], U8, name="up_scale", align_bytes=64)
+        nc.vector.tensor_copy(
+            up_scale[:].rearrange("p (b t m) -> p b t m", b=PASSES, t=PACK),
+            up_raw[:].rearrange("p (b m t) -> p b t m", b=PASSES, t=PACK),
+        )
+        down_scale = keep.tile([P, PASSES * N], U8, name="down_scale", align_bytes=64)
+        nc.vector.tensor_copy(
+            down_scale[:].rearrange("p (b t m) -> p b t m", b=PASSES, t=PACK),
+            down_raw[:].rearrange("p (b m t) -> p b t m", b=PASSES, t=PACK),
+        )
+
+        picked = {}
+        x_codes = {}
+        x_scales = {}
+        dealt = {}
+
+        def gather(a, i, c):
+            lo, hi = CHUNKS[c]
+            if i == 0:
+                picked[a, c] = keep.tile([P, PACK, hi - lo], F32, name="picked%d%d" % (a, c))
+            nc.vector.tensor_tensor(
+                picked[a, c][:, i, :], planes[a, i][:].indirect(offsets[:, lo // 16 : hi // 16]), weight[:, lo:hi], MULT
+            )
+
+        def quantise_x(a, c):
+            lo, hi = CHUNKS[c]
+            woven = keep.tile([P, hi - lo, PACK], BF16, name="woven%d%d" % (a, c), align_bytes=64)
+            nc.scalar.copy(
+                woven[:].rearrange("p (c e) i -> p c i e", e=4),
+                picked[a, c][:].rearrange("p i (c e) -> p c i e", e=4),
+            )
+            x_codes[a, c] = keep.tile([P, hi - lo], U32, name="x_codes%d%d" % (a, c), align_bytes=64)
+            x_scales[a, c] = keep.tile([P, hi - lo], U8, name="x_scales%d%d" % (a, c), align_bytes=64)
+            nc.vector.quantize_mx(
+                out=x_codes[a, c][:].bitcast(E4M3X4),
+                scales=x_scales[a, c][:],
+                in_=woven[:].rearrange("p j i -> p (j i)"),
+            )
+
+        def deal_up(b):
+            for a in range(PASSES):
+                for w in range(2):
+                    dealt[w, a, b] = keep.tile([P, SPAN], I32, name="dealt%d%d%d" % (w, a, b), align_bytes=64)
+                    nc.vector.tensor_copy(
+                        dealt[w, a, b][:].rearrange("p (t m) -> p m t", t=PACK),
+                        raw[w, a, b][:].rearrange("p (m t) -> p m t", t=PACK),
+                    )
+
+        for i in range(PACK):
+            for c in range(len(CHUNKS)):
+                gather(0, i, c)
+        for c in range(len(CHUNKS)):
+            quantise_x(0, c)
+        for i in range(2):
+            for c in range(len(CHUNKS)):
+                gather(1, i, c)
+        deal_up(0)
+        for c in range(len(CHUNKS)):
+            gather(1, 2, c)
+        for c in range(len(CHUNKS)):
+            gather(1, 3, c)
+            quantise_x(1, c)
+        deal_up(1)
+        wd_dealt = keep.tile([P, PASSES, 2 * N], U8, name="wd_dealt", align_bytes=64)
+        nc.vector.tensor_copy(
+            wd_dealt[:].rearrange("p a (t m e) -> p a m t e", t=PACK, e=2),
+            wd_raw[:].rearrange("p a (m t e) -> p a m t e", t=PACK, e=2),
+        )
+
+        h_codes = {}
+        h_scales = {}
+
+        def hidden(s, b):
+            c = max(n for n in range(len(CHUNKS)) if CHUNKS[n][0] <= TILE * s)
+            cols = slice(TILE * s - CHUNKS[c][0], TILE * (s + 1) - CHUNKS[c][0])
+            banks = [psum.tile([P, PACK, TILE], F32, name=name, bufs=3) for name in ("gate", "up")]
+            for a in range(PASSES):
+                for w in range(2):
+                    for t in range(PACK):
+                        nc.tensor.matmul_mx(
+                            out=banks[w][:, t, :],
+                            lhsT=dealt[w, a, b][:, P * t : P * (t + 1)].bitcast(E4M3X4),
+                            lhsT_scale=up_scale[8 * w + 4 * a : P, SPAN * b + P * t : SPAN * b + P * (t + 1)],
+                            rhs=x_codes[a, c][:, cols].bitcast(E4M3X4),
+                            rhs_scale=x_scales[a, c][:, cols],
+                            start=(a == 0 and t == 0),
+                            stop=(a == PASSES - 1 and t == PACK - 1),
+                        )
+            act = ring.tile([P, TILE, PACK], F32, name="act")
+            nc.scalar.activation(act[:], banks[0][:].rearrange("p t j -> p j t"), SILU)
+            h = ring.tile([P, TILE, PACK], BF16, name="h", align_bytes=64)
+            nc.vector.tensor_tensor(h[:], banks[1][:].rearrange("p t j -> p j t"), act[:], MULT)
+            h_codes[s, b] = keep.tile([P, TILE], U32, name="h_codes%d%d" % (s, b), align_bytes=64)
+            h_scales[s, b] = keep.tile([P, TILE], U8, name="h_scales%d%d" % (s, b), align_bytes=64)
+            nc.vector.quantize_mx(
+                out=h_codes[s, b][:].bitcast(E4M3X4), scales=h_scales[s, b][:], in_=h[:].rearrange("p j t -> p (j t)")
+            )
+
+        y_scales = keep.tile([P, J], U8, name="y_scales", align_bytes=64)
+        y_rows = out_0.rearrange("(p t) j -> p t j", t=PACK)
+        code_rows = out_1[0].rearrange("p j i -> p (j i)").bitcast(I32)
+        staged = {}
+
+        def output(s):
+            g = max(n for n in range(len(STORES)) if STORES[n][0] <= TILE * s)
+            lo, hi = STORES[g]
+            if lo == TILE * s:
+                staged[g] = (
+                    keep.tile([P, PACK, hi - lo], F32, name="y%d" % g),
+                    keep.tile([P, hi - lo], I32, name="y_codes%d" % g, align_bytes=64),
+                )
+            y, y_codes = staged[g]
+            cols = slice(TILE * s - lo, TILE * (s + 1) - lo)
+            bank = psum.tile([P, PACK, TILE], F32, name="down", bufs=2)
+            for b in range(PASSES):
+                for t in range(PACK):
+                    nc.tensor.matmul_mx(
+                        out=bank[:, t, :],
+                        lhsT=wd_dealt[:, b, 2 * P * t : 2 * P * (t + 1)].bitcast(E2M1X4),
+                        lhsT_scale=down_scale[:, N * b + P * t : N * b + P * (t + 1)],
+                        rhs=h_codes[s, b][:].bitcast(E4M3X4),
+                        rhs_scale=h_scales[s, b][:],
+                        start=(b == 0 and t == 0),
+                        stop=(b == PASSES - 1 and t == PACK - 1),
+                    )
+            nc.scalar.copy(y[:, :, cols], bank[:])
+            rounded = ring.tile([P, TILE, PACK], BF16, name="rounded", align_bytes=64)
+            nc.scalar.copy(rounded[:], bank[:].rearrange("p t j -> p j t"))
+            nc.vector.quantize_mx(
+                out=y_codes[:, cols].bitcast(E4M3X4),
+                scales=y_scales[:, TILE * s : TILE * (s + 1)],
+                in_=rounded[:].rearrange("p j t -> p (j t)"),
+            )
+            if hi == TILE * (s + 1):
+                nc.sync.dma_start(y_rows[:, :, lo:hi], y[:])
+                nc.sync.dma_start(code_rows[:, lo:hi], y_codes[:])
+
+        for s in range(TILES):
+            hidden(s, 0)
+            hidden(s, 1)
+            if s > 0:
+                output(s - 1)
+        output(TILES - 1)
+        for q in range(4):
+            nc.sync.dma_start(out_2[0, 4 * q : 4 * q + 4, :].bitcast(I32), y_scales[32 * q : 32 * q + 4, :].bitcast(I32))

@@ -22,7 +22,7 @@ SPAN = P * PACK
 PASSES = 2
 TILE = 128
 TILES = J // TILE
-CHUNKS = ((0, 128), (128, 256), (256, 512), (512, 1024))
+CHUNKS = (((0, 512), (512, 1024)), ((0, 128), (128, 256), (256, 512), (512, 768), (768, 1024)))
 STORES = ((0, 256), (256, 512), (512, 768), (768, 896), (896, 1024))
 
 
@@ -49,49 +49,126 @@ def tile_list_silu_noneP_kernel(
         nc.gpsimd.memset(down_raw[:].bitcast(I32), 0)
         for w, scales in enumerate((wg_scales, wu_scales)):
             for q in range(4):
-                nc.gpsimd.dma_start(
+                nc.scalar.dma_start(
                     up_raw[32 * q + 8 * w : 32 * q + 8 * w + 8, :].bitcast(I32),
                     scales[:, 4 * q : 4 * q + 4, :].bitcast(I32),
                 )
-        for q in range(4):
-            nc.gpsimd.dma_start(
-                down_raw[32 * q : 32 * q + 4, :].bitcast(I32).rearrange("r (a n) -> r a n", a=PASSES),
-                wd_scales[:, 4 * q : 4 * q + 4, :].bitcast(I32).rearrange("a r n -> r a n"),
-            )
 
-        weight = keep.tile([P, J], F32, name="weight")
+        weight = [keep.tile([P, J // 2], F32, name="weight%d" % n) for n in range(2)]
         planes = {}
         raw = {}
 
         def load_plane(a, i):
-            planes[a, i] = keep.tile([P, T], F32, name="plane%d%d" % (a, i))
+            planes[a, i] = keep.tile([P, T], F32, name="plane%d%d" % (a, i), align_bytes=64)
             rows = xT[SPAN * a : SPAN * (a + 1), :].rearrange("(p i) t -> p i t", i=PACK)
             nc.sync.dma_start(planes[a, i][:], rows[:, i, :])
 
-        def load_up(b):
-            for a in range(PASSES):
-                for w, words in enumerate((wg_words, wu_words)):
-                    raw[w, a, b] = keep.tile([P, SPAN], I32, name="raw%d%d%d" % (w, a, b))
-                    src = words[a].rearrange("p r i -> p (r i)").bitcast(I32)
-                    nc.sync.dma_start(raw[w, a, b][:], src[:, SPAN * b : SPAN * (b + 1)])
+        def load_up(a, b):
+            for w, words in enumerate((wg_words, wu_words)):
+                raw[w, a, b] = keep.tile([P, SPAN], I32, name="raw%d%d%d" % (w, a, b))
+                src = words[a].rearrange("p r i -> p (r i)").bitcast(I32)
+                nc.sync.dma_start(raw[w, a, b][:], src[:, SPAN * b : SPAN * (b + 1)])
 
         load_plane(0, 0)
-        nc.sync.dma_start(weight[:], wgt)
+        for n in range(2):
+            nc.sync.dma_start(weight[n][:], wgt[:, n * J // 2 : (n + 1) * J // 2])
         for i in range(1, PACK):
             load_plane(0, i)
         load_plane(1, 0)
         load_plane(1, 1)
-        load_up(0)
+        load_up(0, 0)
         load_plane(1, 2)
         load_plane(1, 3)
-        load_up(1)
+        load_up(1, 0)
+        load_up(0, 1)
+        load_up(1, 1)
         wd_raw = keep.tile([P, PASSES, 2 * N], U8, name="wd_raw")
         nc.sync.dma_start(wd_raw[:].bitcast(I32), wd_words.bitcast(I32).rearrange("a p n -> p a n"))
+        for q in range(4):
+            nc.sync.dma_start(
+                down_raw[32 * q : 32 * q + 4, :].bitcast(I32).rearrange("r (a n) -> r a n", a=PASSES),
+                wd_scales[:, 4 * q : 4 * q + 4, :].bitcast(I32).rearrange("a r n -> r a n"),
+            )
 
-        up_scale = keep.tile([P, R], U8, name="up_scale", align_bytes=64)
+        picked = {}
+        x_codes = {}
+        x_scales = {}
+        dealt = {}
+
+        woven = {}
+
+        def gather(a, i, c):
+            lo, hi = CHUNKS[a][c]
+            if i % 2 == 0:
+                late = a == 1 and c == len(CHUNKS[1]) - 1
+                tag = "picked%d%d%d" % ((1, 1, i // 2) if late else (a, i // 2, c))
+                picked[a, i // 2, c] = keep.tile([P, 2, hi - lo], F32, name=tag)
+            half = lo // (J // 2)
+            nc.vector.tensor_tensor(
+                picked[a, i // 2, c][:, i % 2, :],
+                planes[a, i][:].indirect(offsets[:, lo // 16 : hi // 16]),
+                weight[half][:, lo - half * J // 2 : hi - half * J // 2],
+                MULT,
+            )
+
+        def weave(a, u, c):
+            lo, hi = CHUNKS[a][c]
+            if u == 0:
+                woven[a, c] = keep.tile([P, hi - lo, PACK], BF16, name="woven%d%d" % (a, c), align_bytes=64)
+            nc.scalar.copy(woven[a, c][:, :, 2 * u : 2 * u + 2], picked[a, u, c][:].rearrange("p e j -> p j e"))
+
+        def quantise_x(a, c):
+            lo, hi = CHUNKS[a][c]
+            x_codes[a, c] = keep.tile([P, hi - lo], U32, name="x_codes%d%d" % (a, c), align_bytes=64)
+            x_scales[a, c] = keep.tile([P, hi - lo], U8, name="x_scales%d%d" % (a, c), align_bytes=64)
+            nc.vector.quantize_mx(
+                out=x_codes[a, c][:].bitcast(E4M3X4),
+                scales=x_scales[a, c][:],
+                in_=woven[a, c][:].rearrange("p j i -> p (j i)"),
+            )
+
+        def deal_up(a, b):
+            for w in range(2):
+                dealt[w, a, b] = keep.tile([P, SPAN], I32, name="dealt%d%d%d" % (w, a, b), align_bytes=64)
+                nc.vector.tensor_copy(
+                    dealt[w, a, b][:].rearrange("p (t m) -> p m t", t=PACK),
+                    raw[w, a, b][:].rearrange("p (m t) -> p m t", t=PACK),
+                )
+
+        early = range(len(CHUNKS[1]) - 1)
+        last = len(CHUNKS[1]) - 1
+        for i in range(PACK):
+            for c in range(len(CHUNKS[0])):
+                gather(0, i, c)
+                if i % 2 == 1:
+                    weave(0, i // 2, c)
+        for c in range(len(CHUNKS[0])):
+            quantise_x(0, c)
+        up_scale = keep.tile([P, R], U8, name="plane03", align_bytes=64)
         nc.vector.tensor_copy(
             up_scale[:].rearrange("p (b t m) -> p b t m", b=PASSES, t=PACK),
             up_raw[:].rearrange("p (b m t) -> p b t m", b=PASSES, t=PACK),
+        )
+        for i in range(2):
+            for c in early:
+                gather(1, i, c)
+                if i == 1:
+                    weave(1, 0, c)
+        deal_up(0, 0)
+        for c in early:
+            gather(1, 2, c)
+        for c in early:
+            gather(1, 3, c)
+            weave(1, 1, c)
+            quantise_x(1, c)
+            if c == 0:
+                deal_up(1, 0)
+        deal_up(0, 1)
+        deal_up(1, 1)
+        wd_dealt = keep.tile([P, PASSES, 2 * N], U8, name="wd_dealt", align_bytes=64)
+        nc.vector.tensor_copy(
+            wd_dealt[:].bitcast(U16).rearrange("p a (t m) -> p a m t", t=PACK),
+            wd_raw[:].bitcast(U16).rearrange("p a (m t) -> p a m t", t=PACK),
         )
         down_scale = keep.tile([P, PASSES * N], U8, name="down_scale", align_bytes=64)
         nc.vector.tensor_copy(
@@ -99,92 +176,49 @@ def tile_list_silu_noneP_kernel(
             down_raw[:].rearrange("p (b m t) -> p b t m", b=PASSES, t=PACK),
         )
 
-        picked = {}
-        x_codes = {}
-        x_scales = {}
-        dealt = {}
-
-        def gather(a, i, c):
-            lo, hi = CHUNKS[c]
-            if i == 0:
-                picked[a, c] = keep.tile([P, PACK, hi - lo], F32, name="picked%d%d" % (a, c))
-            nc.vector.tensor_tensor(
-                picked[a, c][:, i, :], planes[a, i][:].indirect(offsets[:, lo // 16 : hi // 16]), weight[:, lo:hi], MULT
-            )
-
-        def quantise_x(a, c):
-            lo, hi = CHUNKS[c]
-            woven = keep.tile([P, hi - lo, PACK], BF16, name="woven%d%d" % (a, c), align_bytes=64)
-            nc.scalar.copy(
-                woven[:].rearrange("p (c e) i -> p c i e", e=4),
-                picked[a, c][:].rearrange("p i (c e) -> p c i e", e=4),
-            )
-            x_codes[a, c] = keep.tile([P, hi - lo], U32, name="x_codes%d%d" % (a, c), align_bytes=64)
-            x_scales[a, c] = keep.tile([P, hi - lo], U8, name="x_scales%d%d" % (a, c), align_bytes=64)
-            nc.vector.quantize_mx(
-                out=x_codes[a, c][:].bitcast(E4M3X4),
-                scales=x_scales[a, c][:],
-                in_=woven[:].rearrange("p j i -> p (j i)"),
-            )
-
-        def deal_up(b):
-            for a in range(PASSES):
-                for w in range(2):
-                    dealt[w, a, b] = keep.tile([P, SPAN], I32, name="dealt%d%d%d" % (w, a, b), align_bytes=64)
-                    nc.vector.tensor_copy(
-                        dealt[w, a, b][:].rearrange("p (t m) -> p m t", t=PACK),
-                        raw[w, a, b][:].rearrange("p (m t) -> p m t", t=PACK),
-                    )
-
-        for i in range(PACK):
-            for c in range(len(CHUNKS)):
-                gather(0, i, c)
-        for c in range(len(CHUNKS)):
-            quantise_x(0, c)
-        for i in range(2):
-            for c in range(len(CHUNKS)):
-                gather(1, i, c)
-        deal_up(0)
-        for c in range(len(CHUNKS)):
-            gather(1, 2, c)
-        for c in range(len(CHUNKS)):
-            gather(1, 3, c)
-            quantise_x(1, c)
-        deal_up(1)
-        wd_dealt = keep.tile([P, PASSES, 2 * N], U8, name="wd_dealt", align_bytes=64)
-        nc.vector.tensor_copy(
-            wd_dealt[:].rearrange("p a (t m e) -> p a m t e", t=PACK, e=2),
-            wd_raw[:].rearrange("p a (m t e) -> p a m t e", t=PACK, e=2),
-        )
+        def late_chunk():
+            for i in range(PACK):
+                gather(1, i, last)
+                if i % 2 == 1:
+                    weave(1, i // 2, last)
+            quantise_x(1, last)
 
         h_codes = {}
         h_scales = {}
 
-        def hidden(s, b):
-            c = max(n for n in range(len(CHUNKS)) if CHUNKS[n][0] <= TILE * s)
-            cols = slice(TILE * s - CHUNKS[c][0], TILE * (s + 1) - CHUNKS[c][0])
+        def x_operand(a, s):
+            c = max(n for n in range(len(CHUNKS[a])) if CHUNKS[a][n][0] <= TILE * s)
+            cols = slice(TILE * s - CHUNKS[a][c][0], TILE * (s + 1) - CHUNKS[a][c][0])
+            return x_codes[a, c][:, cols].bitcast(E4M3X4), x_scales[a, c][:, cols]
+
+        def hidden(s, b, h, tag):
             banks = [psum.tile([P, PACK, TILE], F32, name=name, bufs=3) for name in ("gate", "up")]
             for a in range(PASSES):
+                codes, scales = x_operand(a, s)
                 for w in range(2):
                     for t in range(PACK):
                         nc.tensor.matmul_mx(
                             out=banks[w][:, t, :],
                             lhsT=dealt[w, a, b][:, P * t : P * (t + 1)].bitcast(E4M3X4),
                             lhsT_scale=up_scale[8 * w + 4 * a : P, SPAN * b + P * t : SPAN * b + P * (t + 1)],
-                            rhs=x_codes[a, c][:, cols].bitcast(E4M3X4),
-                            rhs_scale=x_scales[a, c][:, cols],
+                            rhs=codes,
+                            rhs_scale=scales,
                             start=(a == 0 and t == 0),
                             stop=(a == PASSES - 1 and t == PACK - 1),
                         )
-            act = ring.tile([P, TILE, PACK], F32, name="act")
+            act = keep.tile([P, TILE, PACK], F32, name=tag, align_bytes=64)
             nc.scalar.activation(act[:], banks[0][:].rearrange("p t j -> p j t"), SILU)
-            h = ring.tile([P, TILE, PACK], BF16, name="h", align_bytes=64)
-            nc.vector.tensor_tensor(h[:], banks[1][:].rearrange("p t j -> p j t"), act[:], MULT)
-            h_codes[s, b] = keep.tile([P, TILE], U32, name="h_codes%d%d" % (s, b), align_bytes=64)
-            h_scales[s, b] = keep.tile([P, TILE], U8, name="h_scales%d%d" % (s, b), align_bytes=64)
+            nc.vector.tensor_tensor(h, banks[1][:].rearrange("p t j -> p j t"), act[:], MULT)
+
+        def quantise_h(units, h, tag):
+            codes = keep.tile([P, len(units) * TILE], U32, name=tag, align_bytes=64)
+            scales = keep.tile([P, len(units) * TILE], U8, name="h_scales%d%d" % units[0], align_bytes=64)
             nc.vector.quantize_mx(
-                out=h_codes[s, b][:].bitcast(E4M3X4), scales=h_scales[s, b][:], in_=h[:].rearrange("p j t -> p (j t)")
+                out=codes[:].bitcast(E4M3X4), scales=scales[:], in_=h[:].rearrange("p n j t -> p (n j t)")
             )
+            for n, unit in enumerate(units):
+                h_codes[unit] = codes[:, TILE * n : TILE * (n + 1)]
+                h_scales[unit] = scales[:, TILE * n : TILE * (n + 1)]
 
         y_scales = keep.tile([P, J], U8, name="y_scales", align_bytes=64)
         y_rows = out_0.rearrange("(p t) j -> p t j", t=PACK)
@@ -208,14 +242,14 @@ def tile_list_silu_noneP_kernel(
                         out=bank[:, t, :],
                         lhsT=wd_dealt[:, b, 2 * P * t : 2 * P * (t + 1)].bitcast(E2M1X4),
                         lhsT_scale=down_scale[:, N * b + P * t : N * b + P * (t + 1)],
-                        rhs=h_codes[s, b][:].bitcast(E4M3X4),
-                        rhs_scale=h_scales[s, b][:],
+                        rhs=h_codes[s, b].bitcast(E4M3X4),
+                        rhs_scale=h_scales[s, b],
                         start=(b == 0 and t == 0),
                         stop=(b == PASSES - 1 and t == PACK - 1),
                     )
-            nc.scalar.copy(y[:, :, cols], bank[:])
             rounded = ring.tile([P, TILE, PACK], BF16, name="rounded", align_bytes=64)
             nc.scalar.copy(rounded[:], bank[:].rearrange("p t j -> p j t"))
+            nc.scalar.copy(y[:, :, cols], bank[:])
             nc.vector.quantize_mx(
                 out=y_codes[:, cols].bitcast(E4M3X4),
                 scales=y_scales[:, TILE * s : TILE * (s + 1)],
@@ -225,11 +259,16 @@ def tile_list_silu_noneP_kernel(
                 nc.sync.dma_start(y_rows[:, :, lo:hi], y[:])
                 nc.sync.dma_start(code_rows[:, lo:hi], y_codes[:])
 
-        for s in range(TILES):
-            hidden(s, 0)
-            hidden(s, 1)
-            if s > 0:
-                output(s - 1)
+        groups = [[(0, 0), (1, 0)]] + [[(s + 2, 0), (s, 1)] for s in range(TILES - 2)] + [[(TILES - 2, 1)], [(TILES - 1, 1)]]
+        for g, units in enumerate(groups):
+            h = ring.tile([P, len(units), TILE, PACK], BF16, name="h", align_bytes=64)
+            for n, (s, b) in enumerate(units):
+                hidden(s, b, h[:, n, :, :], "act%d%d" % (s, b))
+            quantise_h(units, h, "h_codes%d" % g)
+            if g == 2:
+                late_chunk()
+            if g >= 2:
+                output(g - 2)
         output(TILES - 1)
         for q in range(4):
             nc.sync.dma_start(out_2[0, 4 * q : 4 * q + 4, :].bitcast(I32), y_scales[32 * q : 32 * q + 4, :].bitcast(I32))

@@ -23,6 +23,7 @@ PASSES = 2
 TILE = 128
 TILES = J // TILE
 CHUNKS = (((0, 512), (512, 1024)), ((0, 128), (128, 256), (256, 512), (512, 768), (768, 1024)))
+ROUND_ON_VECTOR = (6,)
 STORES = ((0, 256), (256, 512), (512, 768), (768, 896), (896, 1024))
 
 
@@ -49,7 +50,7 @@ def tile_list_silu_noneP_kernel(
         nc.gpsimd.memset(down_raw[:].bitcast(I32), 0)
         for w, scales in enumerate((wg_scales, wu_scales)):
             for q in range(4):
-                nc.scalar.dma_start(
+                nc.gpsimd.dma_start(
                     up_raw[32 * q + 8 * w : 32 * q + 8 * w + 8, :].bitcast(I32),
                     scales[:, 4 * q : 4 * q + 4, :].bitcast(I32),
                 )
@@ -64,10 +65,10 @@ def tile_list_silu_noneP_kernel(
             nc.sync.dma_start(planes[a, i][:], rows[:, i, :])
 
         def load_up(a, b):
+            raw[a, b] = keep.tile([P, 2, SPAN], I32, name="raw%d%d" % (a, b))
             for w, words in enumerate((wg_words, wu_words)):
-                raw[w, a, b] = keep.tile([P, SPAN], I32, name="raw%d%d%d" % (w, a, b))
                 src = words[a].rearrange("p r i -> p (r i)").bitcast(I32)
-                nc.sync.dma_start(raw[w, a, b][:], src[:, SPAN * b : SPAN * (b + 1)])
+                nc.sync.dma_start(raw[a, b][:, w, :], src[:, SPAN * b : SPAN * (b + 1)])
 
         load_plane(0, 0)
         for n in range(2):
@@ -97,12 +98,12 @@ def tile_list_silu_noneP_kernel(
 
         woven = {}
 
-        def gather(a, i, c):
+        def gather(a, i, c, tag=None):
             lo, hi = CHUNKS[a][c]
             if i % 2 == 0:
-                late = a == 1 and c == len(CHUNKS[1]) - 1
-                tag = "picked%d%d%d" % ((1, 1, i // 2) if late else (a, i // 2, c))
-                picked[a, i // 2, c] = keep.tile([P, 2, hi - lo], F32, name=tag)
+                picked[a, i // 2, c] = keep.tile(
+                    [P, 2, hi - lo], F32, name=tag or "picked%d%d%d" % (a, i // 2, c), align_bytes=64
+                )
             half = lo // (J // 2)
             nc.vector.tensor_tensor(
                 picked[a, i // 2, c][:, i % 2, :],
@@ -115,7 +116,7 @@ def tile_list_silu_noneP_kernel(
             lo, hi = CHUNKS[a][c]
             if u == 0:
                 woven[a, c] = keep.tile([P, hi - lo, PACK], BF16, name="woven%d%d" % (a, c), align_bytes=64)
-            nc.scalar.copy(woven[a, c][:, :, 2 * u : 2 * u + 2], picked[a, u, c][:].rearrange("p e j -> p j e"))
+            nc.scalar.copy(woven[a, c][:, :, 2 * u : 2 * u + 2], picked[a, u, c][:, :, :].rearrange("p e j -> p j e"))
 
         def quantise_x(a, c):
             lo, hi = CHUNKS[a][c]
@@ -128,11 +129,11 @@ def tile_list_silu_noneP_kernel(
             )
 
         def deal_up(a, b):
-            for w in range(2):
-                dealt[w, a, b] = keep.tile([P, SPAN], I32, name="dealt%d%d%d" % (w, a, b), align_bytes=64)
+            dealt[a, b] = keep.tile([P, 2, SPAN], I32, name="dealt%d%d" % (a, b), align_bytes=64)
+            for ws in ([0], [1]) if (a, b) == (1, 0) else ([0, 1],):
                 nc.vector.tensor_copy(
-                    dealt[w, a, b][:].rearrange("p (t m) -> p m t", t=PACK),
-                    raw[w, a, b][:].rearrange("p (m t) -> p m t", t=PACK),
+                    dealt[a, b][:, ws[0] : ws[-1] + 1, :].rearrange("p w (t m) -> p w m t", t=PACK),
+                    raw[a, b][:, ws[0] : ws[-1] + 1, :].rearrange("p w (m t) -> p w m t", t=PACK),
                 )
 
         early = range(len(CHUNKS[1]) - 1)
@@ -144,16 +145,19 @@ def tile_list_silu_noneP_kernel(
                     weave(0, i // 2, c)
         for c in range(len(CHUNKS[0])):
             quantise_x(0, c)
-        up_scale = keep.tile([P, R], U8, name="plane03", align_bytes=64)
+        wide = keep.tile([P, 2, J // 2], F32, name="picked100", align_bytes=64)
+        for i in range(2):
+            nc.vector.tensor_tensor(wide[:, i, :], planes[1, i][:].indirect(offsets[:, 0 : J // 32]), weight[0][:], MULT)
+            gather(1, i, 3)
+        for c in range(3):
+            picked[1, 0, c] = wide[:, :, CHUNKS[1][c][0] : CHUNKS[1][c][1]]
+            weave(1, 0, c)
+        weave(1, 0, 3)
+        up_scale = keep.tile([P, R], U8, name="woven01", align_bytes=64)
         nc.vector.tensor_copy(
             up_scale[:].rearrange("p (b t m) -> p b t m", b=PASSES, t=PACK),
             up_raw[:].rearrange("p (b m t) -> p b t m", b=PASSES, t=PACK),
         )
-        for i in range(2):
-            for c in early:
-                gather(1, i, c)
-                if i == 1:
-                    weave(1, 0, c)
         deal_up(0, 0)
         for c in early:
             gather(1, 2, c)
@@ -165,23 +169,26 @@ def tile_list_silu_noneP_kernel(
                 deal_up(1, 0)
         deal_up(0, 1)
         deal_up(1, 1)
-        wd_dealt = keep.tile([P, PASSES, 2 * N], U8, name="wd_dealt", align_bytes=64)
-        nc.vector.tensor_copy(
-            wd_dealt[:].bitcast(U16).rearrange("p a (t m) -> p a m t", t=PACK),
-            wd_raw[:].bitcast(U16).rearrange("p a (m t) -> p a m t", t=PACK),
-        )
-        down_scale = keep.tile([P, PASSES * N], U8, name="down_scale", align_bytes=64)
-        nc.vector.tensor_copy(
-            down_scale[:].rearrange("p (b t m) -> p b t m", b=PASSES, t=PACK),
-            down_raw[:].rearrange("p (b m t) -> p b t m", b=PASSES, t=PACK),
-        )
+        down = {}
 
-        def late_chunk():
-            for i in range(PACK):
-                gather(1, i, last)
-                if i % 2 == 1:
-                    weave(1, i // 2, last)
-            quantise_x(1, last)
+        def deal_down_words(tag):
+            down["words"] = keep.tile([P, PASSES, 2 * N], U8, name=tag, align_bytes=64)
+            nc.vector.tensor_copy(
+                down["words"][:].bitcast(U16).rearrange("p a (t m) -> p a m t", t=PACK),
+                wd_raw[:].bitcast(U16).rearrange("p a (m t) -> p a m t", t=PACK),
+            )
+
+        def deal_down_scales(tag):
+            down["scales"] = keep.tile([P, PASSES * N], U8, name=tag, align_bytes=64)
+            nc.vector.tensor_copy(
+                down["scales"][:].rearrange("p (b t m) -> p b t m", b=PASSES, t=PACK),
+                down_raw[:].rearrange("p (b m t) -> p b t m", b=PASSES, t=PACK),
+            )
+
+        def late_pair(u, tag):
+            gather(1, 2 * u, last, tag)
+            gather(1, 2 * u + 1, last)
+            weave(1, u, last)
 
         h_codes = {}
         h_scales = {}
@@ -193,13 +200,13 @@ def tile_list_silu_noneP_kernel(
 
         def hidden(s, b, h, tag):
             banks = [psum.tile([P, PACK, TILE], F32, name=name, bufs=3) for name in ("gate", "up")]
-            for a in range(PASSES):
-                codes, scales = x_operand(a, s)
-                for w in range(2):
+            for w in range(2):
+                for a in range(PASSES):
+                    codes, scales = x_operand(a, s)
                     for t in range(PACK):
                         nc.tensor.matmul_mx(
                             out=banks[w][:, t, :],
-                            lhsT=dealt[w, a, b][:, P * t : P * (t + 1)].bitcast(E4M3X4),
+                            lhsT=dealt[a, b][:, w, P * t : P * (t + 1)].bitcast(E4M3X4),
                             lhsT_scale=up_scale[8 * w + 4 * a : P, SPAN * b + P * t : SPAN * b + P * (t + 1)],
                             rhs=codes,
                             rhs_scale=scales,
@@ -232,32 +239,40 @@ def tile_list_silu_noneP_kernel(
                 staged[g] = (
                     keep.tile([P, PACK, hi - lo], F32, name="y%d" % g),
                     keep.tile([P, hi - lo], I32, name="y_codes%d" % g, align_bytes=64),
+                    ring.tile([P, hi - lo, PACK], BF16, name="rounded", align_bytes=64),
                 )
-            y, y_codes = staged[g]
+            y, y_codes, pair = staged[g]
             cols = slice(TILE * s - lo, TILE * (s + 1) - lo)
             bank = psum.tile([P, PACK, TILE], F32, name="down", bufs=2)
             for b in range(PASSES):
                 for t in range(PACK):
                     nc.tensor.matmul_mx(
                         out=bank[:, t, :],
-                        lhsT=wd_dealt[:, b, 2 * P * t : 2 * P * (t + 1)].bitcast(E2M1X4),
-                        lhsT_scale=down_scale[:, N * b + P * t : N * b + P * (t + 1)],
+                        lhsT=down["words"][:, b, 2 * P * t : 2 * P * (t + 1)].bitcast(E2M1X4),
+                        lhsT_scale=down["scales"][:, N * b + P * t : N * b + P * (t + 1)],
                         rhs=h_codes[s, b].bitcast(E4M3X4),
                         rhs_scale=h_scales[s, b],
                         start=(b == 0 and t == 0),
                         stop=(b == PASSES - 1 and t == PACK - 1),
                     )
-            rounded = ring.tile([P, TILE, PACK], BF16, name="rounded", align_bytes=64)
-            nc.scalar.copy(rounded[:], bank[:].rearrange("p t j -> p j t"))
-            nc.scalar.copy(y[:, :, cols], bank[:])
-            nc.vector.quantize_mx(
-                out=y_codes[:, cols].bitcast(E4M3X4),
-                scales=y_scales[:, TILE * s : TILE * (s + 1)],
-                in_=rounded[:].rearrange("p j t -> p (j t)"),
-            )
+            rounded = pair[:, cols, :]
+            if s in ROUND_ON_VECTOR:
+                nc.scalar.copy(y[:, :, cols], bank[:])
+                nc.vector.tensor_copy(
+                    rounded.rearrange("p (c e) t -> p c t e", e=4),
+                    y[:, :, cols].rearrange("p t (c e) -> p c t e", e=4),
+                )
+            else:
+                nc.scalar.copy(rounded, bank[:].rearrange("p t j -> p j t"))
+                nc.scalar.copy(y[:, :, cols], bank[:])
             if hi == TILE * (s + 1):
-                nc.sync.dma_start(y_rows[:, :, lo:hi], y[:])
+                nc.vector.quantize_mx(
+                    out=y_codes[:].bitcast(E4M3X4),
+                    scales=y_scales[:, lo:hi],
+                    in_=pair[:].rearrange("p j t -> p (j t)"),
+                )
                 nc.sync.dma_start(code_rows[:, lo:hi], y_codes[:])
+                (nc.scalar if hi == J else nc.sync).dma_start(y_rows[:, :, lo:hi], y[:])
 
         groups = [[(0, 0), (1, 0)]] + [[(s + 2, 0), (s, 1)] for s in range(TILES - 2)] + [[(TILES - 2, 1)], [(TILES - 1, 1)]]
         for g, units in enumerate(groups):
@@ -265,10 +280,16 @@ def tile_list_silu_noneP_kernel(
             for n, (s, b) in enumerate(units):
                 hidden(s, b, h[:, n, :, :], "act%d%d" % (s, b))
             quantise_h(units, h, "h_codes%d" % g)
+            if g == 0:
+                deal_down_words("act00")
+                deal_down_scales("act10")
+            if g == 1:
+                late_pair(0, "act20")
             if g == 2:
-                late_chunk()
+                late_pair(1, "act30")
+                quantise_x(1, last)
             if g >= 2:
                 output(g - 2)
         output(TILES - 1)
         for q in range(4):
-            nc.sync.dma_start(out_2[0, 4 * q : 4 * q + 4, :].bitcast(I32), y_scales[32 * q : 32 * q + 4, :].bitcast(I32))
+            (nc.sync if q < 2 else nc.scalar).dma_start(out_2[0, 4 * q : 4 * q + 4, :].bitcast(I32), y_scales[32 * q : 32 * q + 4, :].bitcast(I32))

@@ -22,8 +22,10 @@ SPAN = P * PACK
 PASSES = 2
 TILE = 128
 TILES = J // TILE
-CHUNKS = (((0, 512), (512, 1024)), ((0, 128), (128, 256), (256, 512), (512, 768), (768, 1024)))
-ROUND_ON_VECTOR = (6,)
+HALF = J // 2
+LATE = ((512, 640), (640, 768), (768, 1024))
+EARLY = ((0, 128), (128, 256), (256, 512))
+ROUND_ON_VECTOR = (5, 6)
 STORES = ((0, 256), (256, 512), (512, 768), (768, 896), (896, 1024))
 
 
@@ -55,34 +57,47 @@ def tile_list_silu_noneP_kernel(
                     scales[:, 4 * q : 4 * q + 4, :].bitcast(I32),
                 )
 
-        weight = [keep.tile([P, J // 2], F32, name="weight%d" % n) for n in range(2)]
+        weight = [keep.tile([P, HALF], F32, name="weight%d" % n) for n in range(2)]
         planes = {}
         raw = {}
+        dealt = {}
+        up_words = (wg_words, wu_words)
 
         def load_plane(a, i):
             planes[a, i] = keep.tile([P, T], F32, name="plane%d%d" % (a, i), align_bytes=64)
             rows = xT[SPAN * a : SPAN * (a + 1), :].rearrange("(p i) t -> p i t", i=PACK)
             nc.sync.dma_start(planes[a, i][:], rows[:, i, :])
 
-        def load_up(a, b):
-            raw[a, b] = keep.tile([P, 2, SPAN], I32, name="raw%d%d" % (a, b))
-            for w, words in enumerate((wg_words, wu_words)):
-                src = words[a].rearrange("p r i -> p (r i)").bitcast(I32)
-                nc.sync.dma_start(raw[a, b][:, w, :], src[:, SPAN * b : SPAN * (b + 1)])
+        def load_up(w, b, passes):
+            tile = keep.tile([P, len(passes), SPAN], I32, name="raw%d%d%d" % (w, b, passes[0]))
+            src = up_words[w].rearrange("a p r i -> p a (r i)").bitcast(I32)
+            nc.sync.dma_start(tile[:], src[:, passes[0] : passes[-1] + 1, SPAN * b : SPAN * (b + 1)])
+            raw[w, b, passes] = tile
 
+        def deal_up(w, b, passes):
+            tile = keep.tile([P, len(passes), SPAN], I32, name="dealt%d%d%d" % (w, b, passes[0]), align_bytes=64)
+            nc.vector.tensor_copy(
+                tile[:].rearrange("p a (t m) -> p a m t", t=PACK),
+                raw[w, b, passes][:].rearrange("p a (m t) -> p a m t", t=PACK),
+            )
+            for n, a in enumerate(passes):
+                dealt[w, b, a] = tile[:, n, :]
+
+        nc.sync.dma_start(weight[0][:], wgt[:, 0:HALF])
         load_plane(0, 0)
-        for n in range(2):
-            nc.sync.dma_start(weight[n][:], wgt[:, n * J // 2 : (n + 1) * J // 2])
+        nc.sync.dma_start(weight[1][:], wgt[:, HALF:J])
         for i in range(1, PACK):
             load_plane(0, i)
         load_plane(1, 0)
         load_plane(1, 1)
-        load_up(0, 0)
+        load_up(0, 0, (0,))
+        load_up(1, 0, (0,))
         load_plane(1, 2)
         load_plane(1, 3)
-        load_up(1, 0)
-        load_up(0, 1)
-        load_up(1, 1)
+        load_up(0, 0, (1,))
+        load_up(1, 0, (1,))
+        load_up(0, 1, (0, 1))
+        load_up(1, 1, (0, 1))
         wd_raw = keep.tile([P, PASSES, 2 * N], U8, name="wd_raw")
         nc.sync.dma_start(wd_raw[:].bitcast(I32), wd_words.bitcast(I32).rearrange("a p n -> p a n"))
         for q in range(4):
@@ -91,84 +106,86 @@ def tile_list_silu_noneP_kernel(
                 wd_scales[:, 4 * q : 4 * q + 4, :].bitcast(I32).rearrange("a r n -> r a n"),
             )
 
-        picked = {}
-        x_codes = {}
-        x_scales = {}
-        dealt = {}
+        woven = {
+            (a, half): keep.tile([P, HALF, PACK], BF16, name="woven%d%d" % (a, half), align_bytes=64)
+            for a in range(PASSES)
+            for half in range(2)
+        }
+        x_operands = {}
 
-        woven = {}
-
-        def gather(a, i, c, tag=None):
-            lo, hi = CHUNKS[a][c]
-            if i % 2 == 0:
-                picked[a, i // 2, c] = keep.tile(
-                    [P, 2, hi - lo], F32, name=tag or "picked%d%d%d" % (a, i // 2, c), align_bytes=64
-                )
-            half = lo // (J // 2)
+        def gather(out, a, i, lo, hi):
+            half = lo // HALF
             nc.vector.tensor_tensor(
-                picked[a, i // 2, c][:, i % 2, :],
+                out,
                 planes[a, i][:].indirect(offsets[:, lo // 16 : hi // 16]),
-                weight[half][:, lo - half * J // 2 : hi - half * J // 2],
+                weight[half][:, lo - half * HALF : hi - half * HALF],
                 MULT,
             )
 
-        def weave(a, u, c):
-            lo, hi = CHUNKS[a][c]
-            if u == 0:
-                woven[a, c] = keep.tile([P, hi - lo, PACK], BF16, name="woven%d%d" % (a, c), align_bytes=64)
-            nc.scalar.copy(woven[a, c][:, :, 2 * u : 2 * u + 2], picked[a, u, c][:, :, :].rearrange("p e j -> p j e"))
-
-        def quantise_x(a, c):
-            lo, hi = CHUNKS[a][c]
-            x_codes[a, c] = keep.tile([P, hi - lo], U32, name="x_codes%d%d" % (a, c), align_bytes=64)
-            x_scales[a, c] = keep.tile([P, hi - lo], U8, name="x_scales%d%d" % (a, c), align_bytes=64)
-            nc.vector.quantize_mx(
-                out=x_codes[a, c][:].bitcast(E4M3X4),
-                scales=x_scales[a, c][:],
-                in_=woven[a, c][:].rearrange("p j i -> p (j i)"),
+        def weave(pair, a, u, lo, hi):
+            half = lo // HALF
+            nc.scalar.copy(
+                woven[a, half][:, lo - half * HALF : hi - half * HALF, 2 * u : 2 * u + 2],
+                pair.rearrange("p e j -> p j e"),
             )
 
-        def deal_up(a, b):
-            dealt[a, b] = keep.tile([P, 2, SPAN], I32, name="dealt%d%d" % (a, b), align_bytes=64)
-            for ws in ([0], [1]) if (a, b) == (1, 0) else ([0, 1],):
-                nc.vector.tensor_copy(
-                    dealt[a, b][:, ws[0] : ws[-1] + 1, :].rearrange("p w (t m) -> p w m t", t=PACK),
-                    raw[a, b][:, ws[0] : ws[-1] + 1, :].rearrange("p w (m t) -> p w m t", t=PACK),
-                )
+        def pick_pair(a, u, lo, hi, tag):
+            pair = keep.tile([P, 2, hi - lo], F32, name=tag, align_bytes=64)
+            for e in range(2):
+                gather(pair[:, e, :], a, 2 * u + e, lo, hi)
+            weave(pair[:], a, u, lo, hi)
 
-        early = range(len(CHUNKS[1]) - 1)
-        last = len(CHUNKS[1]) - 1
-        for i in range(PACK):
-            for c in range(len(CHUNKS[0])):
-                gather(0, i, c)
-                if i % 2 == 1:
-                    weave(0, i // 2, c)
-        for c in range(len(CHUNKS[0])):
-            quantise_x(0, c)
-        wide = keep.tile([P, 2, J // 2], F32, name="picked100", align_bytes=64)
-        for i in range(2):
-            nc.vector.tensor_tensor(wide[:, i, :], planes[1, i][:].indirect(offsets[:, 0 : J // 32]), weight[0][:], MULT)
-            gather(1, i, 3)
-        for c in range(3):
-            picked[1, 0, c] = wide[:, :, CHUNKS[1][c][0] : CHUNKS[1][c][1]]
-            weave(1, 0, c)
-        weave(1, 0, 3)
-        up_scale = keep.tile([P, R], U8, name="woven01", align_bytes=64)
+        def quantise_x(a, lo, hi, tag):
+            half = lo // HALF
+            codes = keep.tile([P, hi - lo], U32, name=tag, align_bytes=64)
+            scales = keep.tile([P, hi - lo], U8, name="x_scales%d_%d" % (a, lo), align_bytes=64)
+            nc.vector.quantize_mx(
+                out=codes[:].bitcast(E4M3X4),
+                scales=scales[:],
+                in_=woven[a, half][:, lo - half * HALF : hi - half * HALF, :].rearrange("p j i -> p (j i)"),
+            )
+            for s in range(lo // TILE, hi // TILE):
+                cols = slice(TILE * s - lo, TILE * (s + 1) - lo)
+                x_operands[a, s] = (codes[:, cols].bitcast(E4M3X4), scales[:, cols])
+
+        def pick_whole_pair(a, u):
+            pairs = [keep.tile([P, 2, HALF], F32, name="picked%d%d%d" % (a, u, n), align_bytes=64) for n in range(2)]
+            for e in range(2):
+                for half in range(2):
+                    gather(pairs[half][:, e, :], a, 2 * u + e, HALF * half, HALF * (half + 1))
+                    if e == 1:
+                        weave(pairs[half][:], a, u, HALF * half, HALF * (half + 1))
+
+        pick_whole_pair(0, 0)
+        pick_whole_pair(0, 1)
+        quantise_x(0, 0, HALF, "x_codes0_0")
+        pick_whole_pair(1, 0)
+        up_scale = keep.tile([P, R], U8, name="picked010", align_bytes=64)
         nc.vector.tensor_copy(
             up_scale[:].rearrange("p (b t m) -> p b t m", b=PASSES, t=PACK),
             up_raw[:].rearrange("p (b m t) -> p b t m", b=PASSES, t=PACK),
         )
-        deal_up(0, 0)
-        for c in early:
-            gather(1, 2, c)
-        for c in early:
-            gather(1, 3, c)
-            weave(1, 1, c)
-            quantise_x(1, c)
-            if c == 0:
-                deal_up(1, 0)
-        deal_up(0, 1)
-        deal_up(1, 1)
+        deal_up(0, 0, (0,))
+        deal_up(1, 0, (0,))
+        first = keep.tile([P, 2, HALF], F32, name="picked110", align_bytes=64)
+        gather(first[:, 0, :], 1, 2, 0, HALF)
+
+        def finish_early(c):
+            lo, hi = EARLY[c]
+            gather(first[:, 1, lo:hi], 1, 3, lo, hi)
+            weave(first[:, :, lo:hi], 1, 1, lo, hi)
+
+        def quantise_early(c):
+            quantise_x(1, EARLY[c][0], EARLY[c][1], "x_codes1_%d" % c)
+
+        finish_early(0)
+        finish_early(1)
+        deal_up(0, 0, (1,))
+        quantise_early(0)
+        deal_up(1, 0, (1,))
+        quantise_early(1)
+        finish_early(2)
+
         down = {}
 
         def deal_down_words(tag):
@@ -185,40 +202,40 @@ def tile_list_silu_noneP_kernel(
                 down_raw[:].rearrange("p (b m t) -> p b t m", b=PASSES, t=PACK),
             )
 
-        def late_pair(u, tag):
-            gather(1, 2 * u, last, tag)
-            gather(1, 2 * u + 1, last)
-            weave(1, u, last)
-
         h_codes = {}
         h_scales = {}
+        h_of = {}
 
-        def x_operand(a, s):
-            c = max(n for n in range(len(CHUNKS[a])) if CHUNKS[a][n][0] <= TILE * s)
-            cols = slice(TILE * s - CHUNKS[a][c][0], TILE * (s + 1) - CHUNKS[a][c][0])
-            return x_codes[a, c][:, cols].bitcast(E4M3X4), x_scales[a, c][:, cols]
+        def open_h(units):
+            h = ring.tile([P, len(units), TILE, PACK], BF16, name="h", align_bytes=64)
+            for n, unit in enumerate(units):
+                h_of[unit] = h[:, n, :, :]
+            return h
 
-        def hidden(s, b, h, tag):
+        def hidden(s, b, held=False):
             banks = [psum.tile([P, PACK, TILE], F32, name=name, bufs=3) for name in ("gate", "up")]
             for w in range(2):
                 for a in range(PASSES):
-                    codes, scales = x_operand(a, s)
+                    codes, scales = x_operands[a, s]
                     for t in range(PACK):
                         nc.tensor.matmul_mx(
                             out=banks[w][:, t, :],
-                            lhsT=dealt[a, b][:, w, P * t : P * (t + 1)].bitcast(E4M3X4),
+                            lhsT=dealt[w, b, a][:, P * t : P * (t + 1)].bitcast(E4M3X4),
                             lhsT_scale=up_scale[8 * w + 4 * a : P, SPAN * b + P * t : SPAN * b + P * (t + 1)],
                             rhs=codes,
                             rhs_scale=scales,
                             start=(a == 0 and t == 0),
                             stop=(a == PASSES - 1 and t == PACK - 1),
                         )
-            act = keep.tile([P, TILE, PACK], F32, name=tag, align_bytes=64)
+            if held:
+                act = keep.tile([P, TILE, PACK], F32, name="act%d%d" % (s, b), align_bytes=64)
+            else:
+                act = ring.tile([P, TILE, PACK], F32, name="act", align_bytes=64)
             nc.scalar.activation(act[:], banks[0][:].rearrange("p t j -> p j t"), SILU)
-            nc.vector.tensor_tensor(h, banks[1][:].rearrange("p t j -> p j t"), act[:], MULT)
+            nc.vector.tensor_tensor(h_of[s, b], banks[1][:].rearrange("p t j -> p j t"), act[:], MULT)
 
-        def quantise_h(units, h, tag):
-            codes = keep.tile([P, len(units) * TILE], U32, name=tag, align_bytes=64)
+        def quantise_h(units, h):
+            codes = keep.tile([P, len(units) * TILE], U32, name="h_codes%d%d" % units[0], align_bytes=64)
             scales = keep.tile([P, len(units) * TILE], U8, name="h_scales%d%d" % units[0], align_bytes=64)
             nc.vector.quantize_mx(
                 out=codes[:].bitcast(E4M3X4), scales=scales[:], in_=h[:].rearrange("p n j t -> p (n j t)")
@@ -231,13 +248,14 @@ def tile_list_silu_noneP_kernel(
         y_rows = out_0.rearrange("(p t) j -> p t j", t=PACK)
         code_rows = out_1[0].rearrange("p j i -> p (j i)").bitcast(I32)
         staged = {}
+        y_tags = ("picked000", "picked001", "picked011", "picked100", "picked101")
 
         def output(s):
             g = max(n for n in range(len(STORES)) if STORES[n][0] <= TILE * s)
             lo, hi = STORES[g]
             if lo == TILE * s:
                 staged[g] = (
-                    keep.tile([P, PACK, hi - lo], F32, name="y%d" % g),
+                    keep.tile([P, PACK, hi - lo], F32, name=y_tags[g], align_bytes=64),
                     keep.tile([P, hi - lo], I32, name="y_codes%d" % g, align_bytes=64),
                     ring.tile([P, hi - lo, PACK], BF16, name="rounded", align_bytes=64),
                 )
@@ -274,22 +292,64 @@ def tile_list_silu_noneP_kernel(
                 nc.sync.dma_start(code_rows[:, lo:hi], y_codes[:])
                 (nc.scalar if hi == J else nc.sync).dma_start(y_rows[:, :, lo:hi], y[:])
 
-        groups = [[(0, 0), (1, 0)]] + [[(s + 2, 0), (s, 1)] for s in range(TILES - 2)] + [[(TILES - 2, 1)], [(TILES - 1, 1)]]
-        for g, units in enumerate(groups):
-            h = ring.tile([P, len(units), TILE, PACK], BF16, name="h", align_bytes=64)
-            for n, (s, b) in enumerate(units):
-                hidden(s, b, h[:, n, :, :], "act%d%d" % (s, b))
-            quantise_h(units, h, "h_codes%d" % g)
-            if g == 0:
-                deal_down_words("act00")
-                deal_down_scales("act10")
-            if g == 1:
-                late_pair(0, "act20")
-            if g == 2:
-                late_pair(1, "act30")
-                quantise_x(1, last)
-            if g >= 2:
-                output(g - 2)
-        output(TILES - 1)
+        def late_tiles(c, tag):
+            lo, hi = LATE[c]
+            pick_pair(1, 1, lo, hi, tag)
+
+        def quantise_late(c):
+            quantise_x(1, LATE[c][0], LATE[c][1], "x_codes1_late%d" % c)
+
+        def group(units, held=()):
+            h = open_h(units)
+            for unit in units:
+                hidden(unit[0], unit[1], unit in held)
+            quantise_h(units, h)
+
+        units = [(s, 0) for s in range(4)]
+        h = open_h(units)
+        hidden(0, 0)
+        quantise_early(2)
+        deal_up(0, 1, (0, 1))
+        hidden(1, 0)
+        deal_up(1, 1, (0, 1))
+        hidden(2, 0, True)
+        hidden(3, 0, True)
+        pair_units = [(0, 1), (1, 1)]
+        h2 = open_h(pair_units)
+        hidden(0, 1, True)
+        quantise_h(units, h)
+        hidden(1, 1, True)
+        deal_down_scales("act20")
+        deal_down_words("act30")
+        quantise_h(pair_units, h2)
+        late_tiles(0, "act01")
+        pair_units = [(2, 1), (3, 1)]
+        h3 = open_h(pair_units)
+        hidden(2, 1, True)
+        quantise_x(0, 512, 768, "act11")
+        quantise_late(0)
+        hidden(3, 1, True)
+        quantise_h(pair_units, h3)
+        output(0)
+        output(1)
+        late_tiles(1, "act21")
+        h4 = open_h([(4, 0), (4, 1)])
+        hidden(4, 0, True)
+        quantise_late(1)
+        output(2)
+        late_tiles(2, "act31")
+        hidden(4, 1)
+        quantise_h([(4, 0), (4, 1)], h4)
+        quantise_x(0, 768, 1024, "act40")
+        quantise_late(2)
+        output(3)
+        group([(5, 0), (5, 1)])
+        output(4)
+        group([(6, 0), (6, 1)])
+        output(5)
+        group([(7, 0)])
+        group([(7, 1)])
+        output(6)
+        output(7)
         for q in range(4):
             (nc.sync if q < 2 else nc.scalar).dma_start(out_2[0, 4 * q : 4 * q + 4, :].bitcast(I32), y_scales[32 * q : 32 * q + 4, :].bitcast(I32))

@@ -24,8 +24,8 @@ TILE = 128
 TILES = J // TILE
 HALF = J // 2
 LATE = ((512, 640), (640, 768), (768, 1024))
-EARLY = ((0, 128), (128, 256), (256, 512))
-ROUND_ON_VECTOR = (5, 6)
+EARLY = ((0, 128), (128, 256), (256, 384), (384, 512))
+ROUND_ON_VECTOR = (2, 3, 4)
 STORES = ((0, 256), (256, 512), (512, 768), (768, 896), (896, 1024))
 
 
@@ -47,17 +47,22 @@ def tile_list_silu_noneP_kernel(
         nc.scalar.activation(warm2[:], warm[:], SILU)
 
         up_raw = keep.tile([P, R], U8, name="up_raw", align_bytes=64)
-        down_raw = keep.tile([P, PASSES * N], U8, name="down_raw", align_bytes=64)
-        nc.gpsimd.memset(up_raw[:].bitcast(I32), 0)
-        nc.gpsimd.memset(down_raw[:].bitcast(I32), 0)
+        down_scale = keep.tile([P, PASSES * N], U8, name="down_scale", align_bytes=64)
+        nc.vector.memset(up_raw[:].bitcast(I32), 0)
+        nc.vector.memset(down_scale[:].bitcast(I32), 0)
         for w, scales in enumerate((wg_scales, wu_scales)):
             for q in range(4):
                 nc.gpsimd.dma_start(
                     up_raw[32 * q + 8 * w : 32 * q + 8 * w + 8, :].bitcast(I32),
                     scales[:, 4 * q : 4 * q + 4, :].bitcast(I32),
                 )
+        for q in range(4):
+            nc.gpsimd.dma_start(
+                up_raw[32 * q + 16 : 32 * q + 20, :].bitcast(I32).rearrange("r (a n) -> r a n", a=PASSES),
+                wd_scales[:, 4 * q : 4 * q + 4, :].bitcast(I32).rearrange("a r n -> r a n"),
+            )
 
-        weight = [keep.tile([P, HALF], F32, name="weight%d" % n) for n in range(2)]
+        weight = keep.tile([P, J], F32, name="weight")
         planes = {}
         raw = {}
         dealt = {}
@@ -69,7 +74,7 @@ def tile_list_silu_noneP_kernel(
             nc.sync.dma_start(planes[a, i][:], rows[:, i, :])
 
         def load_up(w, b, passes):
-            tile = keep.tile([P, len(passes), SPAN], I32, name="raw%d%d%d" % (w, b, passes[0]))
+            tile = keep.tile([P, len(passes), SPAN], I32, name="raw%d%d%d" % (w, b, passes[0]), align_bytes=64)
             src = up_words[w].rearrange("a p r i -> p a (r i)").bitcast(I32)
             nc.sync.dma_start(tile[:], src[:, passes[0] : passes[-1] + 1, SPAN * b : SPAN * (b + 1)])
             raw[w, b, passes] = tile
@@ -83,9 +88,9 @@ def tile_list_silu_noneP_kernel(
             for n, a in enumerate(passes):
                 dealt[w, b, a] = tile[:, n, :]
 
-        nc.sync.dma_start(weight[0][:], wgt[:, 0:HALF])
+        nc.sync.dma_start(weight[:, 0:HALF], wgt[:, 0:HALF])
         load_plane(0, 0)
-        nc.sync.dma_start(weight[1][:], wgt[:, HALF:J])
+        nc.sync.dma_start(weight[:, HALF:J], wgt[:, HALF:J])
         for i in range(1, PACK):
             load_plane(0, i)
         load_plane(1, 0)
@@ -100,34 +105,15 @@ def tile_list_silu_noneP_kernel(
         load_up(1, 1, (0, 1))
         wd_raw = keep.tile([P, PASSES, 2 * N], U8, name="wd_raw")
         nc.sync.dma_start(wd_raw[:].bitcast(I32), wd_words.bitcast(I32).rearrange("a p n -> p a n"))
-        for q in range(4):
-            nc.sync.dma_start(
-                down_raw[32 * q : 32 * q + 4, :].bitcast(I32).rearrange("r (a n) -> r a n", a=PASSES),
-                wd_scales[:, 4 * q : 4 * q + 4, :].bitcast(I32).rearrange("a r n -> r a n"),
-            )
 
-        woven = {
-            (a, half): keep.tile([P, HALF, PACK], BF16, name="woven%d%d" % (a, half), align_bytes=64)
-            for a in range(PASSES)
-            for half in range(2)
-        }
+        woven = [keep.tile([P, J, PACK], BF16, name="woven%d" % a, align_bytes=64) for a in range(PASSES)]
         x_operands = {}
 
         def gather(out, a, i, lo, hi):
-            half = lo // HALF
-            nc.vector.tensor_tensor(
-                out,
-                planes[a, i][:].indirect(offsets[:, lo // 16 : hi // 16]),
-                weight[half][:, lo - half * HALF : hi - half * HALF],
-                MULT,
-            )
+            nc.vector.tensor_tensor(out, planes[a, i][:].indirect(offsets[:, lo // 16 : hi // 16]), weight[:, lo:hi], MULT)
 
         def weave(pair, a, u, lo, hi):
-            half = lo // HALF
-            nc.scalar.copy(
-                woven[a, half][:, lo - half * HALF : hi - half * HALF, 2 * u : 2 * u + 2],
-                pair.rearrange("p e j -> p j e"),
-            )
+            nc.scalar.copy(woven[a][:, lo:hi, 2 * u : 2 * u + 2], pair.rearrange("p e j -> p j e"))
 
         def pick_pair(a, u, lo, hi, tag):
             pair = keep.tile([P, 2, hi - lo], F32, name=tag, align_bytes=64)
@@ -136,42 +122,43 @@ def tile_list_silu_noneP_kernel(
             weave(pair[:], a, u, lo, hi)
 
         def quantise_x(a, lo, hi, tag):
-            half = lo // HALF
             codes = keep.tile([P, hi - lo], U32, name=tag, align_bytes=64)
             scales = keep.tile([P, hi - lo], U8, name="x_scales%d_%d" % (a, lo), align_bytes=64)
             nc.vector.quantize_mx(
                 out=codes[:].bitcast(E4M3X4),
                 scales=scales[:],
-                in_=woven[a, half][:, lo - half * HALF : hi - half * HALF, :].rearrange("p j i -> p (j i)"),
+                in_=woven[a][:, lo:hi, :].rearrange("p j i -> p (j i)"),
             )
             for s in range(lo // TILE, hi // TILE):
                 cols = slice(TILE * s - lo, TILE * (s + 1) - lo)
                 x_operands[a, s] = (codes[:, cols].bitcast(E4M3X4), scales[:, cols])
 
-        def pick_whole_pair(a, u):
-            pairs = [keep.tile([P, 2, HALF], F32, name="picked%d%d%d" % (a, u, n), align_bytes=64) for n in range(2)]
-            for e in range(2):
-                for half in range(2):
-                    gather(pairs[half][:, e, :], a, 2 * u + e, HALF * half, HALF * (half + 1))
-                    if e == 1:
-                        weave(pairs[half][:], a, u, HALF * half, HALF * (half + 1))
+        def pick_cut(a, u, cuts0, cuts1):
+            pair = keep.tile([P, 2, cuts0[-1]], F32, name="picked%d%d" % (a, u), align_bytes=64)
+            for lo, hi in zip(cuts0, cuts0[1:]):
+                gather(pair[:, 0, lo:hi], a, 2 * u, lo, hi)
+            for lo, hi in zip(cuts1, cuts1[1:]):
+                gather(pair[:, 1, lo:hi], a, 2 * u + 1, lo, hi)
+                weave(pair[:, :, lo:hi], a, u, lo, hi)
 
-        pick_whole_pair(0, 0)
-        pick_whole_pair(0, 1)
-        quantise_x(0, 0, HALF, "x_codes0_0")
-        pick_whole_pair(1, 0)
-        up_scale = keep.tile([P, R], U8, name="picked010", align_bytes=64)
+        pick_cut(0, 0, (0, HALF, J), (0, J))
+        pick_cut(0, 1, (0, J), (0, HALF, J))
+        up_scale = keep.tile([P, R], U8, name="plane02", align_bytes=64)
         nc.vector.tensor_copy(
             up_scale[:].rearrange("p (b t m) -> p b t m", b=PASSES, t=PACK),
             up_raw[:].rearrange("p (b m t) -> p b t m", b=PASSES, t=PACK),
         )
+        for q in range(4):
+            nc.gpsimd.dma_start(down_scale[32 * q : 32 * q + 4, :].bitcast(I32), up_scale[32 * q + 16 : 32 * q + 20, :].bitcast(I32))
+        pick_cut(1, 0, (0, 768), (0, HALF, 768))
         deal_up(0, 0, (0,))
+        quantise_x(0, 0, HALF, "raw000")
         deal_up(1, 0, (0,))
-        first = keep.tile([P, 2, HALF], F32, name="picked110", align_bytes=64)
+        first = keep.tile([P, 2, HALF], F32, name="picked11", align_bytes=64)
         gather(first[:, 0, :], 1, 2, 0, HALF)
 
-        def finish_early(c):
-            lo, hi = EARLY[c]
+        def finish_early(s):
+            lo, hi = TILE * s, TILE * (s + 1)
             gather(first[:, 1, lo:hi], 1, 3, lo, hi)
             weave(first[:, :, lo:hi], 1, 1, lo, hi)
 
@@ -185,6 +172,8 @@ def tile_list_silu_noneP_kernel(
         deal_up(1, 0, (1,))
         quantise_early(1)
         finish_early(2)
+        quantise_early(2)
+        finish_early(3)
 
         down = {}
 
@@ -193,13 +182,6 @@ def tile_list_silu_noneP_kernel(
             nc.vector.tensor_copy(
                 down["words"][:].bitcast(U16).rearrange("p a (t m) -> p a m t", t=PACK),
                 wd_raw[:].bitcast(U16).rearrange("p a (m t) -> p a m t", t=PACK),
-            )
-
-        def deal_down_scales(tag):
-            down["scales"] = keep.tile([P, PASSES * N], U8, name=tag, align_bytes=64)
-            nc.vector.tensor_copy(
-                down["scales"][:].rearrange("p (b t m) -> p b t m", b=PASSES, t=PACK),
-                down_raw[:].rearrange("p (b m t) -> p b t m", b=PASSES, t=PACK),
             )
 
         h_codes = {}
@@ -248,7 +230,7 @@ def tile_list_silu_noneP_kernel(
         y_rows = out_0.rearrange("(p t) j -> p t j", t=PACK)
         code_rows = out_1[0].rearrange("p j i -> p (j i)").bitcast(I32)
         staged = {}
-        y_tags = ("picked000", "picked001", "picked011", "picked100", "picked101")
+        y_tags = ("picked00", "picked01", "picked10", "picked11", "y4")
 
         def output(s):
             g = max(n for n in range(len(STORES)) if STORES[n][0] <= TILE * s)
@@ -267,7 +249,7 @@ def tile_list_silu_noneP_kernel(
                     nc.tensor.matmul_mx(
                         out=bank[:, t, :],
                         lhsT=down["words"][:, b, 2 * P * t : 2 * P * (t + 1)].bitcast(E2M1X4),
-                        lhsT_scale=down["scales"][:, N * b + P * t : N * b + P * (t + 1)],
+                        lhsT_scale=down_scale[:, N * b + P * t : N * b + P * (t + 1)],
                         rhs=h_codes[s, b].bitcast(E4M3X4),
                         rhs_scale=h_scales[s, b],
                         start=(b == 0 and t == 0),
@@ -308,7 +290,7 @@ def tile_list_silu_noneP_kernel(
         units = [(s, 0) for s in range(4)]
         h = open_h(units)
         hidden(0, 0)
-        quantise_early(2)
+        quantise_early(3)
         deal_up(0, 1, (0, 1))
         hidden(1, 0)
         deal_up(1, 1, (0, 1))
@@ -317,33 +299,36 @@ def tile_list_silu_noneP_kernel(
         pair_units = [(0, 1), (1, 1)]
         h2 = open_h(pair_units)
         hidden(0, 1, True)
-        quantise_h(units, h)
+        late_tiles(0, "act20")
         hidden(1, 1, True)
-        deal_down_scales("act20")
-        deal_down_words("act30")
+        quantise_x(0, 512, 768, "act30")
+        quantise_late(0)
+        quantise_h(units, h)
+        deal_down_words("act01")
         quantise_h(pair_units, h2)
-        late_tiles(0, "act01")
         pair_units = [(2, 1), (3, 1)]
         h3 = open_h(pair_units)
         hidden(2, 1, True)
-        quantise_x(0, 512, 768, "act11")
-        quantise_late(0)
+        late_tiles(1, "act11")
         hidden(3, 1, True)
+        quantise_late(1)
         quantise_h(pair_units, h3)
         output(0)
-        output(1)
-        late_tiles(1, "act21")
         h4 = open_h([(4, 0), (4, 1)])
         hidden(4, 0, True)
-        quantise_late(1)
+        output(1)
+        pick_pair(1, 0, 768, 1024, "act21")
+        hidden(4, 1, True)
+        quantise_h([(4, 0), (4, 1)], h4)
         output(2)
         late_tiles(2, "act31")
-        hidden(4, 1)
-        quantise_h([(4, 0), (4, 1)], h4)
+        h5 = open_h([(5, 0), (5, 1)])
+        hidden(5, 0)
         quantise_x(0, 768, 1024, "act40")
         quantise_late(2)
         output(3)
-        group([(5, 0), (5, 1)])
+        hidden(5, 1)
+        quantise_h([(5, 0), (5, 1)], h5)
         output(4)
         group([(6, 0), (6, 1)])
         output(5)
@@ -352,4 +337,4 @@ def tile_list_silu_noneP_kernel(
         output(6)
         output(7)
         for q in range(4):
-            (nc.sync if q < 2 else nc.scalar).dma_start(out_2[0, 4 * q : 4 * q + 4, :].bitcast(I32), y_scales[32 * q : 32 * q + 4, :].bitcast(I32))
+            nc.sync.dma_start(out_2[0, 4 * q : 4 * q + 4, :].bitcast(I32), y_scales[32 * q : 32 * q + 4, :].bitcast(I32))

@@ -57,7 +57,7 @@ def tile_list_silu_noneP_kernel(
                     scales[:, 4 * q : 4 * q + 4, :].bitcast(I32),
                 )
         for q in range(4):
-            nc.gpsimd.dma_start(
+            nc.scalar.dma_start(
                 up_raw[32 * q + 16 : 32 * q + 20, :].bitcast(I32).rearrange("r (a n) -> r a n", a=PASSES),
                 wd_scales[:, 4 * q : 4 * q + 4, :].bitcast(I32).rearrange("a r n -> r a n"),
             )
@@ -143,7 +143,7 @@ def tile_list_silu_noneP_kernel(
 
         pick_cut(0, 0, (0, HALF, J), (0, J))
         pick_cut(0, 1, (0, J), (0, HALF, J))
-        up_scale = keep.tile([P, R], U8, name="plane02", align_bytes=64)
+        up_scale = keep.tile([P, R], U8, name="plane03", align_bytes=64)
         nc.vector.tensor_copy(
             up_scale[:].rearrange("p (b t m) -> p b t m", b=PASSES, t=PACK),
             up_raw[:].rearrange("p (b m t) -> p b t m", b=PASSES, t=PACK),

@@ -88,9 +88,9 @@ def tile_list_silu_noneP_kernel(
             for n, a in enumerate(passes):
                 dealt[w, b, a] = tile[:, n, :]
 
-        nc.sync.dma_start(weight[:, 0:HALF], wgt[:, 0:HALF])
+        nc.sync.dma_start(weight[:, 0:256], wgt[:, 0:256])
         load_plane(0, 0)
-        nc.sync.dma_start(weight[:, HALF:J], wgt[:, HALF:J])
+        nc.sync.dma_start(weight[:, 256:J], wgt[:, 256:J])
         for i in range(1, PACK):
             load_plane(0, i)
         load_plane(1, 0)
@@ -141,7 +141,7 @@ def tile_list_silu_noneP_kernel(
                 gather(pair[:, 1, lo:hi], a, 2 * u + 1, lo, hi)
                 weave(pair[:, :, lo:hi], a, u, lo, hi)
 
-        pick_cut(0, 0, (0, HALF, J), (0, J))
+        pick_cut(0, 0, (0, 256, J), (0, J))
         pick_cut(0, 1, (0, J), (0, HALF, J))
         up_scale = keep.tile([P, R], U8, name="plane03", align_bytes=64)
         nc.vector.tensor_copy(
@@ -149,7 +149,7 @@ def tile_list_silu_noneP_kernel(
             up_raw[:].rearrange("p (b m t) -> p b t m", b=PASSES, t=PACK),
         )
         for q in range(4):
-            nc.gpsimd.dma_start(down_scale[32 * q : 32 * q + 4, :].bitcast(I32), up_scale[32 * q + 16 : 32 * q + 20, :].bitcast(I32))
+            nc.sync.dma_start(down_scale[32 * q : 32 * q + 4, :].bitcast(I32), up_scale[32 * q + 16 : 32 * q + 20, :].bitcast(I32))
         pick_cut(1, 0, (0, 768), (0, HALF, 768))
         deal_up(0, 0, (0,))
         quantise_x(0, 0, HALF, "raw000")

@@ -1,6 +1,7 @@
 from contextlib import ExitStack
 
 import concourse.mybir as mybir
+from concourse.masks import make_identity
 
 K, R, N, T, J = 1024, 1024, 512, 2048, 1024
 FLOPS = 2 * J * (2 * K * R + R * N)
@@ -88,9 +89,24 @@ def tile_list_silu_noneP_kernel(
             for n, a in enumerate(passes):
                 dealt[w, b, a] = tile[:, n, :]
 
-        nc.sync.dma_start(weight[:, 0:256], wgt[:, 0:256])
+        ident = keep.tile([P, P], F32, name="ident", align_bytes=64)
+        make_identity(nc, ident[:])
+        head_rows = keep.tile([P, P], F32, name="head_rows", align_bytes=64)
+        nc.vector.memset(head_rows[64:P, :], 0.0)
+        nc.sync.dma_start(head_rows[0:64, :], wgt[0:P:16, :].rearrange("g (c j) -> g c j", j=P))
         load_plane(0, 0)
-        nc.sync.dma_start(weight[:, 256:J], wgt[:, 256:J])
+        turned = psum.tile([P, P], F32, name="down", bufs=2)
+        nc.tensor.transpose(turned[:], head_rows[:], ident[:])
+        spread = keep.tile([P, TILES, 8, 16], F32, name="spread", align_bytes=64)
+        for lo, hi, tag in ((0, 2, "gate"), (2, 5, "up"), (5, 8, "gate")):
+            nc.vector.tensor_copy(
+                spread[:, lo:hi, :, :],
+                turned[:, 0:64].rearrange("p (g c) -> p c g", g=8)[:, lo:hi, :].unsqueeze(3).to_broadcast([P, hi - lo, 8, 16]),
+            )
+            back = psum.tile([P, hi - lo, P], F32, name=tag, bufs=3)
+            for c in range(lo, hi):
+                nc.tensor.transpose(back[:, c - lo, :], spread[:, c, :, :].rearrange("p g r -> p (g r)"), ident[:])
+            nc.scalar.copy(weight[:, P * lo : P * hi], back[:].rearrange("p c j -> p (c j)"))
         for i in range(1, PACK):
             load_plane(0, i)
         load_plane(1, 0)

@@ -24,10 +24,9 @@ PASSES = 2
 TILE = 128
 TILES = J // TILE
 HALF = J // 2
-LATE = ((512, 640), (640, 768), (768, 1024))
-EARLY = ((0, 128), (128, 256), (256, 384), (384, 512))
-ROUND_ON_VECTOR = (2, 3, 4)
-STORES = ((0, 256), (256, 512), (512, 768), (768, 896), (896, 1024))
+PAIR = 2 * TILE
+RUN = 4
+STORES = ((512, 640), (640, 768), (768, 896), (896, 1024))
 
 
 def tile_list_silu_noneP_kernel(
@@ -36,7 +35,6 @@ def tile_list_silu_noneP_kernel(
     nc = tc.nc
     with ExitStack() as ctx:
         keep = ctx.enter_context(tc.tile_pool(name="keep", bufs=1))
-        ring = ctx.enter_context(tc.tile_pool(name="ring", bufs=3))
         psum = ctx.enter_context(tc.psum_pool(name="psum", bufs=1))
 
         offsets = keep.tile([P, J // 16], U16, name="offsets")
@@ -95,47 +93,47 @@ def tile_list_silu_noneP_kernel(
         nc.vector.memset(head_rows[64:P, :], 0.0)
         nc.sync.dma_start(head_rows[0:64, :], wgt[0:P:16, :].rearrange("g (c j) -> g c j", j=P))
         load_plane(0, 0)
-        turned = psum.tile([P, P], F32, name="down", bufs=2)
+        turned = psum.tile([P, P], F32, name="bank", bufs=8)
         nc.tensor.transpose(turned[:], head_rows[:], ident[:])
         spread = keep.tile([P, TILES, 8, 16], F32, name="spread", align_bytes=64)
-        for lo, hi, tag in ((0, 2, "gate"), (2, 5, "up"), (5, 8, "gate")):
+        for lo, hi in ((0, 2), (2, 5), (5, 8)):
             nc.vector.tensor_copy(
                 spread[:, lo:hi, :, :],
                 turned[:, 0:64].rearrange("p (g c) -> p c g", g=8)[:, lo:hi, :].unsqueeze(3).to_broadcast([P, hi - lo, 8, 16]),
             )
-            back = psum.tile([P, hi - lo, P], F32, name=tag, bufs=3)
+            back = psum.tile([P, hi - lo, P], F32, name="bank", bufs=8)
             for c in range(lo, hi):
                 nc.tensor.transpose(back[:, c - lo, :], spread[:, c, :, :].rearrange("p g r -> p (g r)"), ident[:])
             nc.scalar.copy(weight[:, P * lo : P * hi], back[:].rearrange("p c j -> p (c j)"))
         for i in range(1, PACK):
             load_plane(0, i)
         load_plane(1, 0)
-        load_plane(1, 1)
         load_up(0, 0, (0,))
-        load_up(1, 0, (0,))
+        load_plane(1, 1)
         load_plane(1, 2)
+        load_up(1, 0, (0,))
         load_plane(1, 3)
         load_up(0, 0, (1,))
         load_up(1, 0, (1,))
         load_up(0, 1, (0, 1))
         load_up(1, 1, (0, 1))
-        wd_raw = keep.tile([P, PASSES, 2 * N], U8, name="wd_raw")
+        wd_raw = keep.tile([P, PASSES, 2 * N], U8, name="wd_raw", align_bytes=64)
         nc.sync.dma_start(wd_raw[:].bitcast(I32), wd_words.bitcast(I32).rearrange("a p n -> p a n"))
 
         woven = [keep.tile([P, J, PACK], BF16, name="woven%d" % a, align_bytes=64) for a in range(PASSES)]
         x_operands = {}
+
+        def by_runs(slots_first):
+            return slots_first.rearrange("p t (c e) -> p c t e", e=RUN)
+
+        def as_runs(columns_first):
+            return columns_first.rearrange("p (c e) t -> p c t e", e=RUN)
 
         def gather(out, a, i, lo, hi):
             nc.vector.tensor_tensor(out, planes[a, i][:].indirect(offsets[:, lo // 16 : hi // 16]), weight[:, lo:hi], MULT)
 
         def weave(pair, a, u, lo, hi):
             nc.scalar.copy(woven[a][:, lo:hi, 2 * u : 2 * u + 2], pair.rearrange("p e j -> p j e"))
-
-        def pick_pair(a, u, lo, hi, tag):
-            pair = keep.tile([P, 2, hi - lo], F32, name=tag, align_bytes=64)
-            for e in range(2):
-                gather(pair[:, e, :], a, 2 * u + e, lo, hi)
-            weave(pair[:], a, u, lo, hi)
 
         def quantise_x(a, lo, hi, tag):
             codes = keep.tile([P, hi - lo], U32, name=tag, align_bytes=64)
@@ -145,9 +143,10 @@ def tile_list_silu_noneP_kernel(
                 scales=scales[:],
                 in_=woven[a][:, lo:hi, :].rearrange("p j i -> p (j i)"),
             )
-            for s in range(lo // TILE, hi // TILE):
-                cols = slice(TILE * s - lo, TILE * (s + 1) - lo)
-                x_operands[a, s] = (codes[:, cols].bitcast(E4M3X4), scales[:, cols])
+            for width in (TILE, PAIR):
+                for c in range(lo, hi - width + 1, width):
+                    cols = slice(c - lo, c - lo + width)
+                    x_operands[a, c, width] = (codes[:, cols].bitcast(E4M3X4), scales[:, cols])
 
         def pick_cut(a, u, cuts0, cuts1):
             pair = keep.tile([P, 2, cuts0[-1]], F32, name="picked%d%d" % (a, u), align_bytes=64)
@@ -157,7 +156,19 @@ def tile_list_silu_noneP_kernel(
                 gather(pair[:, 1, lo:hi], a, 2 * u + 1, lo, hi)
                 weave(pair[:, :, lo:hi], a, u, lo, hi)
 
-        pick_cut(0, 0, (0, 256, J), (0, J))
+        def pick_late(lo, tag):
+            four = keep.tile([P, PACK, PAIR], F32, name=tag, align_bytes=64)
+            for i in range(PACK):
+                gather(four[:, i, :], 1, i, lo, lo + PAIR)
+            nc.scalar.copy(as_runs(woven[1][:, lo : lo + PAIR, :]), by_runs(four[:]))
+
+        def pick_pair(u, lo, tag):
+            pair = keep.tile([P, 2, PAIR], F32, name=tag, align_bytes=64)
+            for e in range(2):
+                gather(pair[:, e, :], 1, 2 * u + e, lo, lo + PAIR)
+            weave(pair[:], 1, u, lo, lo + PAIR)
+
+        pick_cut(0, 0, (0, 256, 640, J), (0, J))
         pick_cut(0, 1, (0, J), (0, HALF, J))
         up_scale = keep.tile([P, R], U8, name="plane03", align_bytes=64)
         nc.vector.tensor_copy(
@@ -166,30 +177,93 @@ def tile_list_silu_noneP_kernel(
         )
         for q in range(4):
             nc.sync.dma_start(down_scale[32 * q : 32 * q + 4, :].bitcast(I32), up_scale[32 * q + 16 : 32 * q + 20, :].bitcast(I32))
-        pick_cut(1, 0, (0, 768), (0, HALF, 768))
+        quantise_x(0, 0, HALF, "x_codes0_0")
+        pick_cut(1, 0, (0, HALF), (0, HALF))
         deal_up(0, 0, (0,))
-        quantise_x(0, 0, HALF, "raw000")
-        deal_up(1, 0, (0,))
         first = keep.tile([P, 2, HALF], F32, name="picked11", align_bytes=64)
         gather(first[:, 0, :], 1, 2, 0, HALF)
+        deal_up(1, 0, (0,))
+
+        def new_bank(slots, width):
+            return psum.tile([P, slots, width], F32, name="bank", bufs=8)
+
+        def up_pass(bank, w, b, a, lo, width, slots, opens, closes):
+            codes, scales = x_operands[a, lo, width]
+            for n, t in enumerate(slots):
+                nc.tensor.matmul_mx(
+                    out=bank[:, n, :],
+                    lhsT=dealt[w, b, a][:, P * t : P * (t + 1)].bitcast(E4M3X4),
+                    lhsT_scale=up_scale[8 * w + 4 * a : P, SPAN * b + P * t : SPAN * b + P * (t + 1)],
+                    rhs=codes,
+                    rhs_scale=scales,
+                    start=(opens and n == 0),
+                    stop=(closes and n == len(slots) - 1),
+                )
+
+        all_slots = range(PACK)
+        lead = [[new_bank(PACK, TILE) for s in range(4)] for w in range(2)]
+        for w in range(2):
+            for s in range(4):
+                up_pass(lead[w][s], w, 0, 0, TILE * s, TILE, all_slots, True, False)
+
+        h = [keep.tile([P, J, PACK], BF16, name="h%d" % b, align_bytes=64) for b in range(PASSES)]
+        h_codes = [keep.tile([P, J], U32, name="h_codes%d" % b, align_bytes=64) for b in range(PASSES)]
+        h_scales = [keep.tile([P, J], U8, name="h_scales%d" % b, align_bytes=64) for b in range(PASSES)]
+        acts = {}
+
+        def product(bank, act, s, b):
+            nc.vector.tensor_tensor(as_runs(h[b][:, TILE * s : TILE * (s + 1), :]), by_runs(bank[:]), by_runs(act), MULT)
 
         def finish_early(s):
             lo, hi = TILE * s, TILE * (s + 1)
             gather(first[:, 1, lo:hi], 1, 3, lo, hi)
             weave(first[:, :, lo:hi], 1, 1, lo, hi)
 
-        def quantise_early(c):
-            quantise_x(1, EARLY[c][0], EARLY[c][1], "x_codes1_%d" % c)
+        lead_codes = keep.tile([P, HALF], U32, name="lead_codes", align_bytes=64)
+        lead_scales = keep.tile([P, HALF], U8, name="lead_scales", align_bytes=64)
+        for width in (TILE, PAIR):
+            for c in range(0, HALF, width):
+                x_operands[1, c, width] = (lead_codes[:, c : c + width].bitcast(E4M3X4), lead_scales[:, c : c + width])
 
-        finish_early(0)
-        finish_early(1)
-        deal_up(0, 0, (1,))
-        quantise_early(0)
-        deal_up(1, 0, (1,))
-        quantise_early(1)
-        finish_early(2)
-        quantise_early(2)
-        finish_early(3)
+        def lead_unit(s):
+            lo = TILE * s
+            cols = slice(lo, lo + TILE)
+            nc.vector.quantize_mx(
+                out=lead_codes[:, cols].bitcast(E4M3X4),
+                scales=lead_scales[:, cols],
+                in_=woven[1][:, cols, :].rearrange("p j i -> p (j i)"),
+            )
+            for w in range(2):
+                up_pass(lead[w][s], w, 0, 1, lo, TILE, all_slots, False, True)
+            acts[s] = keep.tile([P, PACK, TILE], F32, name="lead_act%d" % s, align_bytes=64)
+            nc.scalar.activation(acts[s][:], lead[0][s][:], SILU)
+
+        def gate_pair(g, b):
+            act = keep.tile([P, PACK, PAIR], F32, name="act%d%d" % (g, b), align_bytes=64)
+            for u in range(2):
+                bank = new_bank(2, PAIR)
+                for a in range(PASSES):
+                    up_pass(bank, 0, b, a, PAIR * g, PAIR, (2 * u, 2 * u + 1), a == 0, a == 1)
+                nc.scalar.activation(act[:, 2 * u : 2 * u + 2, :], bank[:], SILU)
+            acts[g, b] = act
+
+        ups = {}
+
+        def up_tile(s, b):
+            ups[s, b] = new_bank(PACK, TILE)
+            for a in range(PASSES):
+                up_pass(ups[s, b], 1, b, a, TILE * s, TILE, all_slots, a == 0, a == 1)
+
+        def multiply(s, b):
+            e = s % 2
+            product(ups[s, b], acts[s // 2, b][:, :, TILE * e : TILE * (e + 1)], s, b)
+
+        def quantise_h(b, lo, hi):
+            nc.vector.quantize_mx(
+                out=h_codes[b][:, lo:hi].bitcast(E4M3X4),
+                scales=h_scales[b][:, lo:hi],
+                in_=h[b][:, lo:hi, :].rearrange("p j t -> p (j t)"),
+            )
 
         down = {}
 
@@ -200,157 +274,150 @@ def tile_list_silu_noneP_kernel(
                 wd_raw[:].bitcast(U16).rearrange("p a (m t) -> p a m t", t=PACK),
             )
 
-        h_codes = {}
-        h_scales = {}
-        h_of = {}
-
-        def open_h(units):
-            h = ring.tile([P, len(units), TILE, PACK], BF16, name="h", align_bytes=64)
-            for n, unit in enumerate(units):
-                h_of[unit] = h[:, n, :, :]
-            return h
-
-        def hidden(s, b, held=False):
-            banks = [psum.tile([P, PACK, TILE], F32, name=name, bufs=3) for name in ("gate", "up")]
-            for w in range(2):
-                for a in range(PASSES):
-                    codes, scales = x_operands[a, s]
-                    for t in range(PACK):
-                        nc.tensor.matmul_mx(
-                            out=banks[w][:, t, :],
-                            lhsT=dealt[w, b, a][:, P * t : P * (t + 1)].bitcast(E4M3X4),
-                            lhsT_scale=up_scale[8 * w + 4 * a : P, SPAN * b + P * t : SPAN * b + P * (t + 1)],
-                            rhs=codes,
-                            rhs_scale=scales,
-                            start=(a == 0 and t == 0),
-                            stop=(a == PASSES - 1 and t == PACK - 1),
-                        )
-            if held:
-                act = keep.tile([P, TILE, PACK], F32, name="act%d%d" % (s, b), align_bytes=64)
-            else:
-                act = ring.tile([P, TILE, PACK], F32, name="act", align_bytes=64)
-            nc.scalar.activation(act[:], banks[0][:].rearrange("p t j -> p j t"), SILU)
-            nc.vector.tensor_tensor(h_of[s, b], banks[1][:].rearrange("p t j -> p j t"), act[:], MULT)
-
-        def quantise_h(units, h):
-            codes = keep.tile([P, len(units) * TILE], U32, name="h_codes%d%d" % units[0], align_bytes=64)
-            scales = keep.tile([P, len(units) * TILE], U8, name="h_scales%d%d" % units[0], align_bytes=64)
-            nc.vector.quantize_mx(
-                out=codes[:].bitcast(E4M3X4), scales=scales[:], in_=h[:].rearrange("p n j t -> p (n j t)")
+        def down_pass(out, b, t, lo, hi, opens, closes):
+            nc.tensor.matmul_mx(
+                out=out,
+                lhsT=down["words"][:, b, 2 * P * t : 2 * P * (t + 1)].bitcast(E2M1X4),
+                lhsT_scale=down_scale[:, N * b + P * t : N * b + P * (t + 1)],
+                rhs=h_codes[b][:, lo:hi].bitcast(E4M3X4),
+                rhs_scale=h_scales[b][:, lo:hi],
+                start=opens,
+                stop=closes,
             )
-            for n, unit in enumerate(units):
-                h_codes[unit] = codes[:, TILE * n : TILE * (n + 1)]
-                h_scales[unit] = scales[:, TILE * n : TILE * (n + 1)]
 
         y_scales = keep.tile([P, J], U8, name="y_scales", align_bytes=64)
         y_rows = out_0.rearrange("(p t) j -> p t j", t=PACK)
         code_rows = out_1[0].rearrange("p j i -> p (j i)").bitcast(I32)
+        y_wide = keep.tile([P, PACK, HALF], F32, name="picked00", align_bytes=64)
+        rounded = {}
+        y_codes = keep.tile([P, J], I32, name="y_codes", align_bytes=64)
+        y_of = {}
         staged = {}
-        y_tags = ("picked00", "picked01", "picked10", "picked11", "y4")
 
-        def output(s):
-            g = max(n for n in range(len(STORES)) if STORES[n][0] <= TILE * s)
-            lo, hi = STORES[g]
-            if lo == TILE * s:
-                staged[g] = (
-                    keep.tile([P, PACK, hi - lo], F32, name=y_tags[g], align_bytes=64),
-                    keep.tile([P, hi - lo], I32, name="y_codes%d" % g, align_bytes=64),
-                    ring.tile([P, hi - lo, PACK], BF16, name="rounded", align_bytes=64),
-                )
-            y, y_codes, pair = staged[g]
-            cols = slice(TILE * s - lo, TILE * (s + 1) - lo)
-            bank = psum.tile([P, PACK, TILE], F32, name="down", bufs=2)
+        def down_wide(t):
+            bank = new_bank(1, HALF)
+            for b in range(PASSES):
+                down_pass(bank[:, 0, :], b, t, 0, HALF, b == 0, b == 1)
+            nc.scalar.copy(y_wide[:, t, :], bank[:, 0, :])
+            nc.sync.dma_start(y_rows[:, t, 0:HALF], y_wide[:, t, :])
+
+        def down_tile(s):
+            lo, hi = TILE * s, TILE * (s + 1)
+            bank = new_bank(PACK, TILE)
             for b in range(PASSES):
                 for t in range(PACK):
-                    nc.tensor.matmul_mx(
-                        out=bank[:, t, :],
-                        lhsT=down["words"][:, b, 2 * P * t : 2 * P * (t + 1)].bitcast(E2M1X4),
-                        lhsT_scale=down_scale[:, N * b + P * t : N * b + P * (t + 1)],
-                        rhs=h_codes[s, b].bitcast(E4M3X4),
-                        rhs_scale=h_scales[s, b],
-                        start=(b == 0 and t == 0),
-                        stop=(b == PASSES - 1 and t == PACK - 1),
-                    )
-            rounded = pair[:, cols, :]
-            if s in ROUND_ON_VECTOR:
-                nc.scalar.copy(y[:, :, cols], bank[:])
-                nc.vector.tensor_copy(
-                    rounded.rearrange("p (c e) t -> p c t e", e=4),
-                    y[:, :, cols].rearrange("p t (c e) -> p c t e", e=4),
-                )
-            else:
-                nc.scalar.copy(rounded, bank[:].rearrange("p t j -> p j t"))
-                nc.scalar.copy(y[:, :, cols], bank[:])
-            if hi == TILE * (s + 1):
-                nc.vector.quantize_mx(
-                    out=y_codes[:].bitcast(E4M3X4),
-                    scales=y_scales[:, lo:hi],
-                    in_=pair[:].rearrange("p j t -> p (j t)"),
-                )
-                nc.sync.dma_start(code_rows[:, lo:hi], y_codes[:])
-                (nc.scalar if hi == J else nc.sync).dma_start(y_rows[:, :, lo:hi], y[:])
+                    down_pass(bank[:, t, :], b, t, lo, hi, b == 0 and t == 0, b == 1 and t == PACK - 1)
+            lo_s, hi_s = max(span for span in STORES if span[0] <= lo)
+            if lo == lo_s:
+                staged[lo_s] = keep.tile([P, PACK, hi_s - lo_s], F32, name="y%d" % s, align_bytes=64)
+            y_of[s] = staged[lo_s][:, :, lo - lo_s : hi - lo_s]
+            nc.scalar.copy(y_of[s], bank[:])
+            if hi == hi_s:
+                (nc.scalar if hi == J else nc.sync).dma_start(y_rows[:, :, lo_s:hi_s], staged[lo_s][:])
 
-        def late_tiles(c, tag):
-            lo, hi = LATE[c]
-            pick_pair(1, 1, lo, hi, tag)
+        def open_rounded(lo, hi, tag):
+            tile = keep.tile([P, hi - lo, PACK], BF16, name=tag, align_bytes=64)
+            for c in range(lo, hi, TILE):
+                rounded[c] = (tile, lo)
 
-        def quantise_late(c):
-            quantise_x(1, LATE[c][0], LATE[c][1], "x_codes1_late%d" % c)
+        def round_y(copy, y, lo, hi):
+            tile, base = rounded[lo]
+            copy(as_runs(tile[:, lo - base : hi - base, :]), by_runs(y))
 
-        def group(units, held=()):
-            h = open_h(units)
-            for unit in units:
-                hidden(unit[0], unit[1], unit in held)
-            quantise_h(units, h)
+        def quantise_y(lo, hi):
+            nc.vector.quantize_mx(
+                out=y_codes[:, lo:hi].bitcast(E4M3X4),
+                scales=y_scales[:, lo:hi],
+                in_=rounded[lo][0][:].rearrange("p j t -> p (j t)"),
+            )
 
-        units = [(s, 0) for s in range(4)]
-        h = open_h(units)
-        hidden(0, 0)
-        quantise_early(3)
+        def store_codes(lo, hi):
+            nc.sync.dma_start(code_rows[:, lo:hi], y_codes[:, lo:hi])
+
+        finish_early(0)
+        finish_early(1)
+        deal_up(0, 0, (1,))
+        deal_up(1, 0, (1,))
+        lead_unit(0)
+        finish_early(2)
+        lead_unit(1)
+        finish_early(3)
+        lead_unit(2)
         deal_up(0, 1, (0, 1))
-        hidden(1, 0)
+        lead_unit(3)
         deal_up(1, 1, (0, 1))
-        hidden(2, 0, True)
-        hidden(3, 0, True)
-        pair_units = [(0, 1), (1, 1)]
-        h2 = open_h(pair_units)
-        hidden(0, 1, True)
-        late_tiles(0, "act20")
-        hidden(1, 1, True)
-        quantise_x(0, 512, 768, "act30")
-        quantise_late(0)
-        quantise_h(units, h)
+        pick_pair(0, 512, "raw010")
+        pick_pair(1, 512, "raw110")
+        gate_pair(0, 1)
+        up_tile(0, 1)
+        up_tile(1, 1)
+        product(lead[1][0], acts[0][:], 0, 0)
+        product(lead[1][1], acts[1][:], 1, 0)
+        quantise_x(0, 512, 1024, "lead_act0")
+        quantise_x(1, 512, 768, "x_codes1_4")
+        gate_pair(1, 1)
+        up_tile(2, 1)
+        up_tile(3, 1)
+        product(lead[1][2], acts[2][:], 2, 0)
+        pick_pair(0, 768, "lead_act2")
+        product(lead[1][3], acts[3][:], 3, 0)
+        multiply(0, 1)
+        pick_pair(1, 768, "lead_act3")
+        gate_pair(2, 0)
+        up_tile(4, 0)
+        up_tile(5, 0)
+        multiply(1, 1)
+        quantise_x(1, 768, 1024, "x_codes1_6")
+        gate_pair(2, 1)
+        up_tile(4, 1)
+        up_tile(5, 1)
+        multiply(2, 1)
+        multiply(3, 1)
+        quantise_h(0, 0, 512)
         deal_down_words("act01")
-        quantise_h(pair_units, h2)
-        pair_units = [(2, 1), (3, 1)]
-        h3 = open_h(pair_units)
-        hidden(2, 1, True)
-        late_tiles(1, "act11")
-        hidden(3, 1, True)
-        quantise_late(1)
-        quantise_h(pair_units, h3)
-        output(0)
-        h4 = open_h([(4, 0), (4, 1)])
-        hidden(4, 0, True)
-        output(1)
-        pick_pair(1, 0, 768, 1024, "act21")
-        hidden(4, 1, True)
-        quantise_h([(4, 0), (4, 1)], h4)
-        output(2)
-        late_tiles(2, "act31")
-        h5 = open_h([(5, 0), (5, 1)])
-        hidden(5, 0)
-        quantise_x(0, 768, 1024, "act40")
-        quantise_late(2)
-        output(3)
-        hidden(5, 1)
-        quantise_h([(5, 0), (5, 1)], h5)
-        output(4)
-        group([(6, 0), (6, 1)])
-        output(5)
-        group([(7, 0)])
-        group([(7, 1)])
-        output(6)
-        output(7)
+        quantise_h(1, 0, 512)
+        gate_pair(3, 0)
+        up_tile(6, 0)
+        up_tile(7, 0)
+        down_wide(0)
+        down_wide(1)
+        multiply(4, 0)
+        multiply(5, 0)
+        down_wide(2)
+        down_wide(3)
+        gate_pair(3, 1)
+        multiply(4, 1)
+        up_tile(6, 1)
+        multiply(5, 1)
+        up_tile(7, 1)
+        quantise_h(0, 512, 768)
+        multiply(6, 0)
+        quantise_h(1, 512, 768)
+        open_rounded(0, 256, "rounded0")
+        round_y(nc.scalar.copy, y_wide[:, :, 0:256], 0, 256)
+        multiply(7, 0)
+        multiply(6, 1)
+        quantise_h(0, 768, 1024)
+        multiply(7, 1)
+        quantise_h(1, 768, 896)
+        down_tile(4)
+        quantise_y(0, 256)
+        quantise_h(1, 896, 1024)
+        open_rounded(256, 512, "act31")
+        round_y(nc.vector.tensor_copy, y_wide[:, :, 256:512], 256, 512)
+        down_tile(5)
+        down_tile(6)
+        down_tile(7)
+        open_rounded(512, 768, "rounded2")
+        round_y(nc.vector.tensor_copy, y_of[4], 512, 640)
+        quantise_y(256, 512)
+        store_codes(0, 512)
+        round_y(nc.vector.tensor_copy, y_of[5], 640, 768)
+        open_rounded(768, 1024, "rounded3")
+        round_y(nc.vector.tensor_copy, y_of[6], 768, 896)
+        quantise_y(512, 768)
+        round_y(nc.vector.tensor_copy, y_of[7], 896, 1024)
+        quantise_y(768, 1024)
+        store_codes(512, 1024)
         for q in range(4):
             nc.sync.dma_start(out_2[0, 4 * q : 4 * q + 4, :].bitcast(I32), y_scales[32 * q : 32 * q + 4, :].bitcast(I32))

@@ -178,7 +178,7 @@ def tile_list_silu_noneP_kernel(
         for q in range(4):
             nc.sync.dma_start(down_scale[32 * q : 32 * q + 4, :].bitcast(I32), up_scale[32 * q + 16 : 32 * q + 20, :].bitcast(I32))
         quantise_x(0, 0, HALF, "x_codes0_0")
-        pick_cut(1, 0, (0, HALF), (0, HALF))
+        pick_cut(1, 0, (0, 768), (0, HALF, 768))
         deal_up(0, 0, (0,))
         first = keep.tile([P, 2, HALF], F32, name="picked11", align_bytes=64)
         gather(first[:, 0, :], 1, 2, 0, HALF)
@@ -290,7 +290,7 @@ def tile_list_silu_noneP_kernel(
         code_rows = out_1[0].rearrange("p j i -> p (j i)").bitcast(I32)
         y_wide = keep.tile([P, PACK, HALF], F32, name="picked00", align_bytes=64)
         rounded = {}
-        y_codes = keep.tile([P, J], I32, name="y_codes", align_bytes=64)
+        y_codes = keep.tile([P, J], I32, name="spread", align_bytes=64)
         y_of = {}
         staged = {}
 
@@ -346,8 +346,7 @@ def tile_list_silu_noneP_kernel(
         deal_up(0, 1, (0, 1))
         lead_unit(3)
         deal_up(1, 1, (0, 1))
-        pick_pair(0, 512, "raw010")
-        pick_pair(1, 512, "raw110")
+        pick_pair(1, 512, "raw010")
         gate_pair(0, 1)
         up_tile(0, 1)
         up_tile(1, 1)

@@ -38,7 +38,6 @@ def tile_list_silu_noneP_kernel(
         psum = ctx.enter_context(tc.psum_pool(name="psum", bufs=1))
 
         offsets = keep.tile([P, J // 16], U16, name="offsets")
-        nc.sync.dma_start(offsets[:], offs)
 
         warm = keep.tile([P, 8], F32, name="warm")
         warm2 = keep.tile([P, 8], F32, name="warm2")
@@ -76,13 +75,13 @@ def tile_list_silu_noneP_kernel(
             tile = keep.tile([P, len(passes), SPAN], I32, name="raw%d%d%d" % (w, b, passes[0]), align_bytes=64)
             src = up_words[w].rearrange("a p r i -> p a (r i)").bitcast(I32)
             nc.sync.dma_start(tile[:], src[:, passes[0] : passes[-1] + 1, SPAN * b : SPAN * (b + 1)])
-            raw[w, b, passes] = tile
+            raw[w, b, passes] = tile[:]
 
         def deal_up(w, b, passes):
             tile = keep.tile([P, len(passes), SPAN], I32, name="dealt%d%d%d" % (w, b, passes[0]), align_bytes=64)
             nc.vector.tensor_copy(
                 tile[:].rearrange("p a (t m) -> p a m t", t=PACK),
-                raw[w, b, passes][:].rearrange("p a (m t) -> p a m t", t=PACK),
+                raw[w, b, passes].rearrange("p a (m t) -> p a m t", t=PACK),
             )
             for n, a in enumerate(passes):
                 dealt[w, b, a] = tile[:, n, :]
@@ -93,6 +92,7 @@ def tile_list_silu_noneP_kernel(
         nc.vector.memset(head_rows[64:P, :], 0.0)
         nc.sync.dma_start(head_rows[0:64, :], wgt[0:P:16, :].rearrange("g (c j) -> g c j", j=P))
         load_plane(0, 0)
+        nc.sync.dma_start(offsets[:], offs)
         turned = psum.tile([P, P], F32, name="bank", bufs=8)
         nc.tensor.transpose(turned[:], head_rows[:], ident[:])
         spread = keep.tile([P, TILES, 8, 16], F32, name="spread", align_bytes=64)
@@ -120,7 +120,8 @@ def tile_list_silu_noneP_kernel(
         wd_raw = keep.tile([P, PASSES, 2 * N], U8, name="wd_raw", align_bytes=64)
         nc.sync.dma_start(wd_raw[:].bitcast(I32), wd_words.bitcast(I32).rearrange("a p n -> p a n"))
 
-        woven = [keep.tile([P, J, PACK], BF16, name="woven%d" % a, align_bytes=64) for a in range(PASSES)]
+        woven = [keep.tile([P, HALF, PACK], BF16, name="woven%d" % a, align_bytes=64) for a in range(PASSES)]
+        late = keep.tile([P, 2, PASSES, PAIR, PACK], BF16, name="late", align_bytes=64)
         x_operands = {}
 
         def by_runs(slots_first):
@@ -133,7 +134,24 @@ def tile_list_silu_noneP_kernel(
             nc.vector.tensor_tensor(out, planes[a, i][:].indirect(offsets[:, lo // 16 : hi // 16]), weight[:, lo:hi], MULT)
 
         def weave(pair, a, u, lo, hi):
-            nc.scalar.copy(woven[a][:, lo:hi, 2 * u : 2 * u + 2], pair.rearrange("p e j -> p j e"))
+            if lo < HALF:
+                nc.scalar.copy(woven[a][:, lo:hi, 2 * u : 2 * u + 2], pair.rearrange("p e j -> p j e"))
+            else:
+                groups = slice((lo - HALF) // PAIR, (hi - HALF) // PAIR)
+                nc.scalar.copy(late[:, groups, a, :, 2 * u : 2 * u + 2], pair.rearrange("p e (g j) -> p g j e", j=PAIR))
+
+        def quantise_late(lo, tag):
+            codes = keep.tile([P, PASSES, PAIR], U32, name=tag, align_bytes=64)
+            scales = keep.tile([P, PASSES, PAIR], U8, name="x_scales%d" % lo, align_bytes=64)
+            nc.vector.quantize_mx(
+                out=codes[:].rearrange("p a j -> p (a j)").bitcast(E4M3X4),
+                scales=scales[:].rearrange("p a j -> p (a j)"),
+                in_=late[:, (lo - HALF) // PAIR, :, :, :].rearrange("p a j i -> p (a j i)"),
+            )
+            for a in range(PASSES):
+                for width in (TILE, PAIR):
+                    for c in range(0, PAIR, width):
+                        x_operands[a, lo + c, width] = (codes[:, a, c : c + width].bitcast(E4M3X4), scales[:, a, c : c + width])
 
         def quantise_x(a, lo, hi, tag):
             codes = keep.tile([P, hi - lo], U32, name=tag, align_bytes=64)
@@ -148,19 +166,13 @@ def tile_list_silu_noneP_kernel(
                     cols = slice(c - lo, c - lo + width)
                     x_operands[a, c, width] = (codes[:, cols].bitcast(E4M3X4), scales[:, cols])
 
-        def pick_cut(a, u, cuts0, cuts1):
+        def pick_cut(a, u, cuts0, cuts1, weaves):
             pair = keep.tile([P, 2, cuts0[-1]], F32, name="picked%d%d" % (a, u), align_bytes=64)
-            for lo, hi in zip(cuts0, cuts0[1:]):
-                gather(pair[:, 0, lo:hi], a, 2 * u, lo, hi)
-            for lo, hi in zip(cuts1, cuts1[1:]):
-                gather(pair[:, 1, lo:hi], a, 2 * u + 1, lo, hi)
+            for e, cuts in enumerate((cuts0, cuts1)):
+                for lo, hi in zip(cuts, cuts[1:]):
+                    gather(pair[:, e, lo:hi], a, 2 * u + e, lo, hi)
+            for lo, hi in zip(weaves, weaves[1:]):
                 weave(pair[:, :, lo:hi], a, u, lo, hi)
-
-        def pick_late(lo, tag):
-            four = keep.tile([P, PACK, PAIR], F32, name=tag, align_bytes=64)
-            for i in range(PACK):
-                gather(four[:, i, :], 1, i, lo, lo + PAIR)
-            nc.scalar.copy(as_runs(woven[1][:, lo : lo + PAIR, :]), by_runs(four[:]))
 
         def pick_pair(u, lo, tag):
             pair = keep.tile([P, 2, PAIR], F32, name=tag, align_bytes=64)
@@ -168,8 +180,8 @@ def tile_list_silu_noneP_kernel(
                 gather(pair[:, e, :], 1, 2 * u + e, lo, lo + PAIR)
             weave(pair[:], 1, u, lo, lo + PAIR)
 
-        pick_cut(0, 0, (0, 256, 640, J), (0, J))
-        pick_cut(0, 1, (0, J), (0, HALF, J))
+        pick_cut(0, 0, (0, 256, 640, J), (0, J), (0, HALF, J))
+        pick_cut(0, 1, (0, J), (0, HALF, J), (0, HALF, J))
         up_scale = keep.tile([P, R], U8, name="plane03", align_bytes=64)
         nc.vector.tensor_copy(
             up_scale[:].rearrange("p (b t m) -> p b t m", b=PASSES, t=PACK),
@@ -178,7 +190,7 @@ def tile_list_silu_noneP_kernel(
         for q in range(4):
             nc.sync.dma_start(down_scale[32 * q : 32 * q + 4, :].bitcast(I32), up_scale[32 * q + 16 : 32 * q + 20, :].bitcast(I32))
         quantise_x(0, 0, HALF, "x_codes0_0")
-        pick_cut(1, 0, (0, 768), (0, HALF, 768))
+        pick_cut(1, 0, (0, J), (0, HALF, J), (0, HALF, J))
         deal_up(0, 0, (0,))
         first = keep.tile([P, 2, HALF], F32, name="picked11", align_bytes=64)
         gather(first[:, 0, :], 1, 2, 0, HALF)
@@ -206,16 +218,25 @@ def tile_list_silu_noneP_kernel(
             for s in range(4):
                 up_pass(lead[w][s], w, 0, 0, TILE * s, TILE, all_slots, True, False)
 
-        h = [keep.tile([P, J, PACK], BF16, name="h%d" % b, align_bytes=64) for b in range(PASSES)]
-        h_codes = [keep.tile([P, J], U32, name="h_codes%d" % b, align_bytes=64) for b in range(PASSES)]
-        h_scales = [keep.tile([P, J], U8, name="h_scales%d" % b, align_bytes=64) for b in range(PASSES)]
+        h_groups = ((0, HALF), (HALF, 768), (768, J))
+        h = {}
+        h_codes = {}
+        h_scales = {}
+        for lo, hi in h_groups:
+            h[lo] = keep.tile([P, PASSES, hi - lo, PACK], BF16, name="h%d" % lo if lo else "raw010", align_bytes=64)
+            h_codes[lo] = keep.tile([P, PASSES, hi - lo], U32, name="h_codes%d" % lo, align_bytes=64)
+            h_scales[lo] = keep.tile([P, PASSES, hi - lo], U8, name="h_scales%d" % lo, align_bytes=64)
+
+        def h_part(tiles, b, lo, hi):
+            base = max(g for g in tiles if g <= lo)
+            return tiles[base][:, b, lo - base : hi - base]
+
         acts = {}
 
         def product(bank, act, s, b):
-            nc.vector.tensor_tensor(as_runs(h[b][:, TILE * s : TILE * (s + 1), :]), by_runs(bank[:]), by_runs(act), MULT)
+            nc.vector.tensor_tensor(as_runs(h_part(h, b, TILE * s, TILE * (s + 1))), by_runs(bank[:]), by_runs(act), MULT)
 
-        def finish_early(s):
-            lo, hi = TILE * s, TILE * (s + 1)
+        def finish_early(lo, hi):
             gather(first[:, 1, lo:hi], 1, 3, lo, hi)
             weave(first[:, :, lo:hi], 1, 1, lo, hi)
 
@@ -225,14 +246,16 @@ def tile_list_silu_noneP_kernel(
             for c in range(0, HALF, width):
                 x_operands[1, c, width] = (lead_codes[:, c : c + width].bitcast(E4M3X4), lead_scales[:, c : c + width])
 
-        def lead_unit(s):
-            lo = TILE * s
-            cols = slice(lo, lo + TILE)
+        def quantise_lead(lo, hi):
+            cols = slice(lo, hi)
             nc.vector.quantize_mx(
                 out=lead_codes[:, cols].bitcast(E4M3X4),
                 scales=lead_scales[:, cols],
                 in_=woven[1][:, cols, :].rearrange("p j i -> p (j i)"),
             )
+
+        def lead_unit(s):
+            lo = TILE * s
             for w in range(2):
                 up_pass(lead[w][s], w, 0, 1, lo, TILE, all_slots, False, True)
             acts[s] = keep.tile([P, PACK, TILE], F32, name="lead_act%d" % s, align_bytes=64)
@@ -260,9 +283,16 @@ def tile_list_silu_noneP_kernel(
 
         def quantise_h(b, lo, hi):
             nc.vector.quantize_mx(
-                out=h_codes[b][:, lo:hi].bitcast(E4M3X4),
-                scales=h_scales[b][:, lo:hi],
-                in_=h[b][:, lo:hi, :].rearrange("p j t -> p (j t)"),
+                out=h_part(h_codes, b, lo, hi).bitcast(E4M3X4),
+                scales=h_part(h_scales, b, lo, hi),
+                in_=h_part(h, b, lo, hi).rearrange("p j t -> p (j t)"),
+            )
+
+        def quantise_h_group(lo):
+            nc.vector.quantize_mx(
+                out=h_codes[lo][:].rearrange("p b j -> p (b j)").bitcast(E4M3X4),
+                scales=h_scales[lo][:].rearrange("p b j -> p (b j)"),
+                in_=h[lo][:].rearrange("p b j t -> p (b j t)"),
             )
 
         down = {}
@@ -279,8 +309,8 @@ def tile_list_silu_noneP_kernel(
                 out=out,
                 lhsT=down["words"][:, b, 2 * P * t : 2 * P * (t + 1)].bitcast(E2M1X4),
                 lhsT_scale=down_scale[:, N * b + P * t : N * b + P * (t + 1)],
-                rhs=h_codes[b][:, lo:hi].bitcast(E4M3X4),
-                rhs_scale=h_scales[b][:, lo:hi],
+                rhs=h_part(h_codes, b, lo, hi).bitcast(E4M3X4),
+                rhs_scale=h_part(h_scales, b, lo, hi),
                 start=opens,
                 stop=closes,
             )
@@ -293,6 +323,7 @@ def tile_list_silu_noneP_kernel(
         y_codes = keep.tile([P, J], I32, name="spread", align_bytes=64)
         y_of = {}
         staged = {}
+        y_bank = {}
 
         def down_wide(t):
             bank = new_bank(1, HALF)
@@ -310,6 +341,7 @@ def tile_list_silu_noneP_kernel(
             lo_s, hi_s = max(span for span in STORES if span[0] <= lo)
             if lo == lo_s:
                 staged[lo_s] = keep.tile([P, PACK, hi_s - lo_s], F32, name="y%d" % s, align_bytes=64)
+            y_bank[s] = bank
             y_of[s] = staged[lo_s][:, :, lo - lo_s : hi - lo_s]
             nc.scalar.copy(y_of[s], bank[:])
             if hi == hi_s:
@@ -319,6 +351,18 @@ def tile_list_silu_noneP_kernel(
             tile = keep.tile([P, hi - lo, PACK], BF16, name=tag, align_bytes=64)
             for c in range(lo, hi, TILE):
                 rounded[c] = (tile, lo)
+
+        def down_last(s):
+            lo, hi = TILE * s, TILE * (s + 1)
+            banks = [new_bank(2, TILE) for u in range(2)]
+            for b in range(PASSES):
+                for t in range(PACK):
+                    down_pass(banks[t // 2][:, t % 2, :], b, t, lo, hi, b == 0 and t % 2 == 0, b == 1 and t % 2 == 1)
+            y = keep.tile([P, PACK, TILE], F32, name="y%d" % s, align_bytes=64)
+            y_of[s] = y[:]
+            nc.scalar.copy(y[:, 0:2, :], banks[0][:])
+            nc.vector.tensor_copy(y[:, 2:4, :], banks[1][:])
+            nc.scalar.dma_start(y_rows[:, :, lo:hi], y[:])
 
         def round_y(copy, y, lo, hi):
             tile, base = rounded[lo]
@@ -334,89 +378,87 @@ def tile_list_silu_noneP_kernel(
         def store_codes(lo, hi):
             nc.sync.dma_start(code_rows[:, lo:hi], y_codes[:, lo:hi])
 
-        finish_early(0)
-        finish_early(1)
+        finish_early(0, 128)
+        finish_early(128, 256)
         deal_up(0, 0, (1,))
         deal_up(1, 0, (1,))
+        quantise_lead(0, 128)
         lead_unit(0)
-        finish_early(2)
+        finish_early(256, 512)
+        quantise_lead(128, 256)
         lead_unit(1)
-        finish_early(3)
+        quantise_lead(256, 512)
         lead_unit(2)
         deal_up(0, 1, (0, 1))
         lead_unit(3)
         deal_up(1, 1, (0, 1))
-        pick_pair(1, 512, "raw010")
         gate_pair(0, 1)
         up_tile(0, 1)
         up_tile(1, 1)
         product(lead[1][0], acts[0][:], 0, 0)
+        pick_pair(1, 512, "lead_act0")
         product(lead[1][1], acts[1][:], 1, 0)
-        quantise_x(0, 512, 1024, "lead_act0")
-        quantise_x(1, 512, 768, "x_codes1_4")
+        quantise_late(512, "x_codes512")
         gate_pair(1, 1)
         up_tile(2, 1)
         up_tile(3, 1)
         product(lead[1][2], acts[2][:], 2, 0)
-        pick_pair(0, 768, "lead_act2")
         product(lead[1][3], acts[3][:], 3, 0)
+        pick_pair(1, 768, "lead_act2")
         multiply(0, 1)
-        pick_pair(1, 768, "lead_act3")
         gate_pair(2, 0)
         up_tile(4, 0)
         up_tile(5, 0)
         multiply(1, 1)
-        quantise_x(1, 768, 1024, "x_codes1_6")
+        quantise_h(0, 0, 512)
+        multiply(2, 1)
+        quantise_late(768, "x_codes768")
+        multiply(3, 1)
+        deal_down_words("act01")
+        quantise_h(1, 0, 512)
         gate_pair(2, 1)
         up_tile(4, 1)
         up_tile(5, 1)
-        multiply(2, 1)
-        multiply(3, 1)
-        quantise_h(0, 0, 512)
-        deal_down_words("act01")
-        quantise_h(1, 0, 512)
         gate_pair(3, 0)
-        up_tile(6, 0)
-        up_tile(7, 0)
         down_wide(0)
         down_wide(1)
-        multiply(4, 0)
-        multiply(5, 0)
         down_wide(2)
         down_wide(3)
-        gate_pair(3, 1)
+        multiply(4, 0)
+        multiply(5, 0)
         multiply(4, 1)
-        up_tile(6, 1)
         multiply(5, 1)
-        up_tile(7, 1)
-        quantise_h(0, 512, 768)
+        up_tile(6, 0)
+        up_tile(7, 0)
+        open_rounded(0, 512, "woven0")
+        round_y(nc.vector.tensor_copy, y_wide[:, :, 0:256], 0, 256)
+        quantise_h_group(512)
+        round_y(nc.scalar.copy, y_wide[:, :, 256:512], 256, 512)
         multiply(6, 0)
-        quantise_h(1, 512, 768)
-        open_rounded(0, 256, "rounded0")
-        round_y(nc.scalar.copy, y_wide[:, :, 0:256], 0, 256)
         multiply(7, 0)
-        multiply(6, 1)
-        quantise_h(0, 768, 1024)
-        multiply(7, 1)
-        quantise_h(1, 768, 896)
-        down_tile(4)
-        quantise_y(0, 256)
-        quantise_h(1, 896, 1024)
-        open_rounded(256, 512, "act31")
-        round_y(nc.vector.tensor_copy, y_wide[:, :, 256:512], 256, 512)
-        down_tile(5)
-        down_tile(6)
-        down_tile(7)
-        open_rounded(512, 768, "rounded2")
-        round_y(nc.vector.tensor_copy, y_of[4], 512, 640)
-        quantise_y(256, 512)
+        gate_pair(3, 1)
+        quantise_y(0, 512)
         store_codes(0, 512)
-        round_y(nc.vector.tensor_copy, y_of[5], 640, 768)
+        quantise_h(0, 768, 1024)
+        up_tile(6, 1)
+        multiply(6, 1)
+        down_tile(4)
+        open_rounded(512, 768, "rounded2")
+        round_y(nc.scalar.copy, y_bank[4][:], 512, 640)
+        down_tile(5)
+        round_y(nc.scalar.copy, y_bank[5][:], 640, 768)
+        up_tile(7, 1)
+        quantise_h(1, 768, 896)
+        multiply(7, 1)
+        down_tile(6)
+        quantise_h(1, 896, 1024)
+        quantise_y(512, 768)
+        store_codes(512, 768)
         open_rounded(768, 1024, "rounded3")
         round_y(nc.vector.tensor_copy, y_of[6], 768, 896)
-        quantise_y(512, 768)
+        down_last(7)
         round_y(nc.vector.tensor_copy, y_of[7], 896, 1024)
         quantise_y(768, 1024)
-        store_codes(512, 1024)
+        store_codes(768, 1024)
         for q in range(4):
-            nc.sync.dma_start(out_2[0, 4 * q : 4 * q + 4, :].bitcast(I32), y_scales[32 * q : 32 * q + 4, :].bitcast(I32))
+            (nc.sync if q < 2 else nc.scalar).dma_start(out_2[0, 4 * q : 4 * q + 4, :].bitcast(I32), y_scales[32 * q : 32 * q + 4, :].bitcast(I32))

@@ -54,11 +54,6 @@ def tile_list_silu_noneP_kernel(
                     up_raw[32 * q + 8 * w : 32 * q + 8 * w + 8, :].bitcast(I32),
                     scales[:, 4 * q : 4 * q + 4, :].bitcast(I32),
                 )
-        for q in range(4):
-            nc.scalar.dma_start(
-                up_raw[32 * q + 16 : 32 * q + 20, :].bitcast(I32).rearrange("r (a n) -> r a n", a=PASSES),
-                wd_scales[:, 4 * q : 4 * q + 4, :].bitcast(I32).rearrange("a r n -> r a n"),
-            )
 
         weight = keep.tile([P, J], F32, name="weight")
         planes = {}
@@ -93,6 +88,11 @@ def tile_list_silu_noneP_kernel(
         nc.sync.dma_start(head_rows[0:64, :], wgt[0:P:16, :].rearrange("g (c j) -> g c j", j=P))
         load_plane(0, 0)
         nc.sync.dma_start(offsets[:], offs)
+        for q in range(4):
+            nc.sync.dma_start(
+                up_raw[32 * q + 16 : 32 * q + 20, :].bitcast(I32).rearrange("r (a n) -> r a n", a=PASSES),
+                wd_scales[:, 4 * q : 4 * q + 4, :].bitcast(I32).rearrange("a r n -> r a n"),
+            )
         turned = psum.tile([P, P], F32, name="bank", bufs=8)
         nc.tensor.transpose(turned[:], head_rows[:], ident[:])
         spread = keep.tile([P, TILES, 8, 16], F32, name="spread", align_bytes=64)

@@ -182,16 +182,16 @@ def tile_list_silu_noneP_kernel(
 
         pick_cut(0, 0, (0, 256, 640, J), (0, J), (0, HALF, J))
         pick_cut(0, 1, (0, J), (0, HALF, J), (0, HALF, J))
-        up_scale = keep.tile([P, R], U8, name="plane03", align_bytes=64)
+        pick_cut(1, 0, (0, J), (0, HALF, J), (0, HALF, J))
+        deal_up(0, 0, (0,))
+        quantise_x(0, 0, HALF, "plane10")
+        up_scale = keep.tile([P, R], U8, name="raw000", align_bytes=64)
         nc.vector.tensor_copy(
             up_scale[:].rearrange("p (b t m) -> p b t m", b=PASSES, t=PACK),
             up_raw[:].rearrange("p (b m t) -> p b t m", b=PASSES, t=PACK),
         )
         for q in range(4):
             nc.sync.dma_start(down_scale[32 * q : 32 * q + 4, :].bitcast(I32), up_scale[32 * q + 16 : 32 * q + 20, :].bitcast(I32))
-        quantise_x(0, 0, HALF, "x_codes0_0")
-        pick_cut(1, 0, (0, J), (0, HALF, J), (0, HALF, J))
-        deal_up(0, 0, (0,))
         first = keep.tile([P, 2, HALF], F32, name="picked11", align_bytes=64)
         gather(first[:, 0, :], 1, 2, 0, HALF)
         deal_up(1, 0, (0,))
@@ -345,7 +345,7 @@ def tile_list_silu_noneP_kernel(
             y_of[s] = staged[lo_s][:, :, lo - lo_s : hi - lo_s]
             nc.scalar.copy(y_of[s], bank[:])
             if hi == hi_s:
-                (nc.scalar if hi == J else nc.sync).dma_start(y_rows[:, :, lo_s:hi_s], staged[lo_s][:])
+                nc.sync.dma_start(y_rows[:, :, lo_s:hi_s], staged[lo_s][:])
 
         def open_rounded(lo, hi, tag):
             tile = keep.tile([P, hi - lo, PACK], BF16, name=tag, align_bytes=64)
@@ -362,7 +362,7 @@ def tile_list_silu_noneP_kernel(
             y_of[s] = y[:]
             nc.scalar.copy(y[:, 0:2, :], banks[0][:])
             nc.vector.tensor_copy(y[:, 2:4, :], banks[1][:])
-            nc.scalar.dma_start(y_rows[:, :, lo:hi], y[:])
+            nc.sync.dma_start(y_rows[:, :, lo:hi], y[:])
 
         def round_y(copy, y, lo, hi):
             tile, base = rounded[lo]
@@ -384,12 +384,14 @@ def tile_list_silu_noneP_kernel(
         deal_up(1, 0, (1,))
         quantise_lead(0, 128)
         lead_unit(0)
-        finish_early(256, 512)
+        finish_early(256, 384)
         quantise_lead(128, 256)
         lead_unit(1)
-        quantise_lead(256, 512)
+        finish_early(384, 512)
+        quantise_lead(256, 384)
         lead_unit(2)
         deal_up(0, 1, (0, 1))
+        quantise_lead(384, 512)
         lead_unit(3)
         deal_up(1, 1, (0, 1))
         gate_pair(0, 1)
@@ -461,4 +463,4 @@ def tile_list_silu_noneP_kernel(
         quantise_y(768, 1024)
         store_codes(768, 1024)
         for q in range(4):
-            (nc.sync if q < 2 else nc.scalar).dma_start(out_2[0, 4 * q : 4 * q + 4, :].bitcast(I32), y_scales[32 * q : 32 * q + 4, :].bitcast(I32))
+            nc.sync.dma_start(out_2[0, 4 * q : 4 * q + 4, :].bitcast(I32), y_scales[32 * q : 32 * q + 4, :].bitcast(I32))

@@ -26,7 +26,6 @@ TILES = J // TILE
 HALF = J // 2
 PAIR = 2 * TILE
 RUN = 4
-STORES = ((512, 640), (640, 768), (768, 896), (896, 1024))
 
 
 def tile_list_silu_noneP_kernel(
@@ -85,14 +84,14 @@ def tile_list_silu_noneP_kernel(
         make_identity(nc, ident[:])
         head_rows = keep.tile([P, P], F32, name="head_rows", align_bytes=64)
         nc.vector.memset(head_rows[64:P, :], 0.0)
-        nc.sync.dma_start(head_rows[0:64, :], wgt[0:P:16, :].rearrange("g (c j) -> g c j", j=P))
+        half_rows = wgt.rearrange("p (h j) -> (p h) j", h=2)
+        nc.sync.dma_start(head_rows[0:64, :], half_rows[0 : 2 * P : 17, :].rearrange("m (c j) -> m c j", j=P))
         load_plane(0, 0)
         nc.sync.dma_start(offsets[:], offs)
-        for q in range(4):
-            nc.sync.dma_start(
-                up_raw[32 * q + 16 : 32 * q + 20, :].bitcast(I32).rearrange("r (a n) -> r a n", a=PASSES),
-                wd_scales[:, 4 * q : 4 * q + 4, :].bitcast(I32).rearrange("a r n -> r a n"),
-            )
+        nc.sync.dma_start(
+            up_raw[16:32, :].bitcast(I32).rearrange("r (a n) -> r a n", a=PASSES),
+            wd_scales.bitcast(I32).rearrange("a r n -> r a n"),
+        )
         turned = psum.tile([P, P], F32, name="bank", bufs=8)
         nc.tensor.transpose(turned[:], head_rows[:], ident[:])
         spread = keep.tile([P, TILES, 8, 16], F32, name="spread", align_bytes=64)
@@ -120,6 +119,7 @@ def tile_list_silu_noneP_kernel(
         wd_raw = keep.tile([P, PASSES, 2 * N], U8, name="wd_raw", align_bytes=64)
         nc.sync.dma_start(wd_raw[:].bitcast(I32), wd_words.bitcast(I32).rearrange("a p n -> p a n"))
 
+        picked = [keep.tile([P, PACK, J], F32, name="picked%d" % a, align_bytes=64) for a in range(PASSES)]
         woven = [keep.tile([P, HALF, PACK], BF16, name="woven%d" % a, align_bytes=64) for a in range(PASSES)]
         late = keep.tile([P, 2, PASSES, PAIR, PACK], BF16, name="late", align_bytes=64)
         x_operands = {}
@@ -130,70 +130,70 @@ def tile_list_silu_noneP_kernel(
         def as_runs(columns_first):
             return columns_first.rearrange("p (c e) t -> p c t e", e=RUN)
 
-        def gather(out, a, i, lo, hi):
-            nc.vector.tensor_tensor(out, planes[a, i][:].indirect(offsets[:, lo // 16 : hi // 16]), weight[:, lo:hi], MULT)
+        def gather(a, i, lo, hi):
+            nc.vector.tensor_tensor(picked[a][:, i, lo:hi], planes[a, i][:].indirect(offsets[:, lo // 16 : hi // 16]), weight[:, lo:hi], MULT)
 
-        def weave(pair, a, u, lo, hi):
-            if lo < HALF:
-                nc.scalar.copy(woven[a][:, lo:hi, 2 * u : 2 * u + 2], pair.rearrange("p e j -> p j e"))
-            else:
-                groups = slice((lo - HALF) // PAIR, (hi - HALF) // PAIR)
-                nc.scalar.copy(late[:, groups, a, :, 2 * u : 2 * u + 2], pair.rearrange("p e (g j) -> p g j e", j=PAIR))
+        def weave_two(u, lo, hi):
+            slots = slice(2 * u, 2 * u + 2)
+            nc.scalar.copy(woven[1][:, lo:hi, slots], picked[1][:, slots, lo:hi].rearrange("p e j -> p j e"))
 
-        def quantise_late(lo, tag):
+        def weave_late(a, g):
+            lo = HALF + PAIR * g
+            nc.scalar.copy(as_runs(late[:, g, a, :, :]), by_runs(picked[a][:, :, lo : lo + PAIR]))
+
+        def quantise_late(g, tag):
+            lo = HALF + PAIR * g
             codes = keep.tile([P, PASSES, PAIR], U32, name=tag, align_bytes=64)
             scales = keep.tile([P, PASSES, PAIR], U8, name="x_scales%d" % lo, align_bytes=64)
             nc.vector.quantize_mx(
                 out=codes[:].rearrange("p a j -> p (a j)").bitcast(E4M3X4),
                 scales=scales[:].rearrange("p a j -> p (a j)"),
-                in_=late[:, (lo - HALF) // PAIR, :, :, :].rearrange("p a j i -> p (a j i)"),
+                in_=late[:, g, :, :, :].rearrange("p a j i -> p (a j i)"),
             )
             for a in range(PASSES):
                 for width in (TILE, PAIR):
                     for c in range(0, PAIR, width):
                         x_operands[a, lo + c, width] = (codes[:, a, c : c + width].bitcast(E4M3X4), scales[:, a, c : c + width])
 
-        def quantise_x(a, lo, hi, tag):
-            codes = keep.tile([P, hi - lo], U32, name=tag, align_bytes=64)
-            scales = keep.tile([P, hi - lo], U8, name="x_scales%d_%d" % (a, lo), align_bytes=64)
+        lead_codes = {}
+        lead_scales = {}
+
+        def open_lead(a, tag):
+            lead_codes[a] = keep.tile([P, HALF], U32, name=tag, align_bytes=64)
+            lead_scales[a] = keep.tile([P, HALF], U8, name="lead_scales%d" % a, align_bytes=64)
+            for width in (TILE, PAIR):
+                for c in range(0, HALF, width):
+                    x_operands[a, c, width] = (lead_codes[a][:, c : c + width].bitcast(E4M3X4), lead_scales[a][:, c : c + width])
+
+        def quantise_lead(a, lo, hi):
             nc.vector.quantize_mx(
-                out=codes[:].bitcast(E4M3X4),
-                scales=scales[:],
+                out=lead_codes[a][:, lo:hi].bitcast(E4M3X4),
+                scales=lead_scales[a][:, lo:hi],
                 in_=woven[a][:, lo:hi, :].rearrange("p j i -> p (j i)"),
             )
-            for width in (TILE, PAIR):
-                for c in range(lo, hi - width + 1, width):
-                    cols = slice(c - lo, c - lo + width)
-                    x_operands[a, c, width] = (codes[:, cols].bitcast(E4M3X4), scales[:, cols])
 
-        def pick_cut(a, u, cuts0, cuts1, weaves):
-            pair = keep.tile([P, 2, cuts0[-1]], F32, name="picked%d%d" % (a, u), align_bytes=64)
-            for e, cuts in enumerate((cuts0, cuts1)):
-                for lo, hi in zip(cuts, cuts[1:]):
-                    gather(pair[:, e, lo:hi], a, 2 * u + e, lo, hi)
-            for lo, hi in zip(weaves, weaves[1:]):
-                weave(pair[:, :, lo:hi], a, u, lo, hi)
-
-        def pick_pair(u, lo, tag):
-            pair = keep.tile([P, 2, PAIR], F32, name=tag, align_bytes=64)
-            for e in range(2):
-                gather(pair[:, e, :], 1, 2 * u + e, lo, lo + PAIR)
-            weave(pair[:], 1, u, lo, lo + PAIR)
-
-        pick_cut(0, 0, (0, 256, 640, J), (0, J), (0, HALF, J))
-        pick_cut(0, 1, (0, J), (0, HALF, J), (0, HALF, J))
-        pick_cut(1, 0, (0, J), (0, HALF, J), (0, HALF, J))
+        for lo, hi in ((0, 256), (256, 640), (640, J)):
+            gather(0, 0, lo, hi)
+        for i in range(1, PACK):
+            gather(0, i, 0, J)
+        nc.scalar.copy(as_runs(woven[0][:]), by_runs(picked[0][:, :, 0:HALF]))
+        weave_late(0, 0)
+        weave_late(0, 1)
+        gather(1, 0, 0, J)
         deal_up(0, 0, (0,))
-        quantise_x(0, 0, HALF, "plane10")
+        open_lead(0, "plane10")
+        quantise_lead(0, 0, HALF)
         up_scale = keep.tile([P, R], U8, name="raw000", align_bytes=64)
         nc.vector.tensor_copy(
             up_scale[:].rearrange("p (b t m) -> p b t m", b=PASSES, t=PACK),
             up_raw[:].rearrange("p (b m t) -> p b t m", b=PASSES, t=PACK),
         )
         for q in range(4):
-            nc.sync.dma_start(down_scale[32 * q : 32 * q + 4, :].bitcast(I32), up_scale[32 * q + 16 : 32 * q + 20, :].bitcast(I32))
-        first = keep.tile([P, 2, HALF], F32, name="picked11", align_bytes=64)
-        gather(first[:, 0, :], 1, 2, 0, HALF)
+            nc.sync.dma_start(down_scale[32 * q : 32 * q + 4, :].bitcast(I32), up_scale[16 + 4 * q : 20 + 4 * q, :].bitcast(I32))
+        gather(1, 1, 0, HALF)
+        weave_two(0, 0, HALF)
+        gather(1, 1, HALF, J)
+        gather(1, 2, 0, HALF)
         deal_up(1, 0, (0,))
 
         def new_bank(slots, width):
@@ -236,30 +236,27 @@ def tile_list_silu_noneP_kernel(
         def product(bank, act, s, b):
             nc.vector.tensor_tensor(as_runs(h_part(h, b, TILE * s, TILE * (s + 1))), by_runs(bank[:]), by_runs(act), MULT)
 
-        def finish_early(lo, hi):
-            gather(first[:, 1, lo:hi], 1, 3, lo, hi)
-            weave(first[:, :, lo:hi], 1, 1, lo, hi)
+        def finish_early(lo, at):
+            nc.vector.tensor_tensor(picked[1][:, 3, at : at + TILE], planes[1, 3][:].indirect(offsets[:, lo // 16 : (lo + TILE) // 16]), weight[:, lo : lo + TILE], MULT)
+            step = J + at - lo
+            both = picked[1][:].rearrange("p i j -> p (i j)")[:, 2 * J + lo - (step - TILE) : 3 * J + at + TILE]
+            both = both.rearrange("p (e x) -> p x e", e=2)[:, step - TILE : step, :]
+            nc.scalar.copy(woven[1][:, lo : lo + TILE, 2:4], both)
 
-        lead_codes = keep.tile([P, HALF], U32, name="lead_codes", align_bytes=64)
-        lead_scales = keep.tile([P, HALF], U8, name="lead_scales", align_bytes=64)
-        for width in (TILE, PAIR):
-            for c in range(0, HALF, width):
-                x_operands[1, c, width] = (lead_codes[:, c : c + width].bitcast(E4M3X4), lead_scales[:, c : c + width])
+        open_lead(1, "lead_codes")
 
-        def quantise_lead(lo, hi):
-            cols = slice(lo, hi)
-            nc.vector.quantize_mx(
-                out=lead_codes[:, cols].bitcast(E4M3X4),
-                scales=lead_scales[:, cols],
-                in_=woven[1][:, cols, :].rearrange("p j i -> p (j i)"),
-            )
-
-        def lead_unit(s):
+        def lead_unit(s, act):
             lo = TILE * s
             for w in range(2):
                 up_pass(lead[w][s], w, 0, 1, lo, TILE, all_slots, False, True)
-            acts[s] = keep.tile([P, PACK, TILE], F32, name="lead_act%d" % s, align_bytes=64)
-            nc.scalar.activation(acts[s][:], lead[0][s][:], SILU)
+            acts[s] = act
+            nc.scalar.activation(act, lead[0][s][:], SILU)
+
+        def own_act(s):
+            return keep.tile([P, PACK, TILE], F32, name="lead_act%d" % s, align_bytes=64)[:]
+
+        def parked_act(i):
+            return picked[1][:, i, HALF:J].rearrange("p (t j) -> p t j", t=PACK)
 
         def gate_pair(g, b):
             act = keep.tile([P, PACK, PAIR], F32, name="act%d%d" % (g, b), align_bytes=64)
@@ -318,11 +315,10 @@ def tile_list_silu_noneP_kernel(
         y_scales = keep.tile([P, J], U8, name="y_scales", align_bytes=64)
         y_rows = out_0.rearrange("(p t) j -> p t j", t=PACK)
         code_rows = out_1[0].rearrange("p j i -> p (j i)").bitcast(I32)
-        y_wide = keep.tile([P, PACK, HALF], F32, name="picked00", align_bytes=64)
+        y_wide = keep.tile([P, PACK, HALF], F32, name="picked0", align_bytes=64)
         rounded = {}
         y_codes = keep.tile([P, J], I32, name="spread", align_bytes=64)
         y_of = {}
-        staged = {}
         y_bank = {}
 
         def down_wide(t):
@@ -338,14 +334,11 @@ def tile_list_silu_noneP_kernel(
             for b in range(PASSES):
                 for t in range(PACK):
                     down_pass(bank[:, t, :], b, t, lo, hi, b == 0 and t == 0, b == 1 and t == PACK - 1)
-            lo_s, hi_s = max(span for span in STORES if span[0] <= lo)
-            if lo == lo_s:
-                staged[lo_s] = keep.tile([P, PACK, hi_s - lo_s], F32, name="y%d" % s, align_bytes=64)
+            y = keep.tile([P, PACK, TILE], F32, name="y%d" % s, align_bytes=64)
             y_bank[s] = bank
-            y_of[s] = staged[lo_s][:, :, lo - lo_s : hi - lo_s]
-            nc.scalar.copy(y_of[s], bank[:])
-            if hi == hi_s:
-                nc.sync.dma_start(y_rows[:, :, lo_s:hi_s], staged[lo_s][:])
+            y_of[s] = y[:]
+            nc.scalar.copy(y[:], bank[:])
+            nc.sync.dma_start(y_rows[:, :, lo:hi], y[:])
 
         def open_rounded(lo, hi, tag):
             tile = keep.tile([P, hi - lo, PACK], BF16, name=tag, align_bytes=64)
@@ -360,8 +353,8 @@ def tile_list_silu_noneP_kernel(
                     down_pass(banks[t // 2][:, t % 2, :], b, t, lo, hi, b == 0 and t % 2 == 0, b == 1 and t % 2 == 1)
             y = keep.tile([P, PACK, TILE], F32, name="y%d" % s, align_bytes=64)
             y_of[s] = y[:]
-            nc.scalar.copy(y[:, 0:2, :], banks[0][:])
-            nc.vector.tensor_copy(y[:, 2:4, :], banks[1][:])
+            for u, copy in enumerate((nc.scalar.copy, nc.vector.tensor_copy)):
+                copy(y[:, 2 * u : 2 * u + 2, :], banks[u][:])
             nc.sync.dma_start(y_rows[:, :, lo:hi], y[:])
 
         def round_y(copy, y, lo, hi):
@@ -369,53 +362,58 @@ def tile_list_silu_noneP_kernel(
             copy(as_runs(tile[:, lo - base : hi - base, :]), by_runs(y))
 
         def quantise_y(lo, hi):
+            tile, base = rounded[lo]
             nc.vector.quantize_mx(
                 out=y_codes[:, lo:hi].bitcast(E4M3X4),
                 scales=y_scales[:, lo:hi],
-                in_=rounded[lo][0][:].rearrange("p j t -> p (j t)"),
+                in_=tile[:, lo - base : hi - base, :].rearrange("p j t -> p (j t)"),
             )
 
         def store_codes(lo, hi):
             nc.sync.dma_start(code_rows[:, lo:hi], y_codes[:, lo:hi])
 
-        finish_early(0, 128)
-        finish_early(128, 256)
+        finish_early(0, 0)
+        finish_early(128, 128)
+        finish_early(256, 256)
         deal_up(0, 0, (1,))
+        quantise_lead(1, 0, 128)
         deal_up(1, 0, (1,))
-        quantise_lead(0, 128)
-        lead_unit(0)
-        finish_early(256, 384)
-        quantise_lead(128, 256)
-        lead_unit(1)
-        finish_early(384, 512)
-        quantise_lead(256, 384)
-        lead_unit(2)
+        finish_early(384, 0)
+        lead_unit(0, parked_act(2))
+        quantise_lead(1, 128, 256)
+        lead_unit(1, parked_act(3))
+        quantise_lead(1, 256, 384)
+        lead_unit(2, own_act(2))
         deal_up(0, 1, (0, 1))
-        quantise_lead(384, 512)
-        lead_unit(3)
+        quantise_lead(1, 384, 512)
+        lead_unit(3, own_act(3))
         deal_up(1, 1, (0, 1))
         gate_pair(0, 1)
         up_tile(0, 1)
         up_tile(1, 1)
-        product(lead[1][0], acts[0][:], 0, 0)
-        pick_pair(1, 512, "lead_act0")
-        product(lead[1][1], acts[1][:], 1, 0)
-        quantise_late(512, "x_codes512")
+        product(lead[1][0], acts[0], 0, 0)
+        product(lead[1][1], acts[1], 1, 0)
+        gather(1, 2, 512, 768)
+        gather(1, 3, 512, 768)
+        weave_late(1, 0)
         gate_pair(1, 1)
         up_tile(2, 1)
         up_tile(3, 1)
-        product(lead[1][2], acts[2][:], 2, 0)
-        product(lead[1][3], acts[3][:], 3, 0)
-        pick_pair(1, 768, "lead_act2")
+        product(lead[1][2], acts[2], 2, 0)
+        product(lead[1][3], acts[3], 3, 0)
+        quantise_late(0, "x_codes512")
         multiply(0, 1)
         gate_pair(2, 0)
         up_tile(4, 0)
         up_tile(5, 0)
         multiply(1, 1)
+        gather(1, 2, 768, J)
+        gather(1, 3, 768, J)
+        weave_late(1, 1)
         quantise_h(0, 0, 512)
         multiply(2, 1)
-        quantise_late(768, "x_codes768")
         multiply(3, 1)
+        quantise_late(1, "x_codes768")
         deal_down_words("act01")
         quantise_h(1, 0, 512)
         gate_pair(2, 1)
@@ -446,12 +444,12 @@ def tile_list_silu_noneP_kernel(
         multiply(6, 1)
         down_tile(4)
         open_rounded(512, 768, "rounded2")
-        round_y(nc.scalar.copy, y_bank[4][:], 512, 640)
         down_tile(5)
-        round_y(nc.scalar.copy, y_bank[5][:], 640, 768)
         up_tile(7, 1)
         quantise_h(1, 768, 896)
+        round_y(nc.vector.tensor_copy, y_of[4], 512, 640)
         multiply(7, 1)
+        round_y(nc.vector.tensor_copy, y_of[5], 640, 768)
         down_tile(6)
         quantise_h(1, 896, 1024)
         quantise_y(512, 768)

@@ -26,6 +26,7 @@ TILES = J // TILE
 HALF = J // 2
 PAIR = 2 * TILE
 RUN = 4
+GATE, UP = 0, 1
 
 
 def tile_list_silu_noneP_kernel(
@@ -36,92 +37,113 @@ def tile_list_silu_noneP_kernel(
         keep = ctx.enter_context(tc.tile_pool(name="keep", bufs=1))
         psum = ctx.enter_context(tc.psum_pool(name="psum", bufs=1))
 
+        def sbuf(shape, dtype, name):
+            return keep.tile([P] + shape, dtype, name=name, align_bytes=64)
+
+        def bank(n, slots, width):
+            return psum.tile([P, slots, width], F32, name="bank%d" % n)
+
         offsets = keep.tile([P, J // 16], U16, name="offsets")
+
+        scale_raw = sbuf([R], U8, "scale_raw")
+        down_scale = sbuf([PASSES * N], U8, "down_scale")
+        nc.vector.memset(scale_raw[:].bitcast(I32), 0)
+        head_rows = sbuf([P], F32, "head_rows")
+        nc.vector.memset(head_rows[64:P, :], 0.0)
+        nc.vector.memset(down_scale[:].bitcast(I32), 0)
 
         warm = keep.tile([P, 8], F32, name="warm")
         warm2 = keep.tile([P, 8], F32, name="warm2")
         nc.vector.memset(warm[:], 0.0)
         nc.scalar.activation(warm2[:], warm[:], SILU)
 
-        up_raw = keep.tile([P, R], U8, name="up_raw", align_bytes=64)
-        down_scale = keep.tile([P, PASSES * N], U8, name="down_scale", align_bytes=64)
-        nc.vector.memset(up_raw[:].bitcast(I32), 0)
-        nc.vector.memset(down_scale[:].bitcast(I32), 0)
-        for w, scales in enumerate((wg_scales, wu_scales)):
-            for q in range(4):
-                nc.gpsimd.dma_start(
-                    up_raw[32 * q + 8 * w : 32 * q + 8 * w + 8, :].bitcast(I32),
-                    scales[:, 4 * q : 4 * q + 4, :].bitcast(I32),
-                )
+        ident = sbuf([P], F32, "ident")
+        make_identity(nc, ident[:])
 
-        weight = keep.tile([P, J], F32, name="weight")
+        def load_scales(queue, w, q):
+            scales = (wg_scales, wu_scales)[w]
+            queue.dma_start(
+                scale_raw[32 * q + 8 * w : 32 * q + 8 * w + 8, :].bitcast(I32),
+                scales[:, 4 * q : 4 * q + 4, :].bitcast(I32),
+            )
+
         planes = {}
         raw = {}
         dealt = {}
-        up_words = (wg_words, wu_words)
 
         def load_plane(a, i):
-            planes[a, i] = keep.tile([P, T], F32, name="plane%d%d" % (a, i), align_bytes=64)
+            planes[a, i] = sbuf([T], F32, "plane%d%d" % (a, i))
             rows = xT[SPAN * a : SPAN * (a + 1), :].rearrange("(p i) t -> p i t", i=PACK)
             nc.sync.dma_start(planes[a, i][:], rows[:, i, :])
 
-        def load_up(w, b, passes):
-            tile = keep.tile([P, len(passes), SPAN], I32, name="raw%d%d%d" % (w, b, passes[0]), align_bytes=64)
-            src = up_words[w].rearrange("a p r i -> p a (r i)").bitcast(I32)
+        def load_words(w, b, passes):
+            tile = sbuf([len(passes), SPAN], I32, "raw%d%d%d" % (w, b, passes[0]))
+            src = (wg_words, wu_words)[w].rearrange("a p r i -> p a (r i)").bitcast(I32)
             nc.sync.dma_start(tile[:], src[:, passes[0] : passes[-1] + 1, SPAN * b : SPAN * (b + 1)])
-            raw[w, b, passes] = tile[:]
+            raw[w, b, passes] = tile
 
-        def deal_up(w, b, passes):
-            tile = keep.tile([P, len(passes), SPAN], I32, name="dealt%d%d%d" % (w, b, passes[0]), align_bytes=64)
-            nc.vector.tensor_copy(
-                tile[:].rearrange("p a (t m) -> p a m t", t=PACK),
-                raw[w, b, passes].rearrange("p a (m t) -> p a m t", t=PACK),
+        def deal_words(copy, dtype, w, b, passes):
+            tile = sbuf([len(passes), SPAN], I32, "dealt%d%d%d" % (w, b, passes[0]))
+            copy(
+                tile[:].bitcast(dtype).rearrange("p a (t m) -> p a m t", t=PACK),
+                raw[w, b, passes][:].bitcast(dtype).rearrange("p a (m t) -> p a m t", t=PACK),
             )
             for n, a in enumerate(passes):
                 dealt[w, b, a] = tile[:, n, :]
 
-        ident = keep.tile([P, P], F32, name="ident", align_bytes=64)
-        make_identity(nc, ident[:])
-        head_rows = keep.tile([P, P], F32, name="head_rows", align_bytes=64)
-        nc.vector.memset(head_rows[64:P, :], 0.0)
+        def deal_on_scalar(w, b, passes):
+            deal_words(nc.scalar.copy, U32, w, b, passes)
+
+        def deal_on_vector(w, b, passes):
+            deal_words(nc.vector.tensor_copy, I32, w, b, passes)
+
         half_rows = wgt.rearrange("p (h j) -> (p h) j", h=2)
         nc.sync.dma_start(head_rows[0:64, :], half_rows[0 : 2 * P : 17, :].rearrange("m (c j) -> m c j", j=P))
         load_plane(0, 0)
         nc.sync.dma_start(offsets[:], offs)
+        for q in range(4):
+            load_scales(nc.gpsimd, GATE, q)
+        load_plane(0, 1)
+        load_plane(0, 2)
         nc.sync.dma_start(
-            up_raw[16:32, :].bitcast(I32).rearrange("r (a n) -> r a n", a=PASSES),
+            scale_raw[16:32, :].bitcast(I32).rearrange("r (a n) -> r a n", a=PASSES),
             wd_scales.bitcast(I32).rearrange("a r n -> r a n"),
         )
-        turned = psum.tile([P, P], F32, name="bank", bufs=8)
+        for q in range(4):
+            load_scales(nc.sync, UP, q)
+        load_plane(0, 3)
+        load_plane(1, 0)
+        load_plane(1, 1)
+        load_words(GATE, 0, (0,))
+        load_plane(1, 2)
+        load_words(UP, 0, (0,))
+        load_plane(1, 3)
+        load_words(GATE, 0, (1,))
+        load_words(UP, 0, (1,))
+        load_words(GATE, 1, (0, 1))
+        load_words(UP, 1, (0, 1))
+        wd_raw = sbuf([PASSES, 2 * N], U8, "wd_raw")
+        nc.sync.dma_start(wd_raw[:].bitcast(I32), wd_words.bitcast(I32).rearrange("a p n -> p a n"))
+
+        weight = sbuf([J], F32, "weight")
+        turned = psum.tile([P, P], F32, name="bank7")
         nc.tensor.transpose(turned[:], head_rows[:], ident[:])
-        spread = keep.tile([P, TILES, 8, 16], F32, name="spread", align_bytes=64)
-        for lo, hi in ((0, 2), (2, 5), (5, 8)):
+        spread = sbuf([TILES, 8, 16], F32, "spread")
+        for n, (lo, hi) in enumerate(((0, 2), (2, 5), (5, 8))):
             nc.vector.tensor_copy(
                 spread[:, lo:hi, :, :],
                 turned[:, 0:64].rearrange("p (g c) -> p c g", g=8)[:, lo:hi, :].unsqueeze(3).to_broadcast([P, hi - lo, 8, 16]),
             )
-            back = psum.tile([P, hi - lo, P], F32, name="bank", bufs=8)
+            back = bank(n, hi - lo, P)
             for c in range(lo, hi):
                 nc.tensor.transpose(back[:, c - lo, :], spread[:, c, :, :].rearrange("p g r -> p (g r)"), ident[:])
             nc.scalar.copy(weight[:, P * lo : P * hi], back[:].rearrange("p c j -> p (c j)"))
-        for i in range(1, PACK):
-            load_plane(0, i)
-        load_plane(1, 0)
-        load_up(0, 0, (0,))
-        load_plane(1, 1)
-        load_plane(1, 2)
-        load_up(1, 0, (0,))
-        load_plane(1, 3)
-        load_up(0, 0, (1,))
-        load_up(1, 0, (1,))
-        load_up(0, 1, (0, 1))
-        load_up(1, 1, (0, 1))
-        wd_raw = keep.tile([P, PASSES, 2 * N], U8, name="wd_raw", align_bytes=64)
-        nc.sync.dma_start(wd_raw[:].bitcast(I32), wd_words.bitcast(I32).rearrange("a p n -> p a n"))
 
-        picked = [keep.tile([P, PACK, J], F32, name="picked%d" % a, align_bytes=64) for a in range(PASSES)]
-        woven = [keep.tile([P, HALF, PACK], BF16, name="woven%d" % a, align_bytes=64) for a in range(PASSES)]
-        late = keep.tile([P, 2, PASSES, PAIR, PACK], BF16, name="late", align_bytes=64)
+        picked0 = sbuf([PACK, J], F32, "picked0")
+        picked1 = sbuf([PACK, HALF], F32, "picked1")
+        late_picked = [sbuf([PACK + 2 * g, PAIR], F32, "late_picked%d" % g) for g in range(2)]
+        woven = [sbuf([HALF, PACK], BF16, "woven%d" % a) for a in range(PASSES)]
+        late = sbuf([2, PASSES, PAIR, PACK], BF16, "late")
         x_operands = {}
 
         def by_runs(slots_first):
@@ -130,25 +152,40 @@ def tile_list_silu_noneP_kernel(
         def as_runs(columns_first):
             return columns_first.rearrange("p (c e) t -> p c t e", e=RUN)
 
-        def gather(a, i, lo, hi):
-            nc.vector.tensor_tensor(picked[a][:, i, lo:hi], planes[a, i][:].indirect(offsets[:, lo // 16 : hi // 16]), weight[:, lo:hi], MULT)
+        def gather(out, a, i, lo, hi):
+            nc.vector.tensor_tensor(out, planes[a, i][:].indirect(offsets[:, lo // 16 : hi // 16]), weight[:, lo:hi], MULT)
 
-        def weave_two(u, lo, hi):
+        def gather0(i, lo, hi):
+            gather(picked0[:, i, lo:hi], 0, i, lo, hi)
+
+        def gather1(i):
+            gather(picked1[:, i, :], 1, i, 0, HALF)
+
+        def gather_late(i, g):
+            gather(late_picked[g][:, i, :], 1, i, HALF + PAIR * g, HALF + PAIR * (g + 1))
+
+        def weave_pair(a, u):
             slots = slice(2 * u, 2 * u + 2)
-            nc.scalar.copy(woven[1][:, lo:hi, slots], picked[1][:, slots, lo:hi].rearrange("p e j -> p j e"))
+            nc.scalar.copy(woven[a][:, :, slots], (picked0, picked1)[a][:, slots, 0:HALF].rearrange("p e j -> p j e"))
 
-        def weave_late(a, g):
-            lo = HALF + PAIR * g
-            nc.scalar.copy(as_runs(late[:, g, a, :, :]), by_runs(picked[a][:, :, lo : lo + PAIR]))
+        def weave_pair_late0(u):
+            slots = slice(2 * u, 2 * u + 2)
+            nc.scalar.copy(late[:, :, 0, :, slots], picked0[:, slots, HALF:J].rearrange("p e (g j) -> p g j e", g=2))
 
-        def quantise_late(g, tag):
+        def weave_late1(g):
+            nc.scalar.copy(as_runs(late[:, g, 1, :, :]), by_runs(late_picked[g][:, 0:PACK, :]))
+
+        def quantise(codes, scales, values):
+            nc.vector.quantize_mx(out=codes.bitcast(E4M3X4), scales=scales, in_=values)
+
+        def quantise_late(g):
             lo = HALF + PAIR * g
-            codes = keep.tile([P, PASSES, PAIR], U32, name=tag, align_bytes=64)
-            scales = keep.tile([P, PASSES, PAIR], U8, name="x_scales%d" % lo, align_bytes=64)
-            nc.vector.quantize_mx(
-                out=codes[:].rearrange("p a j -> p (a j)").bitcast(E4M3X4),
-                scales=scales[:].rearrange("p a j -> p (a j)"),
-                in_=late[:, g, :, :, :].rearrange("p a j i -> p (a j i)"),
+            codes = sbuf([PASSES, PAIR], U32, "x_codes%d" % lo)
+            scales = sbuf([PASSES, PAIR], U8, "x_scales%d" % lo)
+            quantise(
+                codes[:].rearrange("p a j -> p (a j)"),
+                scales[:].rearrange("p a j -> p (a j)"),
+                late[:, g, :, :, :].rearrange("p a j i -> p (a j i)"),
             )
             for a in range(PASSES):
                 for width in (TILE, PAIR):
@@ -159,51 +196,50 @@ def tile_list_silu_noneP_kernel(
         lead_scales = {}
 
         def open_lead(a, tag):
-            lead_codes[a] = keep.tile([P, HALF], U32, name=tag, align_bytes=64)
-            lead_scales[a] = keep.tile([P, HALF], U8, name="lead_scales%d" % a, align_bytes=64)
+            lead_codes[a] = sbuf([HALF], U32, tag)
+            lead_scales[a] = sbuf([HALF], U8, "lead_scales%d" % a)
             for width in (TILE, PAIR):
                 for c in range(0, HALF, width):
                     x_operands[a, c, width] = (lead_codes[a][:, c : c + width].bitcast(E4M3X4), lead_scales[a][:, c : c + width])
 
         def quantise_lead(a, lo, hi):
-            nc.vector.quantize_mx(
-                out=lead_codes[a][:, lo:hi].bitcast(E4M3X4),
-                scales=lead_scales[a][:, lo:hi],
-                in_=woven[a][:, lo:hi, :].rearrange("p j i -> p (j i)"),
-            )
+            quantise(lead_codes[a][:, lo:hi], lead_scales[a][:, lo:hi], woven[a][:, lo:hi, :].rearrange("p j i -> p (j i)"))
 
         for lo, hi in ((0, 256), (256, 640), (640, J)):
-            gather(0, 0, lo, hi)
-        for i in range(1, PACK):
-            gather(0, i, 0, J)
-        nc.scalar.copy(as_runs(woven[0][:]), by_runs(picked[0][:, :, 0:HALF]))
-        weave_late(0, 0)
-        weave_late(0, 1)
-        gather(1, 0, 0, J)
-        deal_up(0, 0, (0,))
-        open_lead(0, "plane10")
-        quantise_lead(0, 0, HALF)
-        up_scale = keep.tile([P, R], U8, name="raw000", align_bytes=64)
+            gather0(0, lo, hi)
+        gather0(1, 0, J)
+        weave_pair(0, 0)
+        weave_pair_late0(0)
+        gather0(2, 0, J)
+        gather0(3, 0, HALF)
+        weave_pair(0, 1)
+        gather0(3, HALF, J)
+        weave_pair_late0(1)
+        up_scale = sbuf([R], U8, "plane03")
         nc.vector.tensor_copy(
             up_scale[:].rearrange("p (b t m) -> p b t m", b=PASSES, t=PACK),
-            up_raw[:].rearrange("p (b m t) -> p b t m", b=PASSES, t=PACK),
+            scale_raw[:].rearrange("p (b m t) -> p b t m", b=PASSES, t=PACK),
         )
+        gather1(0)
+        gather_late(0, 0)
+        gather_late(0, 1)
+        open_lead(0, "plane10")
+        quantise_lead(0, 0, HALF)
         for q in range(4):
             nc.sync.dma_start(down_scale[32 * q : 32 * q + 4, :].bitcast(I32), up_scale[16 + 4 * q : 20 + 4 * q, :].bitcast(I32))
-        gather(1, 1, 0, HALF)
-        weave_two(0, 0, HALF)
-        gather(1, 1, HALF, J)
-        gather(1, 2, 0, HALF)
-        deal_up(1, 0, (0,))
+        gather1(1)
+        deal_on_scalar(GATE, 0, (0,))
+        weave_pair(1, 0)
+        gather1(2)
+        gather_late(1, 0)
+        gather_late(1, 1)
+        deal_on_scalar(UP, 0, (0,))
 
-        def new_bank(slots, width):
-            return psum.tile([P, slots, width], F32, name="bank", bufs=8)
-
-        def up_pass(bank, w, b, a, lo, width, slots, opens, closes):
+        def up_pass(sums, w, b, a, lo, width, slots, opens, closes):
             codes, scales = x_operands[a, lo, width]
             for n, t in enumerate(slots):
                 nc.tensor.matmul_mx(
-                    out=bank[:, n, :],
+                    out=sums[:, n, :],
                     lhsT=dealt[w, b, a][:, P * t : P * (t + 1)].bitcast(E4M3X4),
                     lhsT_scale=up_scale[8 * w + 4 * a : P, SPAN * b + P * t : SPAN * b + P * (t + 1)],
                     rhs=codes,
@@ -213,7 +249,7 @@ def tile_list_silu_noneP_kernel(
                 )
 
         all_slots = range(PACK)
-        lead = [[new_bank(PACK, TILE) for s in range(4)] for w in range(2)]
+        lead = [[bank(4 * w + s, PACK, TILE) for s in range(4)] for w in range(2)]
         for w in range(2):
             for s in range(4):
                 up_pass(lead[w][s], w, 0, 0, TILE * s, TILE, all_slots, True, False)
@@ -223,80 +259,74 @@ def tile_list_silu_noneP_kernel(
         h_codes = {}
         h_scales = {}
         for lo, hi in h_groups:
-            h[lo] = keep.tile([P, PASSES, hi - lo, PACK], BF16, name="h%d" % lo if lo else "raw010", align_bytes=64)
-            h_codes[lo] = keep.tile([P, PASSES, hi - lo], U32, name="h_codes%d" % lo, align_bytes=64)
-            h_scales[lo] = keep.tile([P, PASSES, hi - lo], U8, name="h_scales%d" % lo, align_bytes=64)
+            h[lo] = sbuf([PASSES, hi - lo, PACK], BF16, "h%d" % lo)
+            h_codes[lo] = sbuf([PASSES, hi - lo], U32, "h_codes%d" % lo)
+            h_scales[lo] = sbuf([PASSES, hi - lo], U8, "h_scales%d" % lo)
 
         def h_part(tiles, b, lo, hi):
             base = max(g for g in tiles if g <= lo)
             return tiles[base][:, b, lo - base : hi - base]
 
         acts = {}
+        ups = {}
 
-        def product(bank, act, s, b):
-            nc.vector.tensor_tensor(as_runs(h_part(h, b, TILE * s, TILE * (s + 1))), by_runs(bank[:]), by_runs(act), MULT)
+        def multiply(s, b):
+            nc.vector.tensor_tensor(as_runs(h_part(h, b, TILE * s, TILE * (s + 1))), by_runs(ups[s, b][:]), by_runs(acts[s, b]), MULT)
 
-        def finish_early(lo, at):
-            nc.vector.tensor_tensor(picked[1][:, 3, at : at + TILE], planes[1, 3][:].indirect(offsets[:, lo // 16 : (lo + TILE) // 16]), weight[:, lo : lo + TILE], MULT)
-            step = J + at - lo
-            both = picked[1][:].rearrange("p i j -> p (i j)")[:, 2 * J + lo - (step - TILE) : 3 * J + at + TILE]
+        def finish_lead(s, at):
+            lo = TILE * s
+            gather(picked1[:, 3, at : at + TILE], 1, 3, lo, lo + TILE)
+            step = HALF + at - lo
+            both = picked1[:].rearrange("p i j -> p (i j)")[:, 2 * HALF + lo - (step - TILE) : 3 * HALF + at + TILE]
             both = both.rearrange("p (e x) -> p x e", e=2)[:, step - TILE : step, :]
             nc.scalar.copy(woven[1][:, lo : lo + TILE, 2:4], both)
 
-        open_lead(1, "lead_codes")
+        open_lead(1, "lead_codes1")
 
         def lead_unit(s, act):
-            lo = TILE * s
             for w in range(2):
-                up_pass(lead[w][s], w, 0, 1, lo, TILE, all_slots, False, True)
-            acts[s] = act
-            nc.scalar.activation(act, lead[0][s][:], SILU)
+                up_pass(lead[w][s], w, 0, 1, TILE * s, TILE, all_slots, False, True)
+            acts[s, 0] = act
+            ups[s, 0] = lead[UP][s]
+            nc.scalar.activation(act, lead[GATE][s][:], SILU)
 
         def own_act(s):
-            return keep.tile([P, PACK, TILE], F32, name="lead_act%d" % s, align_bytes=64)[:]
+            return sbuf([PACK, TILE], F32, "lead_act%d" % s)[:]
 
         def parked_act(i):
-            return picked[1][:, i, HALF:J].rearrange("p (t j) -> p t j", t=PACK)
+            return late_picked[0][:, i : i + 2, :].rearrange("p i (h j) -> p (i h) j", h=2)
 
-        def gate_pair(g, b):
-            act = keep.tile([P, PACK, PAIR], F32, name="act%d%d" % (g, b), align_bytes=64)
+        def gate_pair(g, b, banks, act=None):
+            if act is None:
+                act = sbuf([PACK, PAIR], F32, "act%d%d" % (g, b))[:]
             for u in range(2):
-                bank = new_bank(2, PAIR)
+                sums = bank(banks[u], 2, PAIR)
                 for a in range(PASSES):
-                    up_pass(bank, 0, b, a, PAIR * g, PAIR, (2 * u, 2 * u + 1), a == 0, a == 1)
-                nc.scalar.activation(act[:, 2 * u : 2 * u + 2, :], bank[:], SILU)
-            acts[g, b] = act
+                    up_pass(sums, GATE, b, a, PAIR * g, PAIR, (2 * u, 2 * u + 1), a == 0, a == 1)
+                nc.scalar.activation(act[:, 2 * u : 2 * u + 2, :], sums[:], SILU)
+            for e in range(2):
+                acts[2 * g + e, b] = act[:, :, TILE * e : TILE * (e + 1)]
 
-        ups = {}
-
-        def up_tile(s, b):
-            ups[s, b] = new_bank(PACK, TILE)
+        def up_tile(s, b, n):
+            ups[s, b] = bank(n, PACK, TILE)
             for a in range(PASSES):
-                up_pass(ups[s, b], 1, b, a, TILE * s, TILE, all_slots, a == 0, a == 1)
-
-        def multiply(s, b):
-            e = s % 2
-            product(ups[s, b], acts[s // 2, b][:, :, TILE * e : TILE * (e + 1)], s, b)
+                up_pass(ups[s, b], UP, b, a, TILE * s, TILE, all_slots, a == 0, a == 1)
 
         def quantise_h(b, lo, hi):
-            nc.vector.quantize_mx(
-                out=h_part(h_codes, b, lo, hi).bitcast(E4M3X4),
-                scales=h_part(h_scales, b, lo, hi),
-                in_=h_part(h, b, lo, hi).rearrange("p j t -> p (j t)"),
-            )
+            quantise(h_part(h_codes, b, lo, hi), h_part(h_scales, b, lo, hi), h_part(h, b, lo, hi).rearrange("p j t -> p (j t)"))
 
         def quantise_h_group(lo):
-            nc.vector.quantize_mx(
-                out=h_codes[lo][:].rearrange("p b j -> p (b j)").bitcast(E4M3X4),
-                scales=h_scales[lo][:].rearrange("p b j -> p (b j)"),
-                in_=h[lo][:].rearrange("p b j t -> p (b j t)"),
+            quantise(
+                h_codes[lo][:].rearrange("p b j -> p (b j)"),
+                h_scales[lo][:].rearrange("p b j -> p (b j)"),
+                h[lo][:].rearrange("p b j t -> p (b j t)"),
             )
 
         down = {}
 
         def deal_down_words(tag):
-            down["words"] = keep.tile([P, PASSES, 2 * N], U8, name=tag, align_bytes=64)
-            nc.vector.tensor_copy(
+            down["words"] = sbuf([PASSES, 2 * N], U8, tag)
+            nc.scalar.copy(
                 down["words"][:].bitcast(U16).rearrange("p a (t m) -> p a m t", t=PACK),
                 wd_raw[:].bitcast(U16).rearrange("p a (m t) -> p a m t", t=PACK),
             )
@@ -312,153 +342,129 @@ def tile_list_silu_noneP_kernel(
                 stop=closes,
             )
 
-        y_scales = keep.tile([P, J], U8, name="y_scales", align_bytes=64)
+        y_scales = sbuf([J], U8, "y_scales")
         y_rows = out_0.rearrange("(p t) j -> p t j", t=PACK)
         code_rows = out_1[0].rearrange("p j i -> p (j i)").bitcast(I32)
-        y_wide = keep.tile([P, PACK, HALF], F32, name="picked0", align_bytes=64)
-        rounded = {}
-        y_codes = keep.tile([P, J], I32, name="spread", align_bytes=64)
+        y_codes = sbuf([J], I32, "spread")
+        rounded = sbuf([J, PACK], BF16, "plane01")
         y_of = {}
-        y_bank = {}
 
-        def down_wide(t):
-            bank = new_bank(1, HALF)
-            for b in range(PASSES):
-                down_pass(bank[:, 0, :], b, t, 0, HALF, b == 0, b == 1)
-            nc.scalar.copy(y_wide[:, t, :], bank[:, 0, :])
-            nc.sync.dma_start(y_rows[:, t, 0:HALF], y_wide[:, t, :])
+        def down_wide(banks):
+            y = sbuf([PACK, HALF], F32, "plane00")
+            y_of[0] = y
+            for t in range(PACK):
+                sums = bank(banks[t], 1, HALF)
+                for b in range(PASSES):
+                    down_pass(sums[:, 0, :], b, t, 0, HALF, b == 0, b == 1)
+                nc.scalar.copy(y[:, t, :], sums[:, 0, :])
+                nc.sync.dma_start(y_rows[:, t, 0:HALF], y[:, t, :])
 
-        def down_tile(s):
-            lo, hi = TILE * s, TILE * (s + 1)
-            bank = new_bank(PACK, TILE)
-            for b in range(PASSES):
-                for t in range(PACK):
-                    down_pass(bank[:, t, :], b, t, lo, hi, b == 0 and t == 0, b == 1 and t == PACK - 1)
-            y = keep.tile([P, PACK, TILE], F32, name="y%d" % s, align_bytes=64)
-            y_bank[s] = bank
-            y_of[s] = y[:]
-            nc.scalar.copy(y[:], bank[:])
-            nc.sync.dma_start(y_rows[:, :, lo:hi], y[:])
+        def down_pair(lo, banks):
+            y = sbuf([PACK, PAIR], F32, "y%d" % lo)
+            y_of[lo] = y
+            for u in range(2):
+                sums = bank(banks[u], 2, PAIR)
+                for b in range(PASSES):
+                    for e in range(2):
+                        down_pass(sums[:, e, :], b, 2 * u + e, lo, lo + PAIR, b == 0 and e == 0, b == 1 and e == 1)
+                nc.scalar.copy(y[:, 2 * u : 2 * u + 2, :], sums[:])
+                nc.sync.dma_start(y_rows[:, 2 * u : 2 * u + 2, lo : lo + PAIR], y[:, 2 * u : 2 * u + 2, :])
 
-        def open_rounded(lo, hi, tag):
-            tile = keep.tile([P, hi - lo, PACK], BF16, name=tag, align_bytes=64)
-            for c in range(lo, hi, TILE):
-                rounded[c] = (tile, lo)
-
-        def down_last(s):
-            lo, hi = TILE * s, TILE * (s + 1)
-            banks = [new_bank(2, TILE) for u in range(2)]
+        def down_tile(lo, banks, copies):
+            per = PACK // len(banks)
+            sums = [bank(n, per, TILE) for n in banks]
             for b in range(PASSES):
                 for t in range(PACK):
-                    down_pass(banks[t // 2][:, t % 2, :], b, t, lo, hi, b == 0 and t % 2 == 0, b == 1 and t % 2 == 1)
-            y = keep.tile([P, PACK, TILE], F32, name="y%d" % s, align_bytes=64)
-            y_of[s] = y[:]
-            for u, copy in enumerate((nc.scalar.copy, nc.vector.tensor_copy)):
-                copy(y[:, 2 * u : 2 * u + 2, :], banks[u][:])
-            nc.sync.dma_start(y_rows[:, :, lo:hi], y[:])
+                    down_pass(sums[t // per][:, t % per, :], b, t, lo, lo + TILE, b == 0 and t % per == 0, b == 1 and t % per == per - 1)
+            y = sbuf([PACK, TILE], F32, "y%d" % lo)
+            y_of[lo] = y
+            for u, copy in enumerate(copies):
+                copy(y[:, per * u : per * (u + 1), :], sums[u][:])
+            nc.sync.dma_start(y_rows[:, :, lo : lo + TILE], y[:])
 
-        def round_y(copy, y, lo, hi):
-            tile, base = rounded[lo]
-            copy(as_runs(tile[:, lo - base : hi - base, :]), by_runs(y))
+        def round_y(copy, base, lo, hi):
+            copy(as_runs(rounded[:, lo:hi, :]), by_runs(y_of[base][:, :, lo - base : hi - base]))
 
         def quantise_y(lo, hi):
-            tile, base = rounded[lo]
-            nc.vector.quantize_mx(
-                out=y_codes[:, lo:hi].bitcast(E4M3X4),
-                scales=y_scales[:, lo:hi],
-                in_=tile[:, lo - base : hi - base, :].rearrange("p j t -> p (j t)"),
-            )
-
-        def store_codes(lo, hi):
+            quantise(y_codes[:, lo:hi], y_scales[:, lo:hi], rounded[:, lo:hi, :].rearrange("p j t -> p (j t)"))
             nc.sync.dma_start(code_rows[:, lo:hi], y_codes[:, lo:hi])
 
-        finish_early(0, 0)
-        finish_early(128, 128)
-        finish_early(256, 256)
-        deal_up(0, 0, (1,))
+        finish_lead(0, 0)
+        finish_lead(1, 128)
+        deal_on_vector(GATE, 0, (1,))
+        finish_lead(2, 256)
         quantise_lead(1, 0, 128)
-        deal_up(1, 0, (1,))
-        finish_early(384, 0)
-        lead_unit(0, parked_act(2))
+        deal_on_vector(UP, 0, (1,))
+        finish_lead(3, 128)
+        lead_unit(0, own_act(0))
         quantise_lead(1, 128, 256)
-        lead_unit(1, parked_act(3))
+        lead_unit(1, parked_act(2))
         quantise_lead(1, 256, 384)
         lead_unit(2, own_act(2))
-        deal_up(0, 1, (0, 1))
         quantise_lead(1, 384, 512)
         lead_unit(3, own_act(3))
-        deal_up(1, 1, (0, 1))
-        gate_pair(0, 1)
-        up_tile(0, 1)
-        up_tile(1, 1)
-        product(lead[1][0], acts[0], 0, 0)
-        product(lead[1][1], acts[1], 1, 0)
-        gather(1, 2, 512, 768)
-        gather(1, 3, 512, 768)
-        weave_late(1, 0)
-        gate_pair(1, 1)
-        up_tile(2, 1)
-        up_tile(3, 1)
-        product(lead[1][2], acts[2], 2, 0)
-        product(lead[1][3], acts[3], 3, 0)
-        quantise_late(0, "x_codes512")
+        deal_on_vector(GATE, 1, (0, 1))
+        deal_on_vector(UP, 1, (0, 1))
+        gate_pair(0, 1, (0, 1), late_picked[1][:, 2:6, :])
+        up_tile(0, 1, 2)
+        up_tile(1, 1, 3)
+        multiply(0, 0)
+        multiply(1, 0)
+        gather_late(2, 0)
+        gather_late(3, 0)
+        weave_late1(0)
+        gate_pair(1, 1, (4, 5))
+        up_tile(2, 1, 0)
+        up_tile(3, 1, 1)
+        multiply(2, 0)
+        multiply(3, 0)
+        quantise_late(0)
+        deal_down_words("lead_act3")
+        gate_pair(2, 0, (6, 7))
         multiply(0, 1)
-        gate_pair(2, 0)
-        up_tile(4, 0)
-        up_tile(5, 0)
         multiply(1, 1)
-        gather(1, 2, 768, J)
-        gather(1, 3, 768, J)
-        weave_late(1, 1)
-        quantise_h(0, 0, 512)
+        up_tile(4, 0, 4)
+        up_tile(5, 0, 5)
+        gather_late(2, 1)
+        gather_late(3, 1)
+        weave_late1(1)
+        gate_pair(2, 1, (2, 3))
         multiply(2, 1)
         multiply(3, 1)
-        quantise_late(1, "x_codes768")
-        deal_down_words("act01")
+        up_tile(4, 1, 6)
+        up_tile(5, 1, 7)
+        quantise_late(1)
+        quantise_h(0, 0, 512)
         quantise_h(1, 0, 512)
-        gate_pair(2, 1)
-        up_tile(4, 1)
-        up_tile(5, 1)
-        gate_pair(3, 0)
-        down_wide(0)
-        down_wide(1)
-        down_wide(2)
-        down_wide(3)
+        gate_pair(3, 0, (0, 1))
         multiply(4, 0)
         multiply(5, 0)
+        down_wide((2, 3, 4, 5))
         multiply(4, 1)
         multiply(5, 1)
-        up_tile(6, 0)
-        up_tile(7, 0)
-        open_rounded(0, 512, "woven0")
-        round_y(nc.vector.tensor_copy, y_wide[:, :, 0:256], 0, 256)
+        up_tile(6, 0, 0)
+        up_tile(7, 0, 1)
         quantise_h_group(512)
-        round_y(nc.scalar.copy, y_wide[:, :, 256:512], 256, 512)
+        round_y(nc.vector.tensor_copy, 0, 0, 256)
+        round_y(nc.scalar.copy, 0, 256, 512)
+        gate_pair(3, 1, (6, 7))
         multiply(6, 0)
         multiply(7, 0)
-        gate_pair(3, 1)
+        up_tile(6, 1, 2)
+        up_tile(7, 1, 3)
         quantise_y(0, 512)
-        store_codes(0, 512)
         quantise_h(0, 768, 1024)
-        up_tile(6, 1)
+        down_pair(512, (4, 5))
         multiply(6, 1)
-        down_tile(4)
-        open_rounded(512, 768, "rounded2")
-        down_tile(5)
-        up_tile(7, 1)
-        quantise_h(1, 768, 896)
-        round_y(nc.vector.tensor_copy, y_of[4], 512, 640)
         multiply(7, 1)
-        round_y(nc.vector.tensor_copy, y_of[5], 640, 768)
-        down_tile(6)
+        quantise_h(1, 768, 896)
         quantise_h(1, 896, 1024)
+        down_tile(768, (0,), (nc.scalar.copy,))
+        round_y(nc.vector.tensor_copy, 512, 512, 768)
+        down_tile(896, (6, 7), (nc.scalar.copy, nc.vector.tensor_copy))
         quantise_y(512, 768)
-        store_codes(512, 768)
-        open_rounded(768, 1024, "rounded3")
-        round_y(nc.vector.tensor_copy, y_of[6], 768, 896)
-        down_last(7)
-        round_y(nc.vector.tensor_copy, y_of[7], 896, 1024)
+        round_y(nc.vector.tensor_copy, 768, 768, 896)
+        round_y(nc.vector.tensor_copy, 896, 896, 1024)
         quantise_y(768, 1024)
-        store_codes(768, 1024)
         for q in range(4):
             nc.sync.dma_start(out_2[0, 4 * q : 4 * q + 4, :].bitcast(I32), y_scales[32 * q : 32 * q + 4, :].bitcast(I32))

@@ -27,6 +27,8 @@ HALF = J // 2
 PAIR = 2 * TILE
 RUN = 4
 GATE, UP = 0, 1
+STRIDE = HALF + PAIR
+LEAD2 = 2 * STRIDE - PAIR
 
 
 def tile_list_silu_noneP_kernel(
@@ -109,19 +111,20 @@ def tile_list_silu_noneP_kernel(
             scale_raw[16:32, :].bitcast(I32).rearrange("r (a n) -> r a n", a=PASSES),
             wd_scales.bitcast(I32).rearrange("a r n -> r a n"),
         )
+        load_plane(0, 3)
         for q in range(4):
             load_scales(nc.sync, UP, q)
-        load_plane(0, 3)
         load_plane(1, 0)
-        load_plane(1, 1)
         load_words(GATE, 0, (0,))
-        load_plane(1, 2)
+        load_plane(1, 1)
         load_words(UP, 0, (0,))
+        load_plane(1, 2)
         load_plane(1, 3)
         load_words(GATE, 0, (1,))
         load_words(UP, 0, (1,))
-        load_words(GATE, 1, (0, 1))
-        load_words(UP, 1, (0, 1))
+        for w in (GATE, UP):
+            for a in range(PASSES):
+                load_words(w, 1, (a,))
         wd_raw = sbuf([PASSES, 2 * N], U8, "wd_raw")
         nc.sync.dma_start(wd_raw[:].bitcast(I32), wd_words.bitcast(I32).rearrange("a p n -> p a n"))
 
@@ -140,8 +143,9 @@ def tile_list_silu_noneP_kernel(
             nc.scalar.copy(weight[:, P * lo : P * hi], back[:].rearrange("p c j -> p (c j)"))
 
         picked0 = sbuf([PACK, J], F32, "picked0")
-        picked1 = sbuf([PACK, HALF], F32, "picked1")
-        late_picked = [sbuf([PACK + 2 * g, PAIR], F32, "late_picked%d" % g) for g in range(2)]
+        picked1 = sbuf([2, HALF], F32, "picked1")
+        shared = sbuf([PACK * STRIDE], F32, "shared")
+        late_picked = [shared[:].rearrange("p (i j) -> p i j", i=PACK)[:, :, 0:PAIR], sbuf([PACK + 1, PAIR], F32, "late_picked1")]
         woven = [sbuf([HALF, PACK], BF16, "woven%d" % a) for a in range(PASSES)]
         late = sbuf([2, PASSES, PAIR, PACK], BF16, "late")
         x_operands = {}
@@ -159,7 +163,7 @@ def tile_list_silu_noneP_kernel(
             gather(picked0[:, i, lo:hi], 0, i, lo, hi)
 
         def gather1(i):
-            gather(picked1[:, i, :], 1, i, 0, HALF)
+            gather(picked1[:, i, :] if i < 2 else shared[:, LEAD2 : LEAD2 + HALF], 1, i, 0, HALF)
 
         def gather_late(i, g):
             gather(late_picked[g][:, i, :], 1, i, HALF + PAIR * g, HALF + PAIR * (g + 1))
@@ -215,7 +219,9 @@ def tile_list_silu_noneP_kernel(
         weave_pair(0, 1)
         gather0(3, HALF, J)
         weave_pair_late0(1)
-        up_scale = sbuf([R], U8, "plane03")
+        deal_on_scalar(GATE, 0, (0,))
+        deal_on_scalar(UP, 0, (0,))
+        up_scale = sbuf([R], U8, "up_scale")
         nc.vector.tensor_copy(
             up_scale[:].rearrange("p (b t m) -> p b t m", b=PASSES, t=PACK),
             scale_raw[:].rearrange("p (b m t) -> p b t m", b=PASSES, t=PACK),
@@ -228,12 +234,9 @@ def tile_list_silu_noneP_kernel(
         for q in range(4):
             nc.sync.dma_start(down_scale[32 * q : 32 * q + 4, :].bitcast(I32), up_scale[16 + 4 * q : 20 + 4 * q, :].bitcast(I32))
         gather1(1)
-        deal_on_scalar(GATE, 0, (0,))
         weave_pair(1, 0)
-        gather1(2)
         gather_late(1, 0)
-        gather_late(1, 1)
-        deal_on_scalar(UP, 0, (0,))
+        gather1(2)
 
         def up_pass(sums, w, b, a, lo, width, slots, opens, closes):
             codes, scales = x_operands[a, lo, width]
@@ -275,10 +278,9 @@ def tile_list_silu_noneP_kernel(
 
         def finish_lead(s, at):
             lo = TILE * s
-            gather(picked1[:, 3, at : at + TILE], 1, 3, lo, lo + TILE)
+            gather(shared[:, LEAD2 + HALF + at : LEAD2 + HALF + at + TILE], 1, 3, lo, lo + TILE)
             step = HALF + at - lo
-            both = picked1[:].rearrange("p i j -> p (i j)")[:, 2 * HALF + lo - (step - TILE) : 3 * HALF + at + TILE]
-            both = both.rearrange("p (e x) -> p x e", e=2)[:, step - TILE : step, :]
+            both = shared[:, LEAD2 + lo : LEAD2 + lo + 2 * step].rearrange("p (e x) -> p x e", e=2)[:, 0:TILE, :]
             nc.scalar.copy(woven[1][:, lo : lo + TILE, 2:4], both)
 
         open_lead(1, "lead_codes1")
@@ -293,19 +295,18 @@ def tile_list_silu_noneP_kernel(
         def own_act(s):
             return sbuf([PACK, TILE], F32, "lead_act%d" % s)[:]
 
-        def parked_act(i):
-            return late_picked[0][:, i : i + 2, :].rearrange("p i (h j) -> p (i h) j", h=2)
-
-        def gate_pair(g, b, banks, act=None):
-            if act is None:
-                act = sbuf([PACK, PAIR], F32, "act%d%d" % (g, b))[:]
-            for u in range(2):
-                sums = bank(banks[u], 2, PAIR)
-                for a in range(PASSES):
-                    up_pass(sums, GATE, b, a, PAIR * g, PAIR, (2 * u, 2 * u + 1), a == 0, a == 1)
-                nc.scalar.activation(act[:, 2 * u : 2 * u + 2, :], sums[:], SILU)
+        def gate_half(g, b, u, n, act):
+            sums = bank(n, 2, PAIR)
+            for a in range(PASSES):
+                up_pass(sums, GATE, b, a, PAIR * g, PAIR, (2 * u, 2 * u + 1), a == 0, a == 1)
+            nc.scalar.activation(act[:, 2 * u : 2 * u + 2, :], sums[:], SILU)
             for e in range(2):
                 acts[2 * g + e, b] = act[:, :, TILE * e : TILE * (e + 1)]
+
+        def gate_pair(g, b, banks):
+            act = sbuf([PACK, PAIR], F32, "act%d%d" % (g, b))[:]
+            for u in range(2):
+                gate_half(g, b, u, banks[u], act)
 
         def up_tile(s, b, n):
             ups[s, b] = bank(n, PACK, TILE)
@@ -346,18 +347,21 @@ def tile_list_silu_noneP_kernel(
         y_rows = out_0.rearrange("(p t) j -> p t j", t=PACK)
         code_rows = out_1[0].rearrange("p j i -> p (j i)").bitcast(I32)
         y_codes = sbuf([J], I32, "spread")
-        rounded = sbuf([J, PACK], BF16, "plane01")
+        rounded = {}
         y_of = {}
 
         def down_wide(banks):
             y = sbuf([PACK, HALF], F32, "plane00")
             y_of[0] = y
-            for t in range(PACK):
-                sums = bank(banks[t], 1, HALF)
+            for u in range(2):
+                slots = (2 * u, 2 * u + 1)
+                sums = {t: bank(banks[t], 1, HALF) for t in slots}
                 for b in range(PASSES):
-                    down_pass(sums[:, 0, :], b, t, 0, HALF, b == 0, b == 1)
-                nc.scalar.copy(y[:, t, :], sums[:, 0, :])
-                nc.sync.dma_start(y_rows[:, t, 0:HALF], y[:, t, :])
+                    for t in slots:
+                        down_pass(sums[t][:, 0, :], b, t, 0, HALF, b == 0, b == 1)
+                for t in slots:
+                    nc.scalar.copy(y[:, t, :], sums[t][:, 0, :])
+                    nc.sync.dma_start(y_rows[:, t, 0:HALF], y[:, t, :])
 
         def down_pair(lo, banks):
             y = sbuf([PACK, PAIR], F32, "y%d" % lo)
@@ -382,11 +386,18 @@ def tile_list_silu_noneP_kernel(
                 copy(y[:, per * u : per * (u + 1), :], sums[u][:])
             nc.sync.dma_start(y_rows[:, :, lo : lo + TILE], y[:])
 
-        def round_y(copy, base, lo, hi):
-            copy(as_runs(rounded[:, lo:hi, :]), by_runs(y_of[base][:, :, lo - base : hi - base]))
+        def open_rounded(g, tag):
+            rounded[g] = sbuf([PAIR, PACK], BF16, tag)
 
-        def quantise_y(lo, hi):
-            quantise(y_codes[:, lo:hi], y_scales[:, lo:hi], rounded[:, lo:hi, :].rearrange("p j t -> p (j t)"))
+        def round_y(copy, base, lo, hi):
+            g, c = divmod(lo, PAIR)
+            copy(as_runs(rounded[g][:, c : c + hi - lo, :]), by_runs(y_of[base][:, :, lo - base : hi - base]))
+
+        def quantise_y(g):
+            columns = slice(PAIR * g, PAIR * (g + 1))
+            quantise(y_codes[:, columns], y_scales[:, columns], rounded[g][:].rearrange("p j t -> p (j t)"))
+
+        def store_codes(lo, hi):
             nc.sync.dma_start(code_rows[:, lo:hi], y_codes[:, lo:hi])
 
         finish_lead(0, 0)
@@ -396,75 +407,87 @@ def tile_list_silu_noneP_kernel(
         quantise_lead(1, 0, 128)
         deal_on_vector(UP, 0, (1,))
         finish_lead(3, 128)
-        lead_unit(0, own_act(0))
+        lead_unit(0, shared[:, 3 * STRIDE : 3 * STRIDE + HALF].rearrange("p (t j) -> p t j", t=PACK))
         quantise_lead(1, 128, 256)
-        lead_unit(1, parked_act(2))
+        lead_unit(1, own_act(1))
         quantise_lead(1, 256, 384)
+        deal_on_vector(GATE, 1, (0,))
+        deal_on_vector(GATE, 1, (1,))
         lead_unit(2, own_act(2))
         quantise_lead(1, 384, 512)
         lead_unit(3, own_act(3))
-        deal_on_vector(GATE, 1, (0, 1))
-        deal_on_vector(UP, 1, (0, 1))
-        gate_pair(0, 1, (0, 1), late_picked[1][:, 2:6, :])
+        gather_late(2, 0)
+        deal_on_vector(UP, 1, (0,))
+        multiply(0, 0)
+        deal_on_vector(UP, 1, (1,))
+        gather_late(3, 0)
+        gate_half(0, 1, 0, 0, late_picked[1][:, 1:5, :])
+        weave_late1(0)
+        gate_half(0, 1, 1, 1, late_picked[1][:, 1:5, :])
         up_tile(0, 1, 2)
         up_tile(1, 1, 3)
-        multiply(0, 0)
         multiply(1, 0)
-        gather_late(2, 0)
-        gather_late(3, 0)
-        weave_late1(0)
         gate_pair(1, 1, (4, 5))
         up_tile(2, 1, 0)
         up_tile(3, 1, 1)
         multiply(2, 0)
         multiply(3, 0)
         quantise_late(0)
-        deal_down_words("lead_act3")
+        deal_down_words("plane10")
         gate_pair(2, 0, (6, 7))
         multiply(0, 1)
         multiply(1, 1)
         up_tile(4, 0, 4)
         up_tile(5, 0, 5)
+        multiply(2, 1)
+        gather_late(1, 1)
         gather_late(2, 1)
         gather_late(3, 1)
         weave_late1(1)
         gate_pair(2, 1, (2, 3))
-        multiply(2, 1)
         multiply(3, 1)
+        quantise_h(0, 0, 512)
         up_tile(4, 1, 6)
         up_tile(5, 1, 7)
-        quantise_late(1)
-        quantise_h(0, 0, 512)
         quantise_h(1, 0, 512)
-        gate_pair(3, 0, (0, 1))
+        quantise_late(1)
+        down_wide((0, 1, 2, 3))
         multiply(4, 0)
         multiply(5, 0)
-        down_wide((2, 3, 4, 5))
+        gate_pair(3, 0, (4, 5))
         multiply(4, 1)
         multiply(5, 1)
         up_tile(6, 0, 0)
         up_tile(7, 0, 1)
         quantise_h_group(512)
+        open_rounded(0, "plane01")
         round_y(nc.vector.tensor_copy, 0, 0, 256)
+        open_rounded(1, "dealt100")
         round_y(nc.scalar.copy, 0, 256, 512)
-        gate_pair(3, 1, (6, 7))
+        gate_pair(3, 1, (2, 3))
         multiply(6, 0)
         multiply(7, 0)
-        up_tile(6, 1, 2)
-        up_tile(7, 1, 3)
-        quantise_y(0, 512)
+        up_tile(6, 1, 4)
+        up_tile(7, 1, 5)
+        quantise_y(0)
         quantise_h(0, 768, 1024)
-        down_pair(512, (4, 5))
+        quantise_y(1)
+        store_codes(0, 512)
+        down_pair(512, (6, 7))
         multiply(6, 1)
         multiply(7, 1)
         quantise_h(1, 768, 896)
         quantise_h(1, 896, 1024)
         down_tile(768, (0,), (nc.scalar.copy,))
+        open_rounded(2, "plane02")
         round_y(nc.vector.tensor_copy, 512, 512, 768)
-        down_tile(896, (6, 7), (nc.scalar.copy, nc.vector.tensor_copy))
-        quantise_y(512, 768)
-        round_y(nc.vector.tensor_copy, 768, 768, 896)
+        down_tile(896, (2, 3), (nc.scalar.copy, nc.vector.tensor_copy))
+        quantise_y(2)
+        store_codes(512, 768)
+        open_rounded(3, "plane03")
+        round_y(nc.scalar.copy, 768, 768, 896)
         round_y(nc.vector.tensor_copy, 896, 896, 1024)
-        quantise_y(768, 1024)
+        quantise_y(3)
+        store_codes(768, 1024)
         for q in range(4):
             nc.sync.dma_start(out_2[0, 4 * q : 4 * q + 4, :].bitcast(I32), y_scales[32 * q : 32 * q + 4, :].bitcast(I32))

@@ -103,22 +103,21 @@ def tile_list_silu_noneP_kernel(
         nc.sync.dma_start(head_rows[0:64, :], half_rows[0 : 2 * P : 17, :].rearrange("m (c j) -> m c j", j=P))
         load_plane(0, 0)
         nc.sync.dma_start(offsets[:], offs)
-        for q in range(4):
-            load_scales(nc.gpsimd, GATE, q)
+        for w in (GATE, UP):
+            for q in range(4):
+                load_scales(nc.gpsimd, w, q)
         load_plane(0, 1)
         load_plane(0, 2)
+        load_plane(0, 3)
         nc.sync.dma_start(
             scale_raw[16:32, :].bitcast(I32).rearrange("r (a n) -> r a n", a=PASSES),
             wd_scales.bitcast(I32).rearrange("a r n -> r a n"),
         )
-        load_plane(0, 3)
-        for q in range(4):
-            load_scales(nc.sync, UP, q)
         load_plane(1, 0)
-        load_words(GATE, 0, (0,))
         load_plane(1, 1)
-        load_words(UP, 0, (0,))
+        load_words(GATE, 0, (0,))
         load_plane(1, 2)
+        load_words(UP, 0, (0,))
         load_plane(1, 3)
         load_words(GATE, 0, (1,))
         load_words(UP, 0, (1,))
@@ -220,7 +219,6 @@ def tile_list_silu_noneP_kernel(
         gather0(3, HALF, J)
         weave_pair_late0(1)
         deal_on_scalar(GATE, 0, (0,))
-        deal_on_scalar(UP, 0, (0,))
         up_scale = sbuf([R], U8, "up_scale")
         nc.vector.tensor_copy(
             up_scale[:].rearrange("p (b t m) -> p b t m", b=PASSES, t=PACK),
@@ -237,6 +235,7 @@ def tile_list_silu_noneP_kernel(
         weave_pair(1, 0)
         gather_late(1, 0)
         gather1(2)
+        deal_on_vector(UP, 0, (0,))
 
         def up_pass(sums, w, b, a, lo, width, slots, opens, closes):
             codes, scales = x_operands[a, lo, width]

@@ -27,6 +27,7 @@ HALF = J // 2
 PAIR = 2 * TILE
 RUN = 4
 GATE, UP = 0, 1
+SHIFT = 32
 STRIDE = HALF + PAIR
 LEAD2 = 2 * STRIDE - PAIR
 
@@ -85,9 +86,10 @@ def tile_list_silu_noneP_kernel(
             raw[w, b, passes] = tile
 
         def deal_words(copy, dtype, w, b, passes):
-            tile = sbuf([len(passes), SPAN], I32, "dealt%d%d%d" % (w, b, passes[0]))
+            padded = sbuf([len(passes) * SPAN + 2 * SHIFT], I32, "dealt%d%d%d" % (w, b, passes[0]))
+            tile = padded[:, SHIFT : SHIFT + len(passes) * SPAN].rearrange("p (a r) -> p a r", r=SPAN)
             copy(
-                tile[:].bitcast(dtype).rearrange("p a (t m) -> p a m t", t=PACK),
+                tile.bitcast(dtype).rearrange("p a (t m) -> p a m t", t=PACK),
                 raw[w, b, passes][:].bitcast(dtype).rearrange("p a (m t) -> p a m t", t=PACK),
             )
             for n, a in enumerate(passes):
@@ -325,9 +327,10 @@ def tile_list_silu_noneP_kernel(
         down = {}
 
         def deal_down_words(tag):
-            down["words"] = sbuf([PASSES, 2 * N], U8, tag)
+            padded = sbuf([PASSES * 2 * N + 8 * SHIFT], U8, tag)
+            down["words"] = padded[:, 4 * SHIFT : 4 * SHIFT + PASSES * 2 * N].rearrange("p (a n) -> p a n", a=PASSES)
             nc.scalar.copy(
-                down["words"][:].bitcast(U16).rearrange("p a (t m) -> p a m t", t=PACK),
+                down["words"].bitcast(U16).rearrange("p a (t m) -> p a m t", t=PACK),
                 wd_raw[:].bitcast(U16).rearrange("p a (m t) -> p a m t", t=PACK),
             )
 

@@ -21,15 +21,23 @@ P = 128
 PACK = 4
 SPAN = P * PACK
 PASSES = 2
+HEADS = 8
+GROUP = P // HEADS
+QUADRANT = 32
 TILE = 128
 TILES = J // TILE
-HALF = J // 2
 PAIR = 2 * TILE
+HALF = J // 2
+LEAD = HALF // TILE
+LAST_PAIR = J - PAIR
 RUN = 4
 GATE, UP = 0, 1
+SCALAR_SHARE = 48
 SHIFT = 32
 STRIDE = HALF + PAIR
 LEAD2 = 2 * STRIDE - PAIR
+RING = LEAD2 + HALF
+FIRST_PIECES = ((0, 2), (2, 5), (5, 8))
 
 
 def tile_list_silu_noneP_kernel(
@@ -46,13 +54,13 @@ def tile_list_silu_noneP_kernel(
         def bank(n, slots, width):
             return psum.tile([P, slots, width], F32, name="bank%d" % n)
 
-        offsets = keep.tile([P, J // 16], U16, name="offsets")
+        offsets = keep.tile([P, J // GROUP], U16, name="offsets")
 
         scale_raw = sbuf([R], U8, "scale_raw")
         down_scale = sbuf([PASSES * N], U8, "down_scale")
         nc.vector.memset(scale_raw[:].bitcast(I32), 0)
         head_rows = sbuf([P], F32, "head_rows")
-        nc.vector.memset(head_rows[64:P, :], 0.0)
+        nc.vector.memset(head_rows[HEADS * TILES : P, :], 0.0)
         nc.vector.memset(down_scale[:].bitcast(I32), 0)
 
         warm = keep.tile([P, 8], F32, name="warm")
@@ -63,11 +71,11 @@ def tile_list_silu_noneP_kernel(
         ident = sbuf([P], F32, "ident")
         make_identity(nc, ident[:])
 
-        def load_scales(queue, w, q):
-            scales = (wg_scales, wu_scales)[w]
-            queue.dma_start(
-                scale_raw[32 * q + 8 * w : 32 * q + 8 * w + 8, :].bitcast(I32),
-                scales[:, 4 * q : 4 * q + 4, :].bitcast(I32),
+        def load_scales(w, q):
+            first = QUADRANT * q + 8 * w
+            nc.gpsimd.dma_start(
+                scale_raw[first : first + 8, :].bitcast(I32),
+                (wg_scales, wu_scales)[w][:, 4 * q : 4 * q + 4, :].bitcast(I32),
             )
 
         planes = {}
@@ -79,65 +87,60 @@ def tile_list_silu_noneP_kernel(
             rows = xT[SPAN * a : SPAN * (a + 1), :].rearrange("(p i) t -> p i t", i=PACK)
             nc.sync.dma_start(planes[a, i][:], rows[:, i, :])
 
-        def load_words(w, b, passes):
-            tile = sbuf([len(passes), SPAN], I32, "raw%d%d%d" % (w, b, passes[0]))
-            src = (wg_words, wu_words)[w].rearrange("a p r i -> p a (r i)").bitcast(I32)
-            nc.sync.dma_start(tile[:], src[:, passes[0] : passes[-1] + 1, SPAN * b : SPAN * (b + 1)])
-            raw[w, b, passes] = tile
+        def load_words(w, b, a):
+            raw[w, b, a] = sbuf([1, SPAN], I32, "raw%d%d%d" % (w, b, a))
+            words = (wg_words, wu_words)[w].rearrange("a p r i -> p a (r i)").bitcast(I32)
+            nc.sync.dma_start(raw[w, b, a][:], words[:, a : a + 1, SPAN * b : SPAN * (b + 1)])
 
-        def deal_words(copy, dtype, w, b, passes):
-            padded = sbuf([len(passes) * SPAN + 2 * SHIFT], I32, "dealt%d%d%d" % (w, b, passes[0]))
-            tile = padded[:, SHIFT : SHIFT + len(passes) * SPAN].rearrange("p (a r) -> p a r", r=SPAN)
+        def deal_words(copy, dtype, w, b, a, tag):
+            padded = sbuf([SPAN + 2 * SHIFT], I32, tag)
+            words = padded[:, SHIFT : SHIFT + SPAN].rearrange("p (a r) -> p a r", r=SPAN)
             copy(
-                tile.bitcast(dtype).rearrange("p a (t m) -> p a m t", t=PACK),
-                raw[w, b, passes][:].bitcast(dtype).rearrange("p a (m t) -> p a m t", t=PACK),
+                words.bitcast(dtype).rearrange("p a (t m) -> p a m t", t=PACK),
+                raw[w, b, a][:].bitcast(dtype).rearrange("p a (m t) -> p a m t", t=PACK),
             )
-            for n, a in enumerate(passes):
-                dealt[w, b, a] = tile[:, n, :]
+            dealt[w, b, a] = words[:, 0, :]
 
-        def deal_on_scalar(w, b, passes):
-            deal_words(nc.scalar.copy, U32, w, b, passes)
+        def deal_on_scalar(w, b, a, tag):
+            deal_words(nc.scalar.copy, U32, w, b, a, tag)
 
-        def deal_on_vector(w, b, passes):
-            deal_words(nc.vector.tensor_copy, I32, w, b, passes)
+        def deal_on_vector(w, b, a):
+            deal_words(nc.vector.tensor_copy, I32, w, b, a, "dealt%d%d%d" % (w, b, a))
 
         half_rows = wgt.rearrange("p (h j) -> (p h) j", h=2)
-        nc.sync.dma_start(head_rows[0:64, :], half_rows[0 : 2 * P : 17, :].rearrange("m (c j) -> m c j", j=P))
+        nc.sync.dma_start(head_rows[0 : HEADS * TILES, :], half_rows[0 : 2 * P : GROUP + 1, :].rearrange("m (c j) -> m c j", j=P))
         load_plane(0, 0)
         nc.sync.dma_start(offsets[:], offs)
         for w in (GATE, UP):
             for q in range(4):
-                load_scales(nc.gpsimd, w, q)
-        load_plane(0, 1)
-        load_plane(0, 2)
-        load_plane(0, 3)
+                load_scales(w, q)
+        for i in range(1, PACK):
+            load_plane(0, i)
         nc.sync.dma_start(
             scale_raw[16:32, :].bitcast(I32).rearrange("r (a n) -> r a n", a=PASSES),
             wd_scales.bitcast(I32).rearrange("a r n -> r a n"),
         )
         load_plane(1, 0)
         load_plane(1, 1)
-        load_words(GATE, 0, (0,))
+        load_words(GATE, 0, 0)
         load_plane(1, 2)
-        load_words(UP, 0, (0,))
+        load_words(UP, 0, 0)
         load_plane(1, 3)
-        load_words(GATE, 0, (1,))
-        load_words(UP, 0, (1,))
+        load_words(GATE, 0, 1)
+        load_words(UP, 0, 1)
         for w in (GATE, UP):
             for a in range(PASSES):
-                load_words(w, 1, (a,))
+                load_words(w, 1, a)
         wd_raw = sbuf([PASSES, 2 * N], U8, "wd_raw")
         nc.sync.dma_start(wd_raw[:].bitcast(I32), wd_words.bitcast(I32).rearrange("a p n -> p a n"))
 
         weight = sbuf([J], F32, "weight")
         turned = psum.tile([P, P], F32, name="bank7")
         nc.tensor.transpose(turned[:], head_rows[:], ident[:])
-        spread = sbuf([TILES, 8, 16], F32, "spread")
-        for n, (lo, hi) in enumerate(((0, 2), (2, 5), (5, 8))):
-            nc.vector.tensor_copy(
-                spread[:, lo:hi, :, :],
-                turned[:, 0:64].rearrange("p (g c) -> p c g", g=8)[:, lo:hi, :].unsqueeze(3).to_broadcast([P, hi - lo, 8, 16]),
-            )
+        spread = sbuf([TILES, HEADS, GROUP], F32, "spread")
+        by_tile = turned[:, 0 : HEADS * TILES].rearrange("p (g c) -> p c g", g=HEADS)
+        for n, (lo, hi) in enumerate(FIRST_PIECES):
+            nc.vector.tensor_copy(spread[:, lo:hi, :, :], by_tile[:, lo:hi, :].unsqueeze(3).to_broadcast([P, hi - lo, HEADS, GROUP]))
             back = bank(n, hi - lo, P)
             for c in range(lo, hi):
                 nc.tensor.transpose(back[:, c - lo, :], spread[:, c, :, :].rearrange("p g r -> p (g r)"), ident[:])
@@ -158,13 +161,13 @@ def tile_list_silu_noneP_kernel(
             return columns_first.rearrange("p (c e) t -> p c t e", e=RUN)
 
         def gather(out, a, i, lo, hi):
-            nc.vector.tensor_tensor(out, planes[a, i][:].indirect(offsets[:, lo // 16 : hi // 16]), weight[:, lo:hi], MULT)
+            nc.vector.tensor_tensor(out, planes[a, i][:].indirect(offsets[:, lo // GROUP : hi // GROUP]), weight[:, lo:hi], MULT)
 
         def gather0(i, lo, hi):
             gather(picked0[:, i, lo:hi], 0, i, lo, hi)
 
-        def gather1(i):
-            gather(picked1[:, i, :] if i < 2 else shared[:, LEAD2 : LEAD2 + HALF], 1, i, 0, HALF)
+        def gather_lead1(i, out):
+            gather(out, 1, i, 0, HALF)
 
         def gather_late(i, g):
             gather(late_picked[g][:, i, :], 1, i, HALF + PAIR * g, HALF + PAIR * (g + 1))
@@ -210,8 +213,8 @@ def tile_list_silu_noneP_kernel(
         def quantise_lead(a, lo, hi):
             quantise(lead_codes[a][:, lo:hi], lead_scales[a][:, lo:hi], woven[a][:, lo:hi, :].rearrange("p j i -> p (j i)"))
 
-        for lo, hi in ((0, 256), (256, 640), (640, J)):
-            gather0(0, lo, hi)
+        for lo, hi in FIRST_PIECES:
+            gather0(0, TILE * lo, TILE * hi)
         gather0(1, 0, J)
         weave_pair(0, 0)
         weave_pair_late0(0)
@@ -220,24 +223,26 @@ def tile_list_silu_noneP_kernel(
         weave_pair(0, 1)
         gather0(3, HALF, J)
         weave_pair_late0(1)
-        deal_on_scalar(GATE, 0, (0,))
+        deal_on_scalar(GATE, 0, 0, "dealt000")
         up_scale = sbuf([R], U8, "up_scale")
         nc.vector.tensor_copy(
             up_scale[:].rearrange("p (b t m) -> p b t m", b=PASSES, t=PACK),
             scale_raw[:].rearrange("p (b m t) -> p b t m", b=PASSES, t=PACK),
         )
-        gather1(0)
+        gather_lead1(0, picked1[:, 0, :])
         gather_late(0, 0)
         gather_late(0, 1)
         open_lead(0, "plane10")
         quantise_lead(0, 0, HALF)
         for q in range(4):
-            nc.sync.dma_start(down_scale[32 * q : 32 * q + 4, :].bitcast(I32), up_scale[16 + 4 * q : 20 + 4 * q, :].bitcast(I32))
-        gather1(1)
+            nc.sync.dma_start(
+                down_scale[QUADRANT * q : QUADRANT * q + 4, :].bitcast(I32), up_scale[16 + 4 * q : 20 + 4 * q, :].bitcast(I32)
+            )
+        gather_lead1(1, picked1[:, 1, :])
         weave_pair(1, 0)
         gather_late(1, 0)
-        gather1(2)
-        deal_on_vector(UP, 0, (0,))
+        gather_lead1(2, shared[:, LEAD2:RING])
+        deal_on_vector(UP, 0, 0)
 
         def up_pass(sums, w, b, a, lo, width, slots, opens, closes):
             codes, scales = x_operands[a, lo, width]
@@ -253,12 +258,12 @@ def tile_list_silu_noneP_kernel(
                 )
 
         all_slots = range(PACK)
-        lead = [[bank(4 * w + s, PACK, TILE) for s in range(4)] for w in range(2)]
-        for w in range(2):
-            for s in range(4):
+        lead = [[bank(LEAD * w + s, PACK, TILE) for s in range(LEAD)] for w in (GATE, UP)]
+        for w in (GATE, UP):
+            for s in range(LEAD):
                 up_pass(lead[w][s], w, 0, 0, TILE * s, TILE, all_slots, True, False)
 
-        h_groups = ((0, HALF), (HALF, 768), (768, J))
+        h_groups = ((0, HALF), (HALF, LAST_PAIR), (LAST_PAIR, J - TILE), (J - TILE, J))
         h = {}
         h_codes = {}
         h_scales = {}
@@ -277,9 +282,10 @@ def tile_list_silu_noneP_kernel(
         def multiply(s, b):
             nc.vector.tensor_tensor(as_runs(h_part(h, b, TILE * s, TILE * (s + 1))), by_runs(ups[s, b][:]), by_runs(acts[s, b]), MULT)
 
-        def finish_lead(s, at):
+        def finish_lead(s, c):
             lo = TILE * s
-            gather(shared[:, LEAD2 + HALF + at : LEAD2 + HALF + at + TILE], 1, 3, lo, lo + TILE)
+            at = TILE * c
+            gather(shared[:, RING + at : RING + at + TILE], 1, 3, lo, lo + TILE)
             step = HALF + at - lo
             both = shared[:, LEAD2 + lo : LEAD2 + lo + 2 * step].rearrange("p (e x) -> p x e", e=2)[:, 0:TILE, :]
             nc.scalar.copy(woven[1][:, lo : lo + TILE, 2:4], both)
@@ -287,7 +293,7 @@ def tile_list_silu_noneP_kernel(
         open_lead(1, "lead_codes1")
 
         def lead_unit(s, act):
-            for w in range(2):
+            for w in (GATE, UP):
                 up_pass(lead[w][s], w, 0, 1, TILE * s, TILE, all_slots, False, True)
             acts[s, 0] = act
             ups[s, 0] = lead[UP][s]
@@ -349,7 +355,7 @@ def tile_list_silu_noneP_kernel(
         y_rows = out_0.rearrange("(p t) j -> p t j", t=PACK)
         code_rows = out_1[0].rearrange("p j i -> p (j i)").bitcast(I32)
         y_codes = sbuf([J], I32, "spread")
-        rounded = {}
+        rounded = sbuf([J, PACK], BF16, "plane01")
         y_of = {}
 
         def down_wide(banks):
@@ -365,67 +371,63 @@ def tile_list_silu_noneP_kernel(
                     nc.scalar.copy(y[:, t, :], sums[t][:, 0, :])
                     nc.sync.dma_start(y_rows[:, t, 0:HALF], y[:, t, :])
 
-        def down_pair(lo, banks):
-            y = sbuf([PACK, PAIR], F32, "y%d" % lo)
-            y_of[lo] = y
-            for u in range(2):
-                sums = bank(banks[u], 2, PAIR)
-                for b in range(PASSES):
-                    for e in range(2):
-                        down_pass(sums[:, e, :], b, 2 * u + e, lo, lo + PAIR, b == 0 and e == 0, b == 1 and e == 1)
-                nc.scalar.copy(y[:, 2 * u : 2 * u + 2, :], sums[:])
-                nc.sync.dma_start(y_rows[:, 2 * u : 2 * u + 2, lo : lo + PAIR], y[:, 2 * u : 2 * u + 2, :])
+        y_late = sbuf([PACK, HALF], F32, "y_late")
+        y_of[HALF] = y_late
 
-        def down_tile(lo, banks, copies):
-            per = PACK // len(banks)
-            sums = [bank(n, per, TILE) for n in banks]
+        def down_slots(lo, width, first, count, n):
+            sums = bank(n, count, width)
+            for b in range(PASSES):
+                for e in range(count):
+                    down_pass(sums[:, e, :], b, first + e, lo, lo + width, b == 0 and e == 0, b == 1 and e == count - 1)
+            nc.scalar.copy(y_late[:, first : first + count, lo - HALF : lo - HALF + width], sums[:])
+
+        def store_late(u, lo, hi):
+            nc.sync.dma_start(y_rows[:, 2 * u : 2 * u + 2, lo:hi], y_late[:, 2 * u : 2 * u + 2, lo - HALF : hi - HALF])
+
+        def down_last(banks):
+            lo = J - TILE
+            sums = [bank(n, 2, TILE) for n in banks]
             for b in range(PASSES):
                 for t in range(PACK):
-                    down_pass(sums[t // per][:, t % per, :], b, t, lo, lo + TILE, b == 0 and t % per == 0, b == 1 and t % per == per - 1)
-            y = sbuf([PACK, TILE], F32, "y%d" % lo)
-            y_of[lo] = y
-            for u, copy in enumerate(copies):
-                copy(y[:, per * u : per * (u + 1), :], sums[u][:])
-            nc.sync.dma_start(y_rows[:, :, lo : lo + TILE], y[:])
-
-        def open_rounded(g, tag):
-            rounded[g] = sbuf([PAIR, PACK], BF16, tag)
+                    down_pass(sums[t // 2][:, t % 2, :], b, t, lo, J, b == 0 and t % 2 == 0, b == 1 and t % 2 == 1)
+            for u in range(2):
+                nc.scalar.copy(y_late[:, 2 * u : 2 * u + 2, lo - HALF : HALF], sums[u][:])
 
         def round_y(copy, base, lo, hi):
-            g, c = divmod(lo, PAIR)
-            copy(as_runs(rounded[g][:, c : c + hi - lo, :]), by_runs(y_of[base][:, :, lo - base : hi - base]))
+            copy(as_runs(rounded[:, lo:hi, :]), by_runs(y_of[base][:, :, lo - base : hi - base]))
 
-        def quantise_y(g):
-            columns = slice(PAIR * g, PAIR * (g + 1))
-            quantise(y_codes[:, columns], y_scales[:, columns], rounded[g][:].rearrange("p j t -> p (j t)"))
+        def quantise_y(lo, hi):
+            quantise(y_codes[:, lo:hi], y_scales[:, lo:hi], rounded[:, lo:hi, :].rearrange("p j t -> p (j t)"))
 
         def store_codes(lo, hi):
             nc.sync.dma_start(code_rows[:, lo:hi], y_codes[:, lo:hi])
 
         finish_lead(0, 0)
-        finish_lead(1, 128)
-        deal_on_vector(GATE, 0, (1,))
-        finish_lead(2, 256)
-        quantise_lead(1, 0, 128)
-        deal_on_vector(UP, 0, (1,))
-        finish_lead(3, 128)
+        finish_lead(1, 1)
+        deal_on_vector(GATE, 0, 1)
+        finish_lead(2, 2)
+        quantise_lead(1, 0, TILE)
+        deal_on_scalar(UP, 0, 1, "raw001")
+        finish_lead(3, 0)
         lead_unit(0, shared[:, 3 * STRIDE : 3 * STRIDE + HALF].rearrange("p (t j) -> p t j", t=PACK))
-        quantise_lead(1, 128, 256)
+        quantise_lead(1, TILE, 2 * TILE)
         lead_unit(1, own_act(1))
-        quantise_lead(1, 256, 384)
-        deal_on_vector(GATE, 1, (0,))
-        deal_on_vector(GATE, 1, (1,))
+        quantise_lead(1, 2 * TILE, 3 * TILE)
+        deal_on_vector(GATE, 1, 0)
+        deal_on_vector(GATE, 1, 1)
         lead_unit(2, own_act(2))
-        quantise_lead(1, 384, 512)
+        quantise_lead(1, 3 * TILE, HALF)
         lead_unit(3, own_act(3))
+
         gather_late(2, 0)
-        deal_on_vector(UP, 1, (0,))
+        deal_on_vector(UP, 1, 0)
         multiply(0, 0)
-        deal_on_vector(UP, 1, (1,))
+        deal_on_vector(UP, 1, 1)
         gather_late(3, 0)
-        gate_half(0, 1, 0, 0, late_picked[1][:, 1:5, :])
+        parked_act = late_picked[1][:, 1 : PACK + 1, :]
+        gate_half(0, 1, 0, 0, parked_act)
         weave_late1(0)
-        gate_half(0, 1, 1, 1, late_picked[1][:, 1:5, :])
+        gate_half(0, 1, 1, 1, parked_act)
         up_tile(0, 1, 2)
         up_tile(1, 1, 3)
         multiply(1, 0)
@@ -434,6 +436,7 @@ def tile_list_silu_noneP_kernel(
         up_tile(3, 1, 1)
         multiply(2, 0)
         multiply(3, 0)
+
         quantise_late(0)
         deal_down_words("plane10")
         gate_pair(2, 0, (6, 7))
@@ -442,17 +445,18 @@ def tile_list_silu_noneP_kernel(
         up_tile(4, 0, 4)
         up_tile(5, 0, 5)
         multiply(2, 1)
-        gather_late(1, 1)
-        gather_late(2, 1)
-        gather_late(3, 1)
+        for i in range(1, PACK):
+            gather_late(i, 1)
         weave_late1(1)
         gate_pair(2, 1, (2, 3))
         multiply(3, 1)
-        quantise_h(0, 0, 512)
+        quantise_h(0, 0, HALF)
         up_tile(4, 1, 6)
         up_tile(5, 1, 7)
-        quantise_h(1, 0, 512)
+        quantise_h(1, 0, HALF)
         quantise_late(1)
+
+        last_tile = J - TILE
         down_wide((0, 1, 2, 3))
         multiply(4, 0)
         multiply(5, 0)
@@ -460,36 +464,39 @@ def tile_list_silu_noneP_kernel(
         multiply(4, 1)
         multiply(5, 1)
         up_tile(6, 0, 0)
-        up_tile(7, 0, 1)
-        quantise_h_group(512)
-        open_rounded(0, "plane01")
-        round_y(nc.vector.tensor_copy, 0, 0, 256)
-        open_rounded(1, "dealt100")
-        round_y(nc.scalar.copy, 0, 256, 512)
+        quantise_h_group(HALF)
         gate_pair(3, 1, (2, 3))
+        round_y(nc.vector.tensor_copy, 0, 0, HALF)
         multiply(6, 0)
-        multiply(7, 0)
-        up_tile(6, 1, 4)
-        up_tile(7, 1, 5)
-        quantise_y(0)
-        quantise_h(0, 768, 1024)
-        quantise_y(1)
-        store_codes(0, 512)
-        down_pair(512, (6, 7))
+        up_tile(6, 1, 1)
+        up_tile(7, 0, 4)
+        quantise_y(0, HALF)
+        store_codes(0, HALF)
         multiply(6, 1)
+        down_slots(HALF, PAIR, 0, 2, 6)
+        store_late(0, HALF, LAST_PAIR)
+        multiply(7, 0)
+        up_tile(7, 1, 5)
+        quantise_h_group(LAST_PAIR)
+        quantise_h(0, last_tile, J)
+
+        down_slots(HALF, PAIR, 2, 1, 7)
+        down_slots(HALF, PAIR, 3, 1, 0)
         multiply(7, 1)
-        quantise_h(1, 768, 896)
-        quantise_h(1, 896, 1024)
-        down_tile(768, (0,), (nc.scalar.copy,))
-        open_rounded(2, "plane02")
-        round_y(nc.vector.tensor_copy, 512, 512, 768)
-        down_tile(896, (2, 3), (nc.scalar.copy, nc.vector.tensor_copy))
-        quantise_y(2)
-        store_codes(512, 768)
-        open_rounded(3, "plane03")
-        round_y(nc.scalar.copy, 768, 768, 896)
-        round_y(nc.vector.tensor_copy, 896, 896, 1024)
-        quantise_y(3)
-        store_codes(768, 1024)
+        quantise_h(1, last_tile, J)
+        down_slots(LAST_PAIR, TILE, 2, 2, 1)
+        store_late(1, HALF, last_tile)
+        down_slots(LAST_PAIR, TILE, 0, 2, 2)
+        round_y(nc.vector.tensor_copy, HALF, HALF, LAST_PAIR)
+        down_last((3, 4))
+        store_late(0, LAST_PAIR, J)
+        store_late(1, last_tile, J)
+        round_y(nc.vector.tensor_copy, HALF, LAST_PAIR, last_tile)
+        quantise_y(HALF, LAST_PAIR)
+        quantise_y(LAST_PAIR, last_tile)
+        round_y(nc.vector.tensor_copy, HALF, last_tile, J - SCALAR_SHARE)
+        round_y(nc.scalar.copy, HALF, J - SCALAR_SHARE, J)
+        quantise_y(last_tile, J)
+        store_codes(HALF, J)
         for q in range(4):
-            nc.sync.dma_start(out_2[0, 4 * q : 4 * q + 4, :].bitcast(I32), y_scales[32 * q : 32 * q + 4, :].bitcast(I32))
+            nc.sync.dma_start(out_2[0, 4 * q : 4 * q + 4, :].bitcast(I32), y_scales[QUADRANT * q : QUADRANT * q + 4, :].bitcast(I32))

from contextlib import ExitStack

import concourse.mybir as mybir
from concourse.masks import make_identity

K, R, N, T, J = 1024, 1024, 512, 2048, 1024
FLOPS = 2 * J * (2 * K * R + R * N)

F32 = mybir.dt.float32
BF16 = mybir.dt.bfloat16
I32 = mybir.dt.int32
U32 = mybir.dt.uint32
U16 = mybir.dt.uint16
U8 = mybir.dt.uint8
E4M3X4 = mybir.dt.float8_e4m3fn_x4
E2M1X4 = mybir.dt.float4_e2m1fn_x4
MULT = mybir.AluOpType.mult
SILU = mybir.ActivationFunctionType.Silu

P = 128
PACK = 4
SPAN = P * PACK
PASSES = 2
HEADS = 8
GROUP = P // HEADS
QUADRANT = 32
TILE = 128
TILES = J // TILE
PAIR = 2 * TILE
HALF = J // 2
LEAD = HALF // TILE
LAST_PAIR = J - PAIR
RUN = 4
GATE, UP = 0, 1
SCALAR_SHARE = 48
SHIFT = 32
STRIDE = HALF + PAIR
LEAD2 = 2 * STRIDE - PAIR
RING = LEAD2 + HALF
FIRST_PIECES = ((0, 2), (2, 5), (5, 8))


def tile_list_silu_noneP_kernel(
    tc, xT, wgt, wg_words, wg_scales, wu_words, wu_scales, wd_words, wd_scales, offs, out_0, out_1, out_2
):
    nc = tc.nc
    with ExitStack() as ctx:
        keep = ctx.enter_context(tc.tile_pool(name="keep", bufs=1))
        psum = ctx.enter_context(tc.psum_pool(name="psum", bufs=1))

        def sbuf(shape, dtype, name):
            return keep.tile([P] + shape, dtype, name=name, align_bytes=64)

        def bank(n, slots, width):
            return psum.tile([P, slots, width], F32, name="bank%d" % n)

        offsets = keep.tile([P, J // GROUP], U16, name="offsets")

        scale_raw = sbuf([R], U8, "scale_raw")
        down_scale = sbuf([PASSES * N], U8, "down_scale")
        nc.vector.memset(scale_raw[:].bitcast(I32), 0)
        head_rows = sbuf([P], F32, "head_rows")
        nc.vector.memset(head_rows[HEADS * TILES : P, :], 0.0)
        nc.vector.memset(down_scale[:].bitcast(I32), 0)

        warm = keep.tile([P, 8], F32, name="warm")
        warm2 = keep.tile([P, 8], F32, name="warm2")
        nc.vector.memset(warm[:], 0.0)
        nc.scalar.activation(warm2[:], warm[:], SILU)

        ident = sbuf([P], F32, "ident")
        make_identity(nc, ident[:])

        def load_scales(w, q):
            first = QUADRANT * q + 8 * w
            nc.gpsimd.dma_start(
                scale_raw[first : first + 8, :].bitcast(I32),
                (wg_scales, wu_scales)[w][:, 4 * q : 4 * q + 4, :].bitcast(I32),
            )

        planes = {}
        raw = {}
        dealt = {}

        def load_plane(a, i):
            planes[a, i] = sbuf([T], F32, "plane%d%d" % (a, i))
            rows = xT[SPAN * a : SPAN * (a + 1), :].rearrange("(p i) t -> p i t", i=PACK)
            nc.sync.dma_start(planes[a, i][:], rows[:, i, :])

        def load_words(w, b, a):
            raw[w, b, a] = sbuf([1, SPAN], I32, "raw%d%d%d" % (w, b, a))
            words = (wg_words, wu_words)[w].rearrange("a p r i -> p a (r i)").bitcast(I32)
            nc.sync.dma_start(raw[w, b, a][:], words[:, a : a + 1, SPAN * b : SPAN * (b + 1)])

        def deal_words(copy, dtype, w, b, a, tag):
            padded = sbuf([SPAN + 2 * SHIFT], I32, tag)
            words = padded[:, SHIFT : SHIFT + SPAN].rearrange("p (a r) -> p a r", r=SPAN)
            copy(
                words.bitcast(dtype).rearrange("p a (t m) -> p a m t", t=PACK),
                raw[w, b, a][:].bitcast(dtype).rearrange("p a (m t) -> p a m t", t=PACK),
            )
            dealt[w, b, a] = words[:, 0, :]

        def deal_on_scalar(w, b, a, tag):
            deal_words(nc.scalar.copy, U32, w, b, a, tag)

        def deal_on_vector(w, b, a):
            deal_words(nc.vector.tensor_copy, I32, w, b, a, "dealt%d%d%d" % (w, b, a))

        half_rows = wgt.rearrange("p (h j) -> (p h) j", h=2)
        nc.sync.dma_start(head_rows[0 : HEADS * TILES, :], half_rows[0 : 2 * P : GROUP + 1, :].rearrange("m (c j) -> m c j", j=P))
        load_plane(0, 0)
        nc.sync.dma_start(offsets[:], offs)
        for w in (GATE, UP):
            for q in range(4):
                load_scales(w, q)
        for i in range(1, PACK):
            load_plane(0, i)
        nc.sync.dma_start(
            scale_raw[16:32, :].bitcast(I32).rearrange("r (a n) -> r a n", a=PASSES),
            wd_scales.bitcast(I32).rearrange("a r n -> r a n"),
        )
        load_plane(1, 0)
        load_plane(1, 1)
        load_words(GATE, 0, 0)
        load_plane(1, 2)
        load_words(UP, 0, 0)
        load_plane(1, 3)
        load_words(GATE, 0, 1)
        load_words(UP, 0, 1)
        for w in (GATE, UP):
            for a in range(PASSES):
                load_words(w, 1, a)
        wd_raw = sbuf([PASSES, 2 * N], U8, "wd_raw")
        nc.sync.dma_start(wd_raw[:].bitcast(I32), wd_words.bitcast(I32).rearrange("a p n -> p a n"))

        weight = sbuf([J], F32, "weight")
        turned = psum.tile([P, P], F32, name="bank7")
        nc.tensor.transpose(turned[:], head_rows[:], ident[:])
        spread = sbuf([TILES, HEADS, GROUP], F32, "spread")
        by_tile = turned[:, 0 : HEADS * TILES].rearrange("p (g c) -> p c g", g=HEADS)
        for n, (lo, hi) in enumerate(FIRST_PIECES):
            nc.vector.tensor_copy(spread[:, lo:hi, :, :], by_tile[:, lo:hi, :].unsqueeze(3).to_broadcast([P, hi - lo, HEADS, GROUP]))
            back = bank(n, hi - lo, P)
            for c in range(lo, hi):
                nc.tensor.transpose(back[:, c - lo, :], spread[:, c, :, :].rearrange("p g r -> p (g r)"), ident[:])
            nc.scalar.copy(weight[:, P * lo : P * hi], back[:].rearrange("p c j -> p (c j)"))

        picked0 = sbuf([PACK, J], F32, "picked0")
        picked1 = sbuf([2, HALF], F32, "picked1")
        shared = sbuf([PACK * STRIDE], F32, "shared")
        late_picked = [shared[:].rearrange("p (i j) -> p i j", i=PACK)[:, :, 0:PAIR], sbuf([PACK + 1, PAIR], F32, "late_picked1")]
        woven = [sbuf([HALF, PACK], BF16, "woven%d" % a) for a in range(PASSES)]
        late = sbuf([2, PASSES, PAIR, PACK], BF16, "late")
        x_operands = {}

        def by_runs(slots_first):
            return slots_first.rearrange("p t (c e) -> p c t e", e=RUN)

        def as_runs(columns_first):
            return columns_first.rearrange("p (c e) t -> p c t e", e=RUN)

        def gather(out, a, i, lo, hi):
            nc.vector.tensor_tensor(out, planes[a, i][:].indirect(offsets[:, lo // GROUP : hi // GROUP]), weight[:, lo:hi], MULT)

        def gather0(i, lo, hi):
            gather(picked0[:, i, lo:hi], 0, i, lo, hi)

        def gather_lead1(i, out):
            gather(out, 1, i, 0, HALF)

        def gather_late(i, g):
            gather(late_picked[g][:, i, :], 1, i, HALF + PAIR * g, HALF + PAIR * (g + 1))

        def weave_pair(a, u):
            slots = slice(2 * u, 2 * u + 2)
            nc.scalar.copy(woven[a][:, :, slots], (picked0, picked1)[a][:, slots, 0:HALF].rearrange("p e j -> p j e"))

        def weave_pair_late0(u):
            slots = slice(2 * u, 2 * u + 2)
            nc.scalar.copy(late[:, :, 0, :, slots], picked0[:, slots, HALF:J].rearrange("p e (g j) -> p g j e", g=2))

        def weave_late1(g):
            nc.scalar.copy(as_runs(late[:, g, 1, :, :]), by_runs(late_picked[g][:, 0:PACK, :]))

        def quantise(codes, scales, values):
            nc.vector.quantize_mx(out=codes.bitcast(E4M3X4), scales=scales, in_=values)

        def quantise_late(g):
            lo = HALF + PAIR * g
            codes = sbuf([PASSES, PAIR], U32, "x_codes%d" % lo)
            scales = sbuf([PASSES, PAIR], U8, "x_scales%d" % lo)
            quantise(
                codes[:].rearrange("p a j -> p (a j)"),
                scales[:].rearrange("p a j -> p (a j)"),
                late[:, g, :, :, :].rearrange("p a j i -> p (a j i)"),
            )
            for a in range(PASSES):
                for width in (TILE, PAIR):
                    for c in range(0, PAIR, width):
                        x_operands[a, lo + c, width] = (codes[:, a, c : c + width].bitcast(E4M3X4), scales[:, a, c : c + width])

        lead_codes = {}
        lead_scales = {}

        def open_lead(a, tag):
            lead_codes[a] = sbuf([HALF], U32, tag)
            lead_scales[a] = sbuf([HALF], U8, "lead_scales%d" % a)
            for width in (TILE, PAIR):
                for c in range(0, HALF, width):
                    x_operands[a, c, width] = (lead_codes[a][:, c : c + width].bitcast(E4M3X4), lead_scales[a][:, c : c + width])

        def quantise_lead(a, lo, hi):
            quantise(lead_codes[a][:, lo:hi], lead_scales[a][:, lo:hi], woven[a][:, lo:hi, :].rearrange("p j i -> p (j i)"))

        for lo, hi in FIRST_PIECES:
            gather0(0, TILE * lo, TILE * hi)
        gather0(1, 0, J)
        weave_pair(0, 0)
        weave_pair_late0(0)
        gather0(2, 0, J)
        gather0(3, 0, HALF)
        weave_pair(0, 1)
        gather0(3, HALF, J)
        weave_pair_late0(1)
        deal_on_scalar(GATE, 0, 0, "dealt000")
        up_scale = sbuf([R], U8, "up_scale")
        nc.vector.tensor_copy(
            up_scale[:].rearrange("p (b t m) -> p b t m", b=PASSES, t=PACK),
            scale_raw[:].rearrange("p (b m t) -> p b t m", b=PASSES, t=PACK),
        )
        gather_lead1(0, picked1[:, 0, :])
        gather_late(0, 0)
        gather_late(0, 1)
        open_lead(0, "plane10")
        quantise_lead(0, 0, HALF)
        for q in range(4):
            nc.sync.dma_start(
                down_scale[QUADRANT * q : QUADRANT * q + 4, :].bitcast(I32), up_scale[16 + 4 * q : 20 + 4 * q, :].bitcast(I32)
            )
        gather_lead1(1, picked1[:, 1, :])
        weave_pair(1, 0)
        gather_late(1, 0)
        gather_lead1(2, shared[:, LEAD2:RING])
        deal_on_vector(UP, 0, 0)

        def up_pass(sums, w, b, a, lo, width, slots, opens, closes):
            codes, scales = x_operands[a, lo, width]
            for n, t in enumerate(slots):
                nc.tensor.matmul_mx(
                    out=sums[:, n, :],
                    lhsT=dealt[w, b, a][:, P * t : P * (t + 1)].bitcast(E4M3X4),
                    lhsT_scale=up_scale[8 * w + 4 * a : P, SPAN * b + P * t : SPAN * b + P * (t + 1)],
                    rhs=codes,
                    rhs_scale=scales,
                    start=(opens and n == 0),
                    stop=(closes and n == len(slots) - 1),
                )

        all_slots = range(PACK)
        lead = [[bank(LEAD * w + s, PACK, TILE) for s in range(LEAD)] for w in (GATE, UP)]
        for w in (GATE, UP):
            for s in range(LEAD):
                up_pass(lead[w][s], w, 0, 0, TILE * s, TILE, all_slots, True, False)

        h_groups = ((0, HALF), (HALF, LAST_PAIR), (LAST_PAIR, J - TILE), (J - TILE, J))
        h = {}
        h_codes = {}
        h_scales = {}
        for lo, hi in h_groups:
            h[lo] = sbuf([PASSES, hi - lo, PACK], BF16, "h%d" % lo)
            h_codes[lo] = sbuf([PASSES, hi - lo], U32, "h_codes%d" % lo)
            h_scales[lo] = sbuf([PASSES, hi - lo], U8, "h_scales%d" % lo)

        def h_part(tiles, b, lo, hi):
            base = max(g for g in tiles if g <= lo)
            return tiles[base][:, b, lo - base : hi - base]

        acts = {}
        ups = {}

        def multiply(s, b):
            nc.vector.tensor_tensor(as_runs(h_part(h, b, TILE * s, TILE * (s + 1))), by_runs(ups[s, b][:]), by_runs(acts[s, b]), MULT)

        def finish_lead(s, c):
            lo = TILE * s
            at = TILE * c
            gather(shared[:, RING + at : RING + at + TILE], 1, 3, lo, lo + TILE)
            step = HALF + at - lo
            both = shared[:, LEAD2 + lo : LEAD2 + lo + 2 * step].rearrange("p (e x) -> p x e", e=2)[:, 0:TILE, :]
            nc.scalar.copy(woven[1][:, lo : lo + TILE, 2:4], both)

        open_lead(1, "lead_codes1")

        def lead_unit(s, act):
            for w in (GATE, UP):
                up_pass(lead[w][s], w, 0, 1, TILE * s, TILE, all_slots, False, True)
            acts[s, 0] = act
            ups[s, 0] = lead[UP][s]
            nc.scalar.activation(act, lead[GATE][s][:], SILU)

        def own_act(s):
            return sbuf([PACK, TILE], F32, "lead_act%d" % s)[:]

        def gate_half(g, b, u, n, act):
            sums = bank(n, 2, PAIR)
            for a in range(PASSES):
                up_pass(sums, GATE, b, a, PAIR * g, PAIR, (2 * u, 2 * u + 1), a == 0, a == 1)
            nc.scalar.activation(act[:, 2 * u : 2 * u + 2, :], sums[:], SILU)
            for e in range(2):
                acts[2 * g + e, b] = act[:, :, TILE * e : TILE * (e + 1)]

        def gate_pair(g, b, banks):
            act = sbuf([PACK, PAIR], F32, "act%d%d" % (g, b))[:]
            for u in range(2):
                gate_half(g, b, u, banks[u], act)

        def up_tile(s, b, n):
            ups[s, b] = bank(n, PACK, TILE)
            for a in range(PASSES):
                up_pass(ups[s, b], UP, b, a, TILE * s, TILE, all_slots, a == 0, a == 1)

        def quantise_h(b, lo, hi):
            quantise(h_part(h_codes, b, lo, hi), h_part(h_scales, b, lo, hi), h_part(h, b, lo, hi).rearrange("p j t -> p (j t)"))

        def quantise_h_group(lo):
            quantise(
                h_codes[lo][:].rearrange("p b j -> p (b j)"),
                h_scales[lo][:].rearrange("p b j -> p (b j)"),
                h[lo][:].rearrange("p b j t -> p (b j t)"),
            )

        down = {}

        def deal_down_words(tag):
            padded = sbuf([PASSES * 2 * N + 8 * SHIFT], U8, tag)
            down["words"] = padded[:, 4 * SHIFT : 4 * SHIFT + PASSES * 2 * N].rearrange("p (a n) -> p a n", a=PASSES)
            nc.scalar.copy(
                down["words"].bitcast(U16).rearrange("p a (t m) -> p a m t", t=PACK),
                wd_raw[:].bitcast(U16).rearrange("p a (m t) -> p a m t", t=PACK),
            )

        def down_pass(out, b, t, lo, hi, opens, closes):
            nc.tensor.matmul_mx(
                out=out,
                lhsT=down["words"][:, b, 2 * P * t : 2 * P * (t + 1)].bitcast(E2M1X4),
                lhsT_scale=down_scale[:, N * b + P * t : N * b + P * (t + 1)],
                rhs=h_part(h_codes, b, lo, hi).bitcast(E4M3X4),
                rhs_scale=h_part(h_scales, b, lo, hi),
                start=opens,
                stop=closes,
            )

        y_scales = sbuf([J], U8, "y_scales")
        y_rows = out_0.rearrange("(p t) j -> p t j", t=PACK)
        code_rows = out_1[0].rearrange("p j i -> p (j i)").bitcast(I32)
        y_codes = sbuf([J], I32, "spread")
        rounded = sbuf([J, PACK], BF16, "plane01")
        y_of = {}

        def down_wide(banks):
            y = sbuf([PACK, HALF], F32, "plane00")
            y_of[0] = y
            for u in range(2):
                slots = (2 * u, 2 * u + 1)
                sums = {t: bank(banks[t], 1, HALF) for t in slots}
                for b in range(PASSES):
                    for t in slots:
                        down_pass(sums[t][:, 0, :], b, t, 0, HALF, b == 0, b == 1)
                for t in slots:
                    nc.scalar.copy(y[:, t, :], sums[t][:, 0, :])
                    nc.sync.dma_start(y_rows[:, t, 0:HALF], y[:, t, :])

        y_late = sbuf([PACK, HALF], F32, "y_late")
        y_of[HALF] = y_late

        def down_slots(lo, width, first, count, n):
            sums = bank(n, count, width)
            for b in range(PASSES):
                for e in range(count):
                    down_pass(sums[:, e, :], b, first + e, lo, lo + width, b == 0 and e == 0, b == 1 and e == count - 1)
            nc.scalar.copy(y_late[:, first : first + count, lo - HALF : lo - HALF + width], sums[:])

        def store_late(u, lo, hi):
            nc.sync.dma_start(y_rows[:, 2 * u : 2 * u + 2, lo:hi], y_late[:, 2 * u : 2 * u + 2, lo - HALF : hi - HALF])

        def down_last(banks):
            lo = J - TILE
            sums = [bank(n, 2, TILE) for n in banks]
            for b in range(PASSES):
                for t in range(PACK):
                    down_pass(sums[t // 2][:, t % 2, :], b, t, lo, J, b == 0 and t % 2 == 0, b == 1 and t % 2 == 1)
            for u in range(2):
                nc.scalar.copy(y_late[:, 2 * u : 2 * u + 2, lo - HALF : HALF], sums[u][:])

        def round_y(copy, base, lo, hi):
            copy(as_runs(rounded[:, lo:hi, :]), by_runs(y_of[base][:, :, lo - base : hi - base]))

        def quantise_y(lo, hi):
            quantise(y_codes[:, lo:hi], y_scales[:, lo:hi], rounded[:, lo:hi, :].rearrange("p j t -> p (j t)"))

        def store_codes(lo, hi):
            nc.sync.dma_start(code_rows[:, lo:hi], y_codes[:, lo:hi])

        finish_lead(0, 0)
        finish_lead(1, 1)
        deal_on_vector(GATE, 0, 1)
        finish_lead(2, 2)
        quantise_lead(1, 0, TILE)
        deal_on_scalar(UP, 0, 1, "raw001")
        finish_lead(3, 0)
        lead_unit(0, shared[:, 3 * STRIDE : 3 * STRIDE + HALF].rearrange("p (t j) -> p t j", t=PACK))
        quantise_lead(1, TILE, 2 * TILE)
        lead_unit(1, own_act(1))
        quantise_lead(1, 2 * TILE, 3 * TILE)
        deal_on_vector(GATE, 1, 0)
        deal_on_vector(GATE, 1, 1)
        lead_unit(2, own_act(2))
        quantise_lead(1, 3 * TILE, HALF)
        lead_unit(3, own_act(3))

        gather_late(2, 0)
        deal_on_vector(UP, 1, 0)
        multiply(0, 0)
        deal_on_vector(UP, 1, 1)
        gather_late(3, 0)
        parked_act = late_picked[1][:, 1 : PACK + 1, :]
        gate_half(0, 1, 0, 0, parked_act)
        weave_late1(0)
        gate_half(0, 1, 1, 1, parked_act)
        up_tile(0, 1, 2)
        up_tile(1, 1, 3)
        multiply(1, 0)
        gate_pair(1, 1, (4, 5))
        up_tile(2, 1, 0)
        up_tile(3, 1, 1)
        multiply(2, 0)
        multiply(3, 0)

        quantise_late(0)
        deal_down_words("plane10")
        gate_pair(2, 0, (6, 7))
        multiply(0, 1)
        multiply(1, 1)
        up_tile(4, 0, 4)
        up_tile(5, 0, 5)
        multiply(2, 1)
        for i in range(1, PACK):
            gather_late(i, 1)
        weave_late1(1)
        gate_pair(2, 1, (2, 3))
        multiply(3, 1)
        quantise_h(0, 0, HALF)
        up_tile(4, 1, 6)
        up_tile(5, 1, 7)
        quantise_h(1, 0, HALF)
        quantise_late(1)

        last_tile = J - TILE
        down_wide((0, 1, 2, 3))
        multiply(4, 0)
        multiply(5, 0)
        gate_pair(3, 0, (4, 5))
        multiply(4, 1)
        multiply(5, 1)
        up_tile(6, 0, 0)
        quantise_h_group(HALF)
        gate_pair(3, 1, (2, 3))
        round_y(nc.vector.tensor_copy, 0, 0, HALF)
        multiply(6, 0)
        up_tile(6, 1, 1)
        up_tile(7, 0, 4)
        quantise_y(0, HALF)
        store_codes(0, HALF)
        multiply(6, 1)
        down_slots(HALF, PAIR, 0, 2, 6)
        store_late(0, HALF, LAST_PAIR)
        multiply(7, 0)
        up_tile(7, 1, 5)
        quantise_h_group(LAST_PAIR)
        quantise_h(0, last_tile, J)

        down_slots(HALF, PAIR, 2, 1, 7)
        down_slots(HALF, PAIR, 3, 1, 0)
        multiply(7, 1)
        quantise_h(1, last_tile, J)
        down_slots(LAST_PAIR, TILE, 2, 2, 1)
        store_late(1, HALF, last_tile)
        down_slots(LAST_PAIR, TILE, 0, 2, 2)
        round_y(nc.vector.tensor_copy, HALF, HALF, LAST_PAIR)
        down_last((3, 4))
        store_late(0, LAST_PAIR, J)
        store_late(1, last_tile, J)
        round_y(nc.vector.tensor_copy, HALF, LAST_PAIR, last_tile)
        quantise_y(HALF, LAST_PAIR)
        quantise_y(LAST_PAIR, last_tile)
        round_y(nc.vector.tensor_copy, HALF, last_tile, J - SCALAR_SHARE)
        round_y(nc.scalar.copy, HALF, J - SCALAR_SHARE, J)
        quantise_y(last_tile, J)
        store_codes(HALF, J)
        for q in range(4):
            nc.sync.dma_start(out_2[0, 4 * q : 4 * q + 4, :].bitcast(I32), y_scales[QUADRANT * q : QUADRANT * q + 4, :].bitcast(I32))
